import numpy as np, ml_dtypes
CORES = [8,136,40,168]
N = 4
BF = ml_dtypes.bfloat16
S, SETS, SH, B, L, RO, NS, EPS = 2048, 8, 4, 226, 256, 4, 7, 150
def sky(rng):
    c = rng.integers(0, 16, (N, 8, 16, S)); t = rng.integers(0, S, (N, 8, 16, SETS * B))
    return c, np.where(rng.random(t.shape) < 0.0625, S, t)
def pack(c, t, v):
    return {"cvec": np.ascontiguousarray(c).reshape(N, 128, S).astype(np.float32).astype(BF), "tsee": np.ascontiguousarray(t).reshape(N, 128, SETS * B).astype(np.int32),
            "obs": np.ascontiguousarray(v).reshape(N, 128, NS * L).astype(np.float32).astype(BF)}
def uneven(rng, shape):
    k = shape[:-2] + (1, shape[-1]); m = rng.choice(np.array([0, 1, 2, 4, 7, 11, 15]), k)
    x = np.minimum((rng.random(shape) * (m + 1)).astype(np.int64), m)
    return np.where(rng.random(k) < 0.25, 15 - x, x)
def sized(n):
    w = np.indices((15, 15, 15, 15)).reshape(4, -1).T; at = np.unique(np.sum(w * w, axis=1), return_index=True)[1]
    return np.concatenate([15 * (np.arange(12) < n[..., None] // 225), w[at[n % 225]]], axis=-1)
def setup_inputs(rng):
    c, t = sky(rng); P = 24; pool = rng.integers(0, 16, (8, SETS, 16, P)); size = rng.integers(NS + 2, P + 1, (1, 8, 1, 1))
    pick = np.argsort(rng.random((N, 8, L, P)) + (np.arange(P) >= size), axis=-1)[..., :NS]
    v = pool[np.arange(8).reshape(1, 8, 1, 1), (np.arange(L) % SETS).reshape(1, 1, L, 1), :, pick]
    v = v.transpose(0, 1, 4, 3, 2); near = rng.random((N, 8, 1, NS, L)) < 0.25
    return pack(c, t, np.clip(v + near * rng.integers(-1, 2, v.shape), 0, 15))
def setup_inputs_spread(rng):
    c = uneven(rng, (N, 8, 16, S)); v = uneven(rng, (N, 8, 16, NS * L)).reshape(N, 8, 16, NS, L)
    u = rng.random((N, 8, 16, SETS * B)); t = np.minimum((S * u * u * u * u).astype(np.int64), S - 1)
    return pack(c, np.where(rng.random(t.shape) < 0.08, S, t), v)
def setup_inputs_ends(rng):
    c = 15 * (rng.random((N, 8, 16, S)) < rng.choice(np.array([0.0, 0.25, 0.5, 0.75, 1.0]), (N, 8, 1, S)))
    c[:, 1::2, :, 0] = 15; c[..., S - 1] = 15
    kind = rng.integers(0, 4, (N, 8, 1, 1, L)); kind[..., 0] = 1; kind[..., L - 1] = 0; kind[..., L - 1 - SETS] = 0
    some = rng.random((N, 8, 16, NS, L)) < 0.5; bit = rng.random((N, 8, 1, NS, L)) < 0.5
    v = 15 * np.where(kind == 0, True, np.where(kind == 1, False, np.where(kind == 2, some, bit)))
    u = rng.random((N, 8, 16, SETS * B)); t = np.where(u < 0.4, 0, np.where(u < 0.7, S, np.where(u < 0.8, S - 1, rng.integers(1, S, u.shape))))
    tv = t.reshape(N, 8, 16, SETS, B); m = rng.random((N, 8, 1, SETS)) < 0.5; m[..., SETS - 1] = True
    late = np.array([S] * 13 + [0, S - 1, S - 1]).reshape(1, 1, 16, 1)
    tv[..., B - 1] = np.where(m, late, tv[..., B - 1])
    return pack(c, tv.reshape(N, 8, 16, SETS * B), v)
def setup_inputs_corners(rng):
    c, t = sky(rng); x = np.zeros((10, 16), np.int64)
    x[0, 0:6] = 15; x[1, 0:6] = 15; x[2, 3:6] = 15; x[3, 0:6] = 15; x[4, 0:3] = 15; x[4, 6:9] = 15; x[5, 0:3] = 15; x[6, 3:9] = 15; x[7, 6:9] = 15
    x[1, 12] = EPS // 10; x[1, 13] = EPS % 10; x[3, 12] = (EPS + 1) // 10; x[3, 13] = (EPS + 1) % 10; x[4:6, 12] = 10; x[4:6, 13] = 1
    for k, n in ((8, 675 - EPS), (9, 674 - EPS)):
        x[k, 0:2] = 15; x[k, 2] = n // 15 - 30; x[k, 3:6] = 15; x[k, 12] = (n % 15) // 10; x[k, 13] = (n % 15) % 10
    nm = np.zeros((N, 8, 10), np.int64)
    for q in range(N):
        for g in range(8):
            nm[q, g] = rng.permutation(np.concatenate([np.array([0, S - 1]), 1 + rng.permutation(S - 2)[:8]])); c[q, g][:, nm[q, g]] = x.T
    pt = np.array([[0, 0, 0, 0, 0, 0], [16, 16, 0, 0, 0, 0], [16, 15, 0, 0, 0, 0], [15, 16, 0, 0, 0, 0], [0, 16, 16, 0, 0, 0], [16, 0, 15, 0, 0, 0], [15, 0, 16, 0, 0, 0], [0, 15, 16, 0, 0, 0],
                   [1, 0, 0, 0, 0, 0], [0, 1, 0, 0, 0, 0], [0, 0, 1, 0, 0, 0], [1, 1, 0, 0, 1, 0], [1, 1, 1, 0, 1, 2], [2, 3, 0, 0, 0, 0], [3, 2, 0, 0, 1, 0], [0, 3, 2, 0, 0, 3], [0, 2, 3, 0, 0, 1],
                   [2, 0, 3, 0, 0, 0], [3, 0, 2, 0, 0, 2], [5, 5, 5, 0, 5, 10], [5, 6, 5, 0, 5, 11], [8, 8, 8, 0, 4, 8], [1, 1, 1, 0, 0, 0], [16, 16, 16, 0, 0, 0], [15, 15, 15, 0, 0, 0], [16, 16, 1, 0, 0, 0], [2, 16, 2, 0, 0, 1], [16, 0, 16, 0, 0, 0]])
    kd = rng.integers(0, len(pt), (N, 8, SETS, 5)); pos = np.argsort(rng.random((N, 8, SETS, 5, 16)), axis=-1)
    pos = np.where(rng.random((N, 8, SETS, 5, 1)) < 0.25, 15 - np.arange(16), pos); w = pt[kd][..., None, :]
    hold = ((pos[..., None] - w[..., 3:]) % 16) < w[..., :3]; way = rng.integers(0, 3, pos.shape)
    qi = np.arange(N).reshape(N, 1, 1, 1, 1); gi = np.arange(8).reshape(1, 8, 1, 1, 1)
    na = nm[qi, gi, np.where(hold[..., 0], np.array([0, 1, 8])[way], np.array([2, 3, 9])[way])]
    na = np.where((kd[..., None] == 0) & (rng.random(pos.shape) < 0.5), S, na)
    nb = nm[qi, gi, np.where(hold[..., 2], 4, 5)]; ne = nm[qi, gi, np.where(hold[..., 1], 6, 7)]
    tv = t.reshape(N, 8, 16, SETS, B)
    for k in range(5):
        for y, z in ((na, 1), (nb, 6), (ne, 11)): tv[..., (15 * (k + z)) >> SH] = y[:, :, :, k].transpose(0, 1, 3, 2)
    k = rng.integers(1, 6, (N, 8, L)); v = np.zeros((N, 8, 16, NS, L), np.int64)
    v[:, :, 9:12, 0] = 15; v[:, :, 0:6, 1] = 15; v[:, :, 9, 1] = k; v[:, :, 0:3, 2] = 15; v[:, :, 6:9, 2] = 15; v[:, :, 10, 2] = k + 5; v[:, :, 3:9, 3] = 15; v[:, :, 11, 3] = k + 10
    v[:, :, :, 4:] = np.take_along_axis(v, rng.integers(1, 4, (N, 8, 1, NS - 4, L)), 3)
    v = np.where(rng.random((N, 8, 1, 1, L)) < 0.2, rng.integers(0, 16, v.shape), v)
    return pack(c, tv.reshape(N, 8, 16, SETS * B), v)
def setup_inputs_crowd(rng):
    M = NS + N; base = rng.integers(0, 16, (8, SETS, 16, M)); D = np.einsum("ghfj,ghfk->ghjk", base, base)
    c, t = sky(rng); nm = np.argsort(rng.random((N, 8, S)), axis=-1)[..., :SETS * M].reshape(N, 8, SETS, M); tv = t.reshape(N, 8, 16, SETS, B)
    gi = np.arange(8).reshape(8, 1, 1); hi = np.arange(SETS).reshape(1, SETS, 1); pi = np.arange(16).reshape(1, 1, 16)
    for q in range(N):
        for g in range(8): c[q, g][:, nm[q, g].reshape(-1)] = base[g].transpose(1, 0, 2).reshape(16, -1)
        kind = rng.integers(0, 3, (8, SETS, 1)); miss = rng.integers(0, 16, (8, SETS, 1))
        prs = [(k, k + z) for k in list(range(M - 2, -1, -1)) + [q + N] for z in (3, 2, 1) if k + z < M] + [(q, j) for j in list(range(q)) + list(range(M - 1, q, -1))]
        for k, j in prs:
            know = np.where(kind == 0, True, np.where(kind == 1, pi != miss, rng.random((8, SETS, 16)) < 0.6)); bn = (D[:, :, k, j] >> SH)[:, :, None]
            tv[q, gi, pi, hi, bn] = np.where(know, nm[q, :, :, j][:, :, None], tv[q, gi, pi, hi, bn])
    v = np.zeros((N, 8, 16, NS, L), np.int64); hl = np.arange(L) % SETS
    for r in range(N):
        o = np.zeros((8, L, NS), np.int64) + np.arange(NS) + r
        o[2::4, :, 2:] = 2 + r + np.argsort(rng.random((2, L, NS - 2)), axis=-1)
        odd = (np.arange(L) // SETS) % 2 == 1; o[3::4, odd, 1] = 2 + r; o[3::4, odd, 2] = 1 + r
        v[r] = base[gi, hl.reshape(1, L, 1), :, o].transpose(0, 3, 2, 1)
        for g in (1, 5):
            ln = np.arange(SETS) + SETS * rng.integers(0, L // SETS, SETS); v[r, g][:, :, ln] = rng.integers(0, 16, (16, NS, SETS))
    return pack(c, tv.reshape(N, 8, 16, SETS * B), v)
def setup_inputs_full(rng):
    d = setup_inputs(rng); c = d["cvec"].astype(np.float32).astype(np.int64).reshape(N, 8, 16, S); t = d["tsee"].astype(np.int64).reshape(N, 8, 16, SETS * B); v = d["obs"].astype(np.float32).astype(np.int64).reshape(N, 8, 16, NS, L)
    lane = np.arange(L); lo = ((EPS + 1) >> SH) + 1; hi = (2923 - EPS) >> SH
    for g in (0, 2, 5, 7):
        bn = np.argsort(rng.random((SETS, hi - lo)), axis=1)[:, :L // SETS] + lo
        D = ((bn << SH) + rng.integers(0, 1 << SH, bn.shape)).T.reshape(L)
        if g >= 5: D[1] = EPS; D[2] = EPS + 1
        col = B * (lane % SETS) + (D >> SH)
        for q in range(N):
            nm = rng.permutation(S)[:8 * L].reshape(L, 8)
            off = rng.integers(1 - EPS, EPS, (L, 8)); off[:, :4] = np.array([EPS, -EPS, EPS + 1, -EPS - 1])
            x = sized(np.maximum(D[:, None] + off, 0)); x = np.take_along_axis(x, np.argsort(rng.random(x.shape), axis=-1), -1)
            c[q, g][:, nm.reshape(-1)] = x.reshape(-1, 16).T
            h0 = rng.integers(0, 16, L); h0[0] = 0; h0[L - 1] = 15
            good = rng.random((L, 16)) < rng.random((L, 1)) * (g > 0); good[L - 1] = False; good[lane, h0] = True
            on = np.array([0, 1, 4, 5, 6, 7])[(rng.integers(0, 6, (L, 1)) + np.arange(16)) % 6]
            name = np.take_along_axis(nm, np.where(good, on, rng.integers(2, 4, (L, 16))), 1)
            name = np.where(~good & (rng.random((L, 16)) < 0.25), S, name)
            if g >= 5: name[1] = np.where(np.arange(16) < h0[1], nm[1, 2], S)
            t[q, g][:, col] = name.T
            y = sized(D); y = np.take_along_axis(y, np.argsort(rng.random(y.shape), axis=-1), -1); v[q, g] = y.T[:, None, :]
    return pack(c, t, v)
def check_inputs(d):
    bad = []
    for k, hi in (("cvec", 15), ("tsee", S), ("obs", 15)):
        x = np.asarray(d[k]).astype(np.float32)
        if not np.all((x >= 0) & (x <= hi) & (x == np.floor(x))): bad.append("range of " + k)
    return bad
def reference(cvec, tsee, obs):
    c = cvec.astype(np.float32).astype(np.int32).reshape(N, 8, 16, S); c = np.concatenate([c, np.zeros((N, 8, 16, 1), np.int32)], axis=3)
    t = tsee.astype(np.int64).reshape(N, 8, 16, SETS * B); v = obs.astype(np.float32).astype(np.int64).reshape(N, 8, 16, NS, L)
    gram = np.einsum("rgfjl,rgfkl->rgjkl", v, v)
    st = np.zeros((N, 4, 8, L), np.int64) + np.arange(4).reshape(1, 4, 1, 1)
    gi = np.arange(8).reshape(8, 1); ln = np.arange(L).reshape(1, L); first = B * (ln % SETS)
    out = np.zeros((N, 8, RO, 3, L), np.float32)
    for rnd in range(RO):
        for q in range(N):
            r = (q - rnd) % N
            o, a, b, e = st[r, 0], st[r, 1], st[r, 2], st[r, 3]; G = gram[r]
            col = [first + (G[gi, o, z, ln] >> SH) for z in (a, b, e)]
            nam = [np.take_along_axis(t[q], k[:, None, :], 2) for k in col]
            vec = [np.take_along_axis(c[q], k.reshape(8, 1, 16 * L), 2).reshape(8, 16, 16, L) for k in nam]
            hold = [np.abs(np.sum(vec[i] * vec[j], axis=1) - G[gi, y, z, ln][:, None, :]) <= EPS for i, j, y, z in ((0, 1, a, b), (0, 2, a, e), (1, 2, b, e))]
            every = hold[0] & hold[1] & hold[2]; found = np.any(every, axis=1); p = np.argmax(every, axis=1)
            for k in range(3): out[q, :, rnd, k] = np.where(found, np.take_along_axis(nam[k], p[:, None, :], 1)[:, 0], -1)
            if rnd == RO - 1: continue
            for g in range(8):
                w = np.nonzero(found[g])[0]; cs, at = np.unique(col[0][g, w], return_index=True); t[q, g, p[g, w[at]], cs] = S
            ab, ac, bc = [np.sum(k, axis=1) for k in hold]
            spike = np.argmin(np.stack([ab + ac, ab + bc, ac + bc]), axis=0); nxt = rnd + 4
            st[r] = np.stack([np.where(found, a, o), np.where(found, b, np.where(spike == 0, nxt, a)), np.where(found, e, np.where(spike == 1, nxt, b)), np.where(found, nxt, np.where(spike == 2, nxt, e))])
    return {"yn": out.reshape(N, 8, RO * 3 * L)}

@@ -1,0 +1,442 @@
+from concourse.mybir import AluOpType, ActivationFunctionType, AxisListType
+
+A, F = AluOpType, ActivationFunctionType
+RO, NB = 4, 4
+M = 12582912.0
+W = 32768.0
+NQ = [21, 15, 10, 6]
+PAIRS = [(2, 3), (1, 3), (1, 2), (0, 2), (0, 3), (0, 1)] + [(j, 4) for j in range(4)] + [(j, 5) for j in range(5)] + [(j, 6) for j in range(6)]
+BC, AC, AB, OB, OC, OA, ON, AN, BN, CN = range(10)
+
+
+def upd(b):
+    return [[b + 1, b, b, b], [b + 2, b + 4, b + 1, b + 1], [b + 3, b + 2, b + 4, b + 2], [b + 4, b + 3, b + 3, b + 4]]
+
+
+PI = [[CN, BC, CN, BN], [BN, CN, AC, AN], [BC, BN, AN, AB], [AC, OB, ON, OB], [AN, OC, OC, ON], [AB, ON, OA, OA]] + upd(10) + upd(15) + [[20] * 4]
+MIX = [[[0, 1, 0, 0], [0, 1, 0, 0]], [[0, 1, 0, 0], [0, 0, 1, 0]], [[0, 1, 0, 1], [1, 0, 0, 0]], [[0, 0, 1, 1], [1, 1, 1, 0]]]
+SLACK, EARLY, LATE, SEED, NOISE = 0.0, 1.1, 1.6, 0, 0.0
+CYC, GAM, PEC, HOP = 0.83, 1.56, 0.42, 200.0
+
+S_, P_, B_, F_, H_, U_, I_ = "sbuf", "psum", "bfloat16", "float32", "float16", "uint16", "int32"
+SCRATCH = {}
+for _n, _w, _d in [
+        ("ob", 1792, B_), ("cv", 2064, B_), ("ones", 2048, B_), ("idb", 128, B_), ("id4", 128, B_), ("idf", 128, F_),
+        ("d8a", 8, B_), ("d8", 8, B_), ("d8f", 8, F_), ("e2", 144, B_), ("eo", 32, H_), ("eo3", 24, B_), ("off0", 24, F_), ("off", 24, F_), ("pint", 16, I_), ("pf", 24, F_), ("rs4", 480, F_),
+        ("ee0", 384, B_), ("ee", 384, B_), ("cst", 384, B_), ("t1", 256, B_), ("binw", 912, B_), ("wt0", 320, B_), ("wt1", 320, B_), ("wt", 320, B_),
+        ("c2k", 128, B_), ("geo", 64, F_), ("cw", 8, B_), ("bcm", 2048, B_), ("rg0", 128, B_), ("rg1", 128, B_), ("rg", 128, B_),
+        ("mk0", 256, F_), ("mk1", 256, F_), ("mk2", 256, F_), ("mk", 256, B_), ("h4", 8, B_), ("dum", 16, F_), ("rst", 64, F_),
+        ("lv", 96, I_), ("lf", 128, F_), ("lg", 24, F_), ("l1", 32, U_), ("l2", 32, U_), ("l3", 16, U_), ("l4", 24, U_), ("ot", 256, F_)]:
+    SCRATCH[_n] = (S_, [128, _w], _d)
+SCRATCH["gp"] = (S_, [128, 21, 256], B_)
+SCRATCH["yb"] = (S_, [128, 4, 256], F_)
+for _c in "01":
+    for _n, _w, _d in [
+            ("raw", [904], I_), ("tab", [1032], F_), ("gm", [4, 192], F_), ("nx", [3, 120], F_), ("cl", [24], U_), ("nf", [384], F_), ("nu", [384], U_),
+            ("xh", [56], B_), ("xt", [128], B_), ("bh", [128], B_), ("cand", [480], F_), ("va", [2048], B_), ("vb", [2048], B_), ("vc", [2048], B_),
+            ("pr", [2048], B_), ("pw", [2048], F_), ("yy", [128], F_), ("yz", [128], F_), ("ab", [384], B_), ("hf", [384], B_), ("ev", [128], B_), ("mi", [64], F_), ("cd", [8], B_),
+            ("pm", [480], F_), ("pn", [480], F_), ("ohb", [128], B_), ("ohf", [128], F_), ("sel", [384], H_), ("fl", [256], B_), ("so", [8], F_), ("su", [8], U_)]:
+        SCRATCH[_n + _c] = (S_, [128] + _w, _d)
+for _n in ["rp0", "rp1", "mp0", "mp1", "up0", "up1", "up2", "up3"]:
+    SCRATCH[_n] = (P_, [128, 512], F_)
+SEMAPHORES = ["v", "s", "p", "g", "sent", "o0", "o1", "cv", "t0", "t1", "y0", "y1", "y2", "y3"] + ["a%d%d" % (t, c) for t in range(1, 4) for c in range(2)]
+
+
+def build(g, T, dst):
+    ops = []; stage = [99.0]; crit = [0]
+    V, S, P = g.vector, g.scalar, g.tensor
+
+    def op(eng, rd, wr, ns, fn, bank=None, sem=None, lat=0.0):
+        fx = {"v": 50.0, "s": 65.0, "p": 60.0}.get(eng, ns)
+        ops.append({"fx": fx, "n": (ns - fx) / (PEC if eng == "p" else CYC), "ga": any(wr[0].startswith(x) for x in ("va", "vb", "vc", "nf", "nu", "bh", "cand", "pm", "yb", "sel")) and bank is None,
+                    "e": eng, "r": rd, "w": wr, "ns": ns, "fn": fn, "b": bank, "sem": sem, "lat": lat, "k": stage[0], "c": crit[0]})
+
+    def v(rd, wr, n, fn, bank=None): op("v", rd, wr, 50 + max(n, 16) * CYC, fn, bank)
+    def s(rd, wr, n, fn, bank=None): op("s", rd, wr, 65 + max(n, 16) * CYC, fn, bank)
+    def gp(rd, wr, n, fn): op("g", rd, wr, 170 + 2 * n * CYC, fn)
+
+    def pe(rd, wr, mms, bank):
+        def fn():
+            for (o, l, r, a, z, n) in mms: last = P.matmul(o, l, r, a, z)
+            return last
+        op("p", rd, wr, 60 + sum(m[5] for m in mms) * PEC, fn, bank)
+
+    def ts(o, i, a, b, o0, o1=None):
+        return (lambda: V.tensor_scalar(o, i, a, None, o0)) if o1 is None else (lambda: V.tensor_scalar(o, i, a, b, o0, o1))
+
+    def tt(o, i, j, f): return lambda: V.tensor_tensor(o, i, j, f)
+    def cp(o, i): return lambda: V.tensor_copy(o, i)
+    def ms(o, x): return lambda: V.memset(o, x)
+    def scan(o, i, j, x, f0, f1): return lambda: V.tensor_tensor_scan(o, i, j, x, f0, f1)
+    def act(o, i, f, **k): return lambda: S.activation(o, i, f, **k)
+    def io(o, pat, b, cm): return lambda: g.iota(o, pat, b, cm, allow_small_or_imprecise_dtypes=True)
+    def ioi(o, pat, b, cm): return lambda: g.iota(o, pat, b, cm)
+    def sl(o, i, pat, f, b, cm): return lambda: g.affine_select(o, i, pat, f, 0.0, b, cm)
+    def dma(q, rd, wr, o, i, sem, lat): op(q, rd, wr, 60, lambda: (g.sync if q == "y" else S).dma_start(o, i), None, sem, lat)
+
+    dma("y", [], ["ob0"], T.ob[:, 0:1024], T.obs[:, 0:1024], "o0", 2500)
+    for c in range(2):
+        for h in range(4):
+            dma("s" if c == 0 else "y", [], ["raw%d.%d" % (c, h)], T["raw%d" % c][:, 226 * h:226 * h + 226],
+                T.tsee[:, 226 * (2 * h + c):226 * (2 * h + c) + 226], "t%d" % c, 4000 + 3000 * c)
+        if c == 0:
+            dma("y", [], ["cv"], T.cv[:, 0:2048], T.cvec[:, :], "cv", 5000)
+            dma("y", [], ["ob1"], T.ob[:, 1024:1792], T.obs[:, 1024:1792], "o1", 5500)
+
+    v([], ["on1"], 192, ms(T.ones[:, 0:384], 1.0))
+    gp(["on1"], ["idb"], 128, sl(T.idb[:, :], T.ones[:, 0:128], [[-1, 128]], A.is_equal, 0, 1))
+    gp(["on1"], ["d8a"], 8, sl(T.d8a[:, :], T.ones[:, 0:8], [[-16, 8]], A.is_ge, 0, 1))
+    gp(["d8a"], ["d8"], 8, sl(T.d8[:, :], T.d8a[:, :], [[16, 8]], A.is_ge, 15, -1))
+    v([], ["e2"], 72, ms(T.e2[:, :], 0.0))
+    v(["d8"], ["e2"], 8, cp(T.e2[:, 15:143:16], T.d8[:, :]))
+    gp([], ["off0"], 24, io(T.off0[:, :], [[0, 6], [226, 4]], 0, 0))
+    v(["off0"], ["off"], 24, ts(T.off[:, :], T.off0[:, :], M, None, A.add))
+    v([], ["cvz"], 8, ms(T.cv[:, 2048:2064], 0.0))
+    s(["idb"], ["idf"], 128, act(T.idf[:, :], T.idb[:, :], F.Copy))
+    s(["idb"], ["id4"], 128, act(T.id4[:, :], T.idb[:, :], F.Copy, scale=4096.0))
+    s(["d8"], ["d8f"], 8, act(T.d8f[:, :], T.d8[:, :], F.Copy))
+    v([], ["ee0"], 192, ms(T.ee0[:, :], -16.0))
+    v([], ["ee0"], 64, ms(T.ee0[:, 128:256], -65536.0))
+    gp(["ee0"], ["ee0"], 384, sl(T.ee0[:, :], T.ee0[:, :], [[-2, 24], [0, 16]], A.is_ge, -8, 1))
+    gp(["ee0"], ["ee", "eeb"], 384, sl(T.ee[:, :], T.ee0[:, :], [[2, 24], [0, 16]], A.is_ge, 9, -1))
+    v([], ["cst"], 192, ms(T.cst[0:64, :], 0.0))
+    for r0, c0, x in ((0, 0, -7.5), (0, 128, -30720.0), (32, 128, -1800.0), (0, 256, -7.5), (32, 256, 1800.0)):
+        v([], ["cst"], 64, ms(T.cst[r0:r0 + 1, c0:c0 + 128], x))
+    gp([], ["lv0"], 1, ioi(T.lv[:, 0:1], [[0, 1]], 0, 1))
+    for k, (sh, an) in enumerate([(3, 1), (0, 15), (0, 7), (6, 1), (0, 1), (1, 7), (4, 3)]):
+        v(["lv0"], ["pi%d" % k], 1, ts(T.pint[:, k:k + 1], T.lv[:, 0:1], sh, an, A.logical_shift_right, A.bitwise_and))
+    v(["pi%d" % k for k in range(3)], ["pf"], 8, cp(T.pf[:, 0:3], T.pint[:, 0:3]))
+    v(["pi%d" % k for k in range(3, 7)], ["pg"], 8, cp(T.pf[:, 3:7], T.pint[:, 3:7]))
+    HI, P16, P8, KK, P2, PH, K4 = [T.pf[:, k:k + 1] for k in range(7)]
+    gp([], ["lg"], 24, io(T.lg[:, :], [[128, 3], [2, 8]], 0, 0))
+    v(["pf"], ["pq4"], 1, ts(T.pf[:, 13:14], P8, 16.0, HI, A.mult, A.add))
+    v(["lg", "pq4"], ["l4"], 24, ts(T.l4[:, :], T.lg[:, :], T.pf[:, 13:14], None, A.add))
+    WT = [[(0, 0), (2, 2), (-2, 0), (-2, 0)], [(0, 0), (-2, 0), (2, 2), (0, -2)], [(0, 0), (0, -2), (0, -2), (2, 2)],
+          [(64, 64), (-64, -64), (-64, -64), (-64, -64)], [(-1, -1), (1, 1), (-1, 1), (-1, -1)]]
+    names = []
+    for e in range(5):
+        k = 0
+        while k < 4:
+            n = 1
+            while k + n < 4 and WT[e][k + n] == WT[e][k]: n += 1
+            x, y = WT[e][k]
+            gp([], ["wt0.%d.%d" % (e, k)], 16 * n, io(T.wt0[:, 64 * e + 16 * k:64 * e + 16 * (k + n)], [[0, 8 * n], [y - x, 2]], x, 0))
+            names.append("wt0.%d.%d" % (e, k)); k += n
+    gp(names, ["wt1"], 320, sl(T.wt1[:, :], T.wt0[:, :], [[0, 20], [-16, 8], [0, 2]], A.is_ge, 0, 1))
+    gp(["wt1"], ["wt"], 320, sl(T.wt[:, :], T.wt1[:, :], [[0, 20], [16, 8], [0, 2]], A.is_ge, 15, -1))
+    gp([], ["c2k"], 128, io(T.c2k[:, :], [[0, 128]], int(W) // 16, 0))
+    gp([], ["rst"], 64, io(T.rst[:, :], [[0, 32], [-32767, 2]], 32767, 0))
+    s(["rst"], ["rst"], 64, act(T.rst[:, :], T.rst[:, :], F.Copy, scale=2.0 ** 20))
+    v([], ["ge0"], 16, ms(T.geo[:, 0:16], 2.0 ** -9))
+    v([], ["ge1"], 16, ms(T.geo[:, 16:32], 0.0))
+    v(["ge0", "ge1"], ["ge2"], 16, scan(T.geo[:, 32:48], T.geo[:, 0:16], T.geo[:, 16:32], 2.0 ** 57, A.mult, A.add))
+    gp([], ["lf0"], 16, io(T.lf[:, 0:16], [[1, 16]], 0, 0))
+    v(["lf0", "pf"], ["lf1"], 16, ts(T.lf[:, 16:32], T.lf[:, 0:16], P16, None, A.is_equal))
+    v(["lf1", "ge2"], ["ge3"], 32, tt(T.geo[:, 48:64], T.lf[:, 16:32], T.geo[:, 32:48], A.mult))
+    v(["ge3"], ["wp"], 16, lambda: V.tensor_reduce(T.pf[:, 8:9], T.geo[:, 48:64], AxisListType.X, A.add))
+    v(["wp", "d8"], ["cw"], 8, ts(T.cw[:, :], T.d8[:, :], T.pf[:, 8:9], None, A.mult))
+    v(["wp"], ["wq"], 1, ts(T.pf[:, 9:10], T.pf[:, 8:9], W, None, A.mult))
+    for q in range(15):
+        gp([], ["lv1.%d" % q], 2, io(T.lf[:, 32 + 2 * q:34 + 2 * q], [[0, 2]], 2 * sum(PI[q][x] * 32 ** x for x in range(4)) + 1, 0))
+    for k, (sh, an) in enumerate([(0, 3), (2, 3), (1, 1)]):
+        v(["lv0"], ["pj%d" % k], 1, ts(T.pint[:, 8 + k:9 + k], T.lv[:, 0:1], sh, an, A.logical_shift_right, A.bitwise_and))
+    v(["pj0", "pj1", "pj2"], ["ph"], 8, cp(T.pf[:, 16:19], T.pint[:, 8:11]))
+    v(["pg"], ["pq6"], 1, ts(T.pf[:, 19:20], P2, -31.0 / 64, 0.5, A.mult, A.add))
+    v(["ph"], ["pq7"], 1, ts(T.pf[:, 20:21], T.pf[:, 18:19], -1023.0 / 1024, 1.0, A.mult, A.add))
+    v(["pq6", "pq7"], ["pq8"], 1, tt(T.pf[:, 21:22], T.pf[:, 19:20], T.pf[:, 20:21], A.mult))
+    v(["pq8"] + ["lv1.%d" % q for q in range(15)], ["lf2"], 30, ts(T.lf[:, 64:94], T.lf[:, 32:62], T.pf[:, 21:22], -0.5, A.mult, A.add))
+    v(["lf2"], ["lf3"], 30, ts(T.lf[:, 96:126], T.lf[:, 64:94], M, None, A.add))
+    v(["lf3"], ["lv2"], 30, ts(T.lv[:, 32:62], T.lf[:, 96:126], -M, None, A.add))
+    v(["lv2"], ["lv3"], 30, ts(T.lv[:, 64:94], T.lv[:, 32:62], 31, None, A.bitwise_and))
+    v(["lv3", "ph"], ["lf2"], 30, ts(T.lf[:, 64:94], T.lv[:, 64:94], 8.0, T.pf[:, 17:18], A.mult, A.add))
+    gp([], ["mk2"], 30, io(T.mk2[:, 0:30], [[0, 15], [4, 2]], 0, 0))
+    v(["lf2", "mk2"], ["lf3"], 60, tt(T.lf[:, 96:126], T.lf[:, 64:94], T.mk2[:, 0:30], A.add))
+    v(["lf3"], ["l1"], 30, cp(T.l1[:, 0:30], T.lf[:, 96:126]))
+    v(["ph"], ["pq9"], 1, ts(T.pf[:, 15:16], T.pf[:, 16:17], 8.0, T.pf[:, 17:18], A.mult, A.add))
+    v(["pq9"], ["pq5"], 1, ts(T.pf[:, 14:15], T.pf[:, 15:16], 2.0, 1.0, A.mult, A.add))
+    v(["mk2", "pq5", "l1"], ["l2"], 30, ts(T.l2[:, 0:30], T.mk2[:, 0:30], 2.0, T.pf[:, 14:15], A.mult, A.add))
+    gp([], ["rs4"], 480, io(T.rs4[:, :], [[0, 120], [1, 4]], 0, 0))
+    v(["rs4"], ["rs4"], 480, ts(T.rs4[:, :], T.rs4[:, :], 0.0, -2.0 ** 40, A.is_equal, A.mult))
+    v(["pg"], ["pq0"], 1, ts(T.pf[:, 10:11], P2, 128.0, None, A.mult))
+    v(["pg", "pq0"], ["pq1"], 1, ts(T.pf[:, 11:12], PH, 16.0, T.pf[:, 10:11], A.mult, A.add))
+    v(["lf0", "pq1"], ["l3"], 16, ts(T.l3[:, :], T.lf[:, 0:16], T.pf[:, 11:12], None, A.add))
+    v([], ["on2"], 832, ms(T.ones[:, 384:2048], 1.0))
+    gp(["on1", "on2"], ["bcm"], 2048, sl(T.bcm[:, :], T.ones[:, :], [[-1, 16], [-16, 8], [0, 16]], A.is_equal, 0, 1))
+    v(["d8"], ["eo"], 8, ts(T.eo[:, :], T.ones[:, 0:32], 0.0, None, A.mult))
+    v(["d8"], ["eo"], 8, cp(T.eo[:, 2:26:3], T.d8[:, :]))
+    for m in range(3):
+        s(["d8"], ["eo3.%d" % m], 8, act(T.eo3[:, m:24:3], T.d8[:, :], F.Copy, scale=1.0 / 4096))
+    gp([], ["ot0", "ot1"], 256, io(T.ot[:, :], [[0, 256]], 0, 0))
+    gp([], ["binw"], 904, io(T.binw[:, 0:904], [[0, 4], [1, 226]], 0, 0))
+    for kk in range(2):
+        gp(["on1"], ["t1.%d" % kk], 128, sl(T.t1[:, 128 * kk:128 * kk + 128], T.ones[:, 0:128], [[0, 2], [-1, 4], [0, 16]], A.is_equal, -4 * kk, 1))
+    gp(["on1"], ["rg0"], 128, sl(T.rg0[:, :], T.ones[:, 0:128], [[-16, 8], [0, 16]], A.is_ge, 0, 1))
+    gp(["rg0"], ["rg1"], 128, sl(T.rg1[:, :], T.rg0[:, :], [[16, 8], [0, 16]], A.is_ge, 15, -1))
+    s(["rg1"], ["rg"], 128, act(T.rg[:, :], T.rg1[:, :], F.Copy, scale=-0.0625))
+    gp([], ["mk0"], 256, io(T.mk0[:, :], [[-1, 2], [0, 8], [-2, 16]], 0, 0))
+    v(["pg", "pf"], ["pq2"], 1, ts(T.pf[:, 12:13], P16, 2.0, KK, A.mult, A.add))
+    v(["mk0", "pq2"], ["mk1"], 256, ts(T.mk1[:, :], T.mk0[:, :], T.pf[:, 12:13], 512.0, A.add, A.mult))
+    v(["mk1", "l2"], ["mk2"], 256, ts(T.mk2[:, :], T.mk1[:, :], -0.5, 256.0, A.mult, A.min))
+    v(["mk1", "mk2"], ["mk"], 512, tt(T.mk[:, :], T.mk1[:, :], T.mk2[:, :], A.max))
+    v(["lf0", "pg"], ["h4"], 4, ts(T.h4[:, 0:4], T.lf[:, 0:4], K4, 4096.0, A.is_equal, A.mult))
+    gp([], ["du0"], 8, io(T.dum[:, 8:16], [[16, 8]], int(M) + 904, 0))
+    v(["du0", "pf"], ["dum"], 8, ts(T.dum[:, 0:8], T.dum[:, 8:16], P16, None, A.add))
+
+    def oc(j): return slice(256 * j, 256 * j + 256)
+    place = {1: (0, 0), 2: (0, 1), 3: (1, 0), 4: (2, 0), 5: (2, 1), 6: (3, 0)}
+    def pj(j): return T["up%d" % place[j][0]][:, oc(place[j][1])]
+    for u, js in ((0, [1, 2]), (1, [3]), (2, [4, 5]), (3, [6])):
+        pe(["idb", "ob0" if u < 2 else "ob1"], ["up%d" % u], [(T["up%d" % u][:, 0:256 * len(js)], T.idb[:, :], T.ob[:, 256 * js[0]:256 * (js[-1] + 1)], True, True, 256 * len(js))], "up%d" % u)
+
+    def gram(q0, q1):
+        for q in range(q0, q1):
+            j, k = PAIRS[q]; u = "up%d" % place[k][0]
+            v(["ob0" if j < 4 else "ob1", u], ["gp%d" % q], 256, tt(T.gp[:, q, :], T.ob[:, oc(j)], pj(k), A.mult), u)
+        for c in range(2):
+            n = 8 * (q1 - q0); mp = T["mp%d" % c]
+            pe(["e2"] + ["gp%d" % q for q in range(q0, q1)], ["mg%d" % c],
+               [(mp[:, 0:n], T.e2[:, 15 - r:143 - r], T.gp[:, q0:q1, 16 * r + c:16 * r + 16:2], r == 0, r == 15, max(64, n)) for r in range(16)], "mp%d" % c)
+            s(["mg%d" % c], ["g%d0.%d" % (c, q0)], n, act(T["gm%d" % c][:, 0, 24 + 8 * q0:24 + 8 * q1], mp[:, 0:n], F.Copy, scale=0.0625, bias=-0.46875), "mp%d" % c)
+    gram(3, 6)
+    for c in range(2):
+        v(["raw%d.%d" % (c, h) for h in range(4)], ["tab%d" % c], 904, cp(T["tab%d" % c][:, 0:904], T["raw%d" % c][:, :]))
+        gp([], ["tad%d" % c], 128, io(T["tab%d" % c][:, 904:1032], [[0, 128]], 0, 0))
+    gram(0, 3)
+    gram(6, 21)
+
+    ubank = [0]
+    def nextu():
+        ubank[0] = (ubank[0] + 1) % 4
+        return "up%d" % ubank[0]
+
+    win = T.cv[:, 0:2064]
+    for t in range(RO):
+        for c in range(2):
+            def b(n): return T[n + str(c)]
+            def k(n): return n + str(c)
+            G = b("gm"); last = t == RO - 1
+            gO, gE, gN = (["g%d0.3" % c], ["g%d0.0" % c], ["g%d0.6" % c]) if t == 0 else (["g%d%d" % (c, t)],) * 3
+            cf = "cf%d%d" % (c, t); rp, mp = b("rp"), b("mp")
+            stage[0] = 2 * t + c - EARLY; crit[0] = 1
+            v(gO + ["off"], [cf], 48, tt(G[:, t, 0:24], G[:, t, 48:72], T.off[:, :], A.add))
+            v([cf], [k("cl")], 24, ts(b("cl")[:, :], G[:, t, 0:24], -M, None, A.add))
+            nfs = [k("nf0"), k("nf1"), k("nf2")]
+            for m0, m1 in SPLIT:
+                s([k("cl"), k("tab")], nfs[m0:m1], 128 * (m1 - m0) * GAM, act(b("nf")[:, 128 * m0:128 * m1], b("tab")[:, 0:904].indirect(b("cl")[:, 8 * m0:8 * m1]), F.Copy))
+                v(nfs[m0:m1] + ["l4"], [k("nu%d" % m) for m in range(m0, m1)], 128 * (m1 - m0) * GAM,
+                  cp(b("nu")[:, 128 * m0:128 * m1], b("nf")[:, 128 * m0:128 * m1].indirect(T.l4[:, 0:8 * (m1 - m0)])))
+            crit[0] = 0
+            v([cf, "off"], [k("xb")], 16, tt(b("xh")[:, 0:8], G[:, t, 16:24], T.off[:, 0:8], A.subtract))
+            s(gE, [k("xu")], 24, act(b("xh")[:, 8:56:2], G[:, t, 24:48], F.Copy))
+            v(gE + [k("xu")], [k("xl")], 48, tt(b("xh")[:, 9:56:2], G[:, t, 24:48], b("xh")[:, 8:56:2], A.subtract))
+            pe([k("xb"), k("xu"), k("xl"), "idb"], [k("mx")], [(mp[0:56, 0:128], b("xh")[:, :], T.idb[:, :], True, True, 128)], k("mp"))
+            s([k("mx")], [k("xt")], 128, act(b("xt")[0:56, :], mp[0:56, 0:128], F.Copy), k("mp"))
+            if not last:
+                nq = NQ[t + 1]
+                s([k("cl"), "binw"], [k("bh")], 128 * GAM, act(b("bh")[:, :], T.binw[:, 0:904].indirect(b("cl")[:, 16:24]), F.Copy))
+                s(gO + gE + gN + ["l1"], [k("cand")], 32 * nq * GAM, act(b("cand")[:, 0:32 * nq], G[:, t, 24:24 + 8 * NQ[t]].indirect(T.l1[:, 0:2 * nq]), F.Copy))
+            stage[0] = 2 * t + c
+            def sub(e, col): return (rp[:, 128 * col:128 * col + 128], T.ee[0:56, 128 * e:128 * e + 128], b("xt")[0:56, :], False, False, 128)
+            pe(["cst", "on1"], [k("rd0"), k("rd1"), k("rd2")], [(rp[:, 0:384], T.ones[0:64, 0:128], T.cst[0:64, 0:384], True, False, 384)], k("rp"))
+            pe([k("xt"), "ee", "eeb", k("rd0")], [k("rx")], [sub(0, 0), sub(1, 1), sub(2, 2)], k("rp"))
+            red = [k("rx")]
+            NB = len(CUT) - 1
+            for n in range(NB):
+                R = range(CUT[n], CUT[n + 1]); E = 128 * len(R); cs = slice(128 * CUT[n], 128 * CUT[n + 1]); x = "%d.%d" % (c, n)
+                def gat(m): return win.indirect(b("nu")[:, 128 * m + 8 * CUT[n]:128 * m + 8 * CUT[n + 1]])
+                cvr = ["cv", "cvz"]
+                s(cvr + [k("nu0")], ["vb" + x], E * GAM, act(b("vb")[:, cs], gat(0), F.Copy))
+                s(cvr + [k("nu1")], ["vc" + x], E * GAM, act(b("vc")[:, cs], gat(1), F.Copy))
+                if MIX[t][c][n]: v(cvr + [k("nu2")], ["va" + x], E * GAM, cp(b("va")[:, cs], gat(2)))
+                else: s(cvr + [k("nu2")], ["va" + x], E * GAM, act(b("va")[:, cs], gat(2), F.Copy))
+                ub, uc = nextu(), nextu()
+                pe(["vb" + x, "vc" + x, "idb", "id4"], [ub], [(T[ub][:, 0:E], T.idb[:, :], b("vb")[:, cs], True, False, E), (T[ub][:, 0:E], T.id4[:, :], b("vc")[:, cs], False, True, E)], ub)
+                pe(["vb" + x, "idb"], [uc], [(T[uc][:, 0:E], T.idb[:, :], b("vb")[:, cs], True, True, E)], uc)
+                v(["va" + x, ub], ["p1" + x], E, tt(b("pw")[:, cs], b("va")[:, cs], T[ub][:, 0:E], A.mult), ub)
+                v(["vc" + x, uc], ["p0" + x], E, tt(b("pr")[:, cs], b("vc")[:, cs], T[uc][:, 0:E], A.mult), uc)
+                pe(["p1" + x, "d8f", k("rd0")], ["r1" + x], [(rp[:, 128 + r:256:16], b("pw")[:, 128 * r:128 * r + 128], T.d8f[:, :], False, False, 256) for r in R], k("rp"))
+                red.append("r1" + x)
+                pe(["p0" + x, "d8", k("rd0")] + (red if n == NB - 1 else []), ["r0" + x],
+                   [(rp[:, r:128:16], b("pr")[:, 128 * r:128 * r + 128], T.d8[:, :], False, r == 15, 64) for r in R], k("rp"))
+                red.append("r0" + x)
+            crit[0] = 1
+            v(red, [k("yy")], 128, ts(b("yy")[:, :], rp[:, 128:256], 1.5 * 2.0 ** 35, -1.5 * 2.0 ** 35, A.add, A.add), k("rp"))
+            v([k("yy")] + red, [k("yz")], 128, tt(b("yz")[:, :], rp[:, 256:384], b("yy")[:, :], A.subtract), k("rp"))
+            v([k("yz")], [k("rd1")], 128, tt(rp[:, 128:256], rp[:, 128:256], b("yz")[:, :], A.add), k("rp"))
+            s([k("yy")], [k("ac")], 128, act(b("ab")[:, 256:384], b("yy")[:, :], F.Abs, scale=1.0 / 4096))
+            s([k("rd0"), k("rd1")], [k("ab")], 256, act(b("ab")[:, 0:256], rp[:, 0:256], F.Abs), k("rp"))
+            v([k("ab"), k("ac")], [k("hf")], 192, ts(b("hf")[:, :], b("ab")[:, :], 150.0, W, A.is_le, A.mult))
+            pe([k("hf"), "idb"], [k("rs")], [(rp[:, 384:512], T.idb[:, :], b("hf")[:, 128 * e:128 * e + 128], e == 0, e == 2, 128) for e in range(3)], k("rp"))
+            v([k("rs")], [k("ev")], 128, ts(b("ev")[:, :], rp[:, 384:512], 3 * W, W, A.is_equal, A.mult), k("rp"))
+            mm = [(mp[:, 192:200], b("ev")[:, :], T.cw[:, :], True, True, 64)]
+            if not last:
+                mm = [(mp[:, 128:192], T.c2k[:, :], T.wt[:, 256:320], True, False, 64)] + \
+                     [(mp[:, 128:192], b("hf")[:, 128 * e:128 * e + 128], T.wt[:, 64 * w:64 * w + 64], False, False, 64) for e, w in enumerate((0, 2, 1))] + \
+                     [(mp[:, 128:192], b("ev")[:, :], T.wt[:, 192:256], False, True, 64)] + mm
+            pe([k("hf"), k("ev"), "cw", "wt", "c2k"], [k("mc")], mm, k("mp"))
+            if not last:
+                v([k("mc"), "rst"], [k("mi")], 64, scan(b("mi")[:, :], T.rst[:, :], mp[:, 128:192], 0.0, A.add, A.min), k("mp"))
+            v([k("mc")], [k("cd")], 8, cp(b("cd")[:, :], mp[:, 192:200]), k("mp"))
+            if last:
+                pe([k("cd"), "bcm"], [k("mb")], [(mp[:, 256 + 8 * r:264 + 8 * r], T.bcm[:, 128 * r:128 * r + 128], b("cd")[:, :], True, True, 64) for r in range(16)], k("mp"))
+                v([k("mb"), "wq"], [k("ohb")], 128, ts(b("ohb")[:, :], mp[:, 256:384], T.pf[:, 9:10], 4096.0, A.is_equal, A.mult), k("mp"))
+                for e in range(3):
+                    v([k("ohb"), nfs[e], "l4"], [k("sel%d" % e)], 128 * GAM, tt(b("sel")[:, 128 * e:128 * e + 128], b("nf")[:, 128 * e:128 * e + 128].indirect(T.l4[:, 0:8]), b("ohb")[:, :], A.min))
+            else:
+                v([k("mi"), k("cand"), "l2"], [k("pm")], 32 * nq * GAM, tt(b("pm")[:, 0:32 * nq], b("mi")[:, :].indirect(T.l2[:, 0:2 * nq]), b("cand")[:, 0:32 * nq], A.min))
+                v([k("pm"), "rs4"], [k("pn")], 32 * nq, scan(b("pn")[:, 0:32 * nq], T.rs4[:, 0:32 * nq], b("pm")[:, 0:32 * nq], 0.0, A.add, A.max))
+                v([k("pn")], ["nx%d%d" % (c, t)], 8 * nq, cp(b("nx")[:, t, 0:8 * nq], b("pn")[:, 3:32 * nq:4]))
+                an = "a%d%d" % (t + 1, c)
+                op("g", ["nx%d%d" % (c, t)], ["g%d%d" % (c, t + 1)], 500,
+                   (lambda o, i, a: lambda: g.remote_dma(o, i, T.sem[a], T.sem.sent, dst[1], dst[0], dst[2]))(G[:, t + 1, 24:24 + 8 * nq], b("nx")[:, t, 0:8 * nq], an),
+                   None, an, RLAT)
+                crit[0] = 0
+                pe([k("cd"), "bcm"], [k("mb")], [(mp[:, 256 + r:384:16], T.bcm[:, 128 * r:128 * r + 128], b("cd")[:, :], True, True, 64) for r in range(16)], k("mp"))
+                v([k("mb"), "wq"], [k("ohb")], 128, ts(b("ohb")[:, :], mp[:, 256:384], T.pf[:, 9:10], 4096.0, A.is_equal, A.mult), k("mp"))
+                s([k("ohb")], [k("ohf")], 128, act(b("ohf")[:, :], b("ohb")[:, :], F.Copy, scale=0.5))
+                mm = []
+                for kk in range(2):
+                    o = rp[:, 128 * kk:128 * kk + 128]
+                    mm += [(o, T.t1[0:32, 128 * kk:128 * kk + 128], b("xt")[0:32, :], True, False, 128), (o, b("bh")[:, :], T.rg[:, :], False, False, 128),
+                           (o, T.idb[:, :], T.mk[:, 128 * kk:128 * kk + 128], False, False, 128), (o, b("ohb")[:, :], T.rg[:, :], False, True, 128)]
+                pe([k("xt"), k("bh"), k("ohb"), "t1.0", "t1.1", "rg", "mk", "idb"], [k("rd0"), k("rd1")], mm, k("rp"))
+                v([k("rd0"), k("rd1")], [k("fl")], 256, ts(b("fl")[:, :], rp[:, 0:256], 0.0, None, A.is_equal), k("rp"))
+                pe([k("fl"), cf, "idf", "h4"], [k("my")], [(mp[:, 200:208], T.idf[:, :], G[:, t, 16:24], True, False, 256)] +
+                   [(mp[:, 200 + 4 * kk:204 + 4 * kk], b("fl")[:, 128 * kk:128 * kk + 128], T.h4[:, 0:4], False, kk == 1, 64) for kk in range(2)], k("mp"))
+                v([k("my"), "dum"], [k("so")], 8, tt(b("so")[:, :], mp[:, 200:208], T.dum[:, 0:8], A.min), k("mp"))
+                v([k("so")], [k("su")], 8, ts(b("su")[:, :], b("so")[:, :], -M, None, A.add))
+                v([k("su"), nfs[2], k("ohf"), k("tad")], [k("tab")], 128 * 3.8, tt(b("tab")[:, :].indirect(b("su")[:, :]), b("nf")[:, 256:384], b("ohf")[:, :], A.max))
+                pe([k("ohb"), "idb"], [k("rd0"), k("rd1"), k("rd2")], [(rp[:, 128 * e:128 * e + 128], T.idb[:, :], b("ohb")[:, :], True, True, 128) for e in range(3)], k("rp"))
+                v([k("rd0"), k("rd1"), k("rd2")] + nfs, [k("sel0"), k("sel1"), k("sel2")], 384, tt(b("sel")[:, :], b("nf")[:, :], rp[:, 0:384], A.min), k("rp"))
+                stage[0] = 2 * t + c + LATE
+            pe([k("sel0"), k("sel1"), k("sel2"), k("ohb"), "eo", "eo3.0", "eo3.1", "eo3.2"], [k("mo")], [(mp[0:24, 384:512], T.eo3[:, :], b("ohb")[:, :], True, False, 128)] +
+               [(mp[0:24, 384:512], T.eo[:, 2 - m:26 - m], b("sel")[:, 128 * e:128 * e + 128], False, e == 2, 128) for e, m in enumerate((1, 2, 0))], k("mp"))
+            if last: s([k("mo")], ["yb3.%d" % c], 128, act(T.yb[0:24, t, c:256:2], mp[0:24, 384:512], F.Copy, bias=-1.0), k("mp"))
+            else: s([k("mo")], [k("ot")], 128, act(T.ot[0:24, 128 * c:128 * c + 128], mp[0:24, 384:512], F.Copy), k("mp"))
+        if not last: s(["ot0", "ot1", "l3"], ["yb%d" % t], 256 * GAM, act(T.yb[:, t, :], T.ot[:, :].indirect(T.l3[:, :]), F.Copy, bias=-1.0))
+        dma("y", ["yb3.0", "yb3.1"] if last else ["yb%d" % t], ["yn%d" % t], T.yn[:, 768 * t:768 * t + 768], T.yb[0:24, t, :], "y%d" % t, 2000)
+    return ops
+
+
+DEFER, SLC, RLAT = 1, 100.0, 3000
+SPLIT = [(0, 2), (2, 3)]
+CUT = [0, 4, 8, 12, 16]
+
+
+def order(ops):
+    n = len(ops); lw, rds, lb = {}, {}, {}
+    for i, o in enumerate(ops):
+        d = set()
+        for r in o["r"]:
+            d.add(lw[r])
+        for w in o["w"]:
+            if w in lw: d.add(lw[w])
+            d.update(rds.get(w, []))
+        if o["b"] is not None:
+            run = lb.get(o["b"], [])
+            if run and ops[run[-1]]["e"] == o["e"]:
+                o["bd"] = ops[run[-1]]["bd"]; run.append(i)
+            else:
+                o["bd"] = set(run); lb[o["b"]] = [i]
+            d |= o["bd"]
+        d.discard(i); o["d"] = d
+        for r in o["r"]: rds.setdefault(r, []).append(i)
+        for w in o["w"]: lw[w] = i; rds[w] = []
+    succ = [[] for _ in ops]
+    for i, o in enumerate(ops):
+        for j in o["d"]: succ[j].append(i)
+    pri = [0.0] * n
+    for i in range(n - 1, -1, -1):
+        ops[i]["k"] = min([ops[i]["k"]] + [ops[j]["k"] for j in succ[i]])
+        pri[i] = (((i + 1) * SEED * 2654435761) % 4096) / 4096.0 * NOISE + ops[i]["ns"] + ops[i]["lat"] + max([pri[j] + HOP for j in succ[i]] + [0.0])
+    free = {e: 0.0 for e in "vspgy"}; fin = [None] * n; left = [len(o["d"]) for o in ops]
+    ready = [i for i in range(n) if left[i] == 0]; at = [0.0] * n; seq = []
+    while ready:
+        st = {i: max(at[i], free[ops[i]["e"]]) for i in ready}
+        t0 = min(st.values()); e = ops[min(ready, key=lambda i: (st[i], -pri[i]))]["e"]
+        best = max([i for i in ready if ops[i]["e"] == e and st[i] <= t0 + (SLC if ops[i]["c"] else SLACK)], key=lambda i: (-ops[i]["k"], pri[i]))
+        ready.remove(best); seq.append(best)
+        free[e] = st[best] + ops[best]["ns"]; fin[best] = free[e] + ops[best]["lat"]; ops[best]["t"] = st[best]
+        for j in succ[best]:
+            at[j] = max(at[j], fin[best] + (0.0 if e == "p" and ops[j]["e"] == "p" else HOP)); left[j] -= 1
+            if left[j] == 0: ready.append(j)
+    return seq, succ, max(fin)
+
+
+CASES = [(1.56, 0.42, 150.0, 1.1), (1.2, 0.52, 250.0, 1.25), (2.0, 0.52, 200.0, 1.0)]
+STEPS = 40000
+KEPT = {}
+
+
+def polish(ops, seq, succ, steps):
+    n = len(ops); eng = ["vspgy".index(o["e"]) for o in ops]; lat = [o["lat"] for o in ops]
+    dep = [[(j, not (o["e"] == "p" and ops[j]["e"] == "p")) for j in o["d"]] for o in ops]
+    cost = [[o["fx"] + o["n"] * (pc if o["e"] == "p" else CYC * gm / GAM if o["ga"] else CYC * f) for o in ops] for gm, pc, hop, f in CASES]
+
+    def span(sq):
+        tot = 0.0
+        for ns, (gm, pc, hop, f) in zip(cost, CASES):
+            free = [0.0] * 5; fin = [0.0] * n
+            for i in sq:
+                st = free[eng[i]]
+                for j, h in dep[i]:
+                    x = fin[j] + hop if h else fin[j]
+                    if x > st: st = x
+                st += ns[i]; free[eng[i]] = st; fin[i] = st + lat[i]
+            tot += max(fin) + 0.02 * sum(fin) / n
+        return tot / len(CASES)
+    best = span(seq); r = 12345
+    for it in range(steps):
+        r = (r * 1103515245 + 12345) % 2147483648; a = (r >> 8) % n; i = seq[a]
+        if eng[i] > 2: continue
+        r = (r * 1103515245 + 12345) % 2147483648; hops = 1 + (r >> 8) % 3; up = (r >> 20) & 1
+        near = set(ops[i]["d"]) if up else set(succ[i]); p = a; to = None
+        while hops and 0 < p < n - 1:
+            p += -1 if up else 1
+            if seq[p] in near: break
+            if eng[seq[p]] == eng[i]: to = p; hops -= 1
+        if to is None: continue
+        sq = seq[:a] + seq[a + 1:]; sq.insert(to, i); x = span(sq)
+        if x <= best + 60.0 * (1.0 - it / steps): best, seq = x, sq
+    return seq, best
+
+
+def rank_program(g, core, T, topo):
+    rank = T.rank_of(core)
+    if rank is None:
+        return
+    nxt = T.cores[(rank + 1) % len(T.cores)]
+    rid, pid = topo.addr(nxt, core)
+    ops = build(g, T, (rid, pid, topo.mask(core, nxt)))
+    nen = len(topo.engines(core, nxt))
+    seq, succ, _ = order(ops)
+    if "seq" not in KEPT: KEPT["seq"] = polish(ops, seq, succ, STEPS)[0]
+    seq = KEPT["seq"]
+    for a, i in enumerate(seq): ops[i]["t"] = a
+    Q = {"v": g.vector, "s": g.scalar, "p": g.tensor, "g": g, "y": g.sync}
+    total = {}
+    for o in ops:
+        if o["sem"]: total[o["sem"]] = total.get(o["sem"], 0) + (nen if o["e"] == "g" else 16)
+    count = {e: 0 for e in "vspg"}; known = {e: {} for e in Q}; mark = {}; clock = {}
+    for i in seq:
+        o = ops[i]; e = o["e"]; kn = known[e]; need = {}
+        deps = [j for j in o["d"] if not (e == "p" and ops[j]["e"] == "p")]
+        for j in deps:
+            sm, val = mark[j]
+            need[sm] = max(need.get(sm, 0), val)
+        for j in sorted(deps, key=lambda j: -ops[j]["t"]):
+            sm, val = mark[j]
+            if val == need[sm] and kn.get(sm, 0) < val:
+                Q[e].wait_ge(T.sem[sm], val); kn[sm] = val
+                for a, x in clock[j].items(): kn[a] = max(kn.get(a, 0), x)
+        ins = o["fn"]()
+        if o["sem"]:
+            mark[i] = (o["sem"], total[o["sem"]]); clock[i] = {}
+            if e != "g": ins.then_inc(T.sem[o["sem"]], 16)
+        elif [j for j in succ[i] if not (e == "p" and ops[j]["e"] == "p")]:
+            count[e] += 1; ins.then_inc(T.sem[e], 1); mark[i] = (e, count[e]); clock[i] = dict(kn)
+    for e in "vspg":
+        g.wait_ge(T.sem[e], count[e])
+    g.wait_ge(T.sem.sent, nen * 6)
+    for t in range(RO):
+        g.wait_ge(T.sem["y%d" % t], 16)

@@ -1,44 +1,55 @@
 from concourse.mybir import AluOpType, ActivationFunctionType, AxisListType
 
 A, F = AluOpType, ActivationFunctionType
-RO, NB = 4, 4
+RO = 4
 M = 12582912.0
-W = 32768.0
-NQ = [21, 15, 10, 6]
-PAIRS = [(2, 3), (1, 3), (1, 2), (0, 2), (0, 3), (0, 1)] + [(j, 4) for j in range(4)] + [(j, 5) for j in range(5)] + [(j, 6) for j in range(6)]
-BC, AC, AB, OB, OC, OA, ON, AN, BN, CN = range(10)
+SC = 218.0 / 128
+PAIRS = [(0, 2), (0, 3), (0, 1), (1, 2), (2, 3), (1, 3)] + [(j, 4) for j in range(4)] + [(j, 5) for j in range(5)] + [(j, 6) for j in range(6)]
+OB, OC, OA, ONE, AB, BC, AC = range(7)
+NEXT = [[1, 2, 3, 4, 5, 6], [0, 4, 2, 3, 5, 6], [0, 1, 4, 3, 5, 6], [0, 1, 2, 4, 5, 6]]
+PRIO = [-1, 2 + 64, 1 + 64, 0]
 
 
-def upd(b):
-    return [[b + 1, b, b, b], [b + 2, b + 4, b + 1, b + 1], [b + 3, b + 2, b + 4, b + 2], [b + 4, b + 3, b + 3, b + 4]]
+def slot(l): return l if l < ONE else l + 1
 
 
-PI = [[CN, BC, CN, BN], [BN, CN, AC, AN], [BC, BN, AN, AB], [AC, OB, ON, OB], [AN, OC, OC, ON], [AB, ON, OA, OA]] + upd(10) + upd(15) + [[20] * 4]
-MIX = [[[0, 1, 0, 0], [0, 1, 0, 0]], [[0, 1, 0, 0], [0, 0, 1, 0]], [[0, 1, 0, 1], [1, 0, 0, 0]], [[0, 0, 1, 1], [1, 1, 1, 0]]]
-SLACK, EARLY, LATE, SEED, NOISE = 0.0, 1.1, 1.6, 0, 0.0
+SRC = [[None] * 16 for _ in NEXT]
+for _x, _nx in enumerate(NEXT):
+    SRC[_x][ONE] = ONE
+    for _l, (_j, _k) in enumerate(PAIRS[:15]):
+        SRC[_x][slot(_l)] = slot(PAIRS.index(tuple(sorted((_nx[_j], _nx[_k])))))
+CUT = [0, 4, 8, 12, 16]
+MIX = [[[2, 0, 2, 0], [1, 2, 0, 0]], [[1, 0, 0, 0], [1, 0, 0, 0]], [[1, 0, 0, 1], [1, 0, 0, 0]], [[1, 2, 2, 1], [1, 1, 0, 0]]]
+SLACK, EARLY, LATE = 0.0, 1.1, 1.6
 CYC, GAM, PEC, HOP = 0.83, 1.56, 0.42, 200.0
+SLC, RLAT, TWO = 100.0, 3000, 1
+SPLIT = [(0, 1), (1, 4)]
 
 S_, P_, B_, F_, H_, U_, I_ = "sbuf", "psum", "bfloat16", "float32", "float16", "uint16", "int32"
 SCRATCH = {}
 for _n, _w, _d in [
-        ("ob", 1792, B_), ("cv", 2064, B_), ("ones", 2048, B_), ("idb", 128, B_), ("id4", 128, B_), ("idf", 128, F_),
-        ("d8a", 8, B_), ("d8", 8, B_), ("d8f", 8, F_), ("e2", 144, B_), ("eo", 32, H_), ("eo3", 24, B_), ("off0", 24, F_), ("off", 24, F_), ("pint", 16, I_), ("pf", 24, F_), ("rs4", 480, F_),
-        ("ee0", 384, B_), ("ee", 384, B_), ("cst", 384, B_), ("t1", 256, B_), ("binw", 912, B_), ("wt0", 320, B_), ("wt1", 320, B_), ("wt", 320, B_),
-        ("c2k", 128, B_), ("geo", 64, F_), ("cw", 8, B_), ("bcm", 2048, B_), ("rg0", 128, B_), ("rg1", 128, B_), ("rg", 128, B_),
-        ("mk0", 256, F_), ("mk1", 256, F_), ("mk2", 256, F_), ("mk", 256, B_), ("h4", 8, B_), ("dum", 16, F_), ("rst", 64, F_),
-        ("lv", 96, I_), ("lf", 128, F_), ("lg", 24, F_), ("l1", 32, U_), ("l2", 32, U_), ("l3", 16, U_), ("l4", 24, U_), ("ot", 256, F_)]:
+        ("cv", 2064, B_), ("ones", 512, B_), ("zr", 512, B_), ("idb", 128, B_), ("id4", 128, B_), ("ids", 128, H_),
+        ("d8a", 8, B_), ("d8", 8, B_), ("d8s", 8, B_), ("d8f", 8, F_), ("eo", 32, H_), ("eo3", 24, B_), ("pint", 16, I_), ("pf", 24, F_), ("rst", 512, B_),
+        ("eh", 384, H_), ("cst", 384, B_), ("t1", 256, H_), ("binw", 912, B_), ("kw0", 128, B_), ("kw", 512, B_),
+        ("csf", 24, F_), ("cs", 24, H_), ("geo", 64, F_), ("cw", 8, B_), ("bcm", 2048, B_), ("rg0", 128, B_), ("rg", 128, B_), ("rg2", 128, B_),
+        ("mk0", 256, B_), ("mk1", 256, B_), ("mk2", 256, B_), ("mk", 256, B_), ("h4", 8, B_), ("dum", 16, F_),
+        ("lv", 8, I_), ("lf", 32, F_), ("lg", 24, F_), ("l4", 24, U_)]:
     SCRATCH[_n] = (S_, [128, _w], _d)
-SCRATCH["gp"] = (S_, [128, 21, 256], B_)
+SCRATCH["ob"] = (S_, [128, 7, 16, 16], B_)
+SCRATCH["gp"] = (S_, [128, 16, 352], B_)
 SCRATCH["yb"] = (S_, [128, 4, 256], F_)
+SCRATCH["ph"] = (S_, [128, 8, 128], H_)
 for _c in "01":
     for _n, _w, _d in [
-            ("raw", [904], I_), ("tab", [1032], F_), ("gm", [4, 192], F_), ("nx", [3, 120], F_), ("cl", [24], U_), ("nf", [384], F_), ("nu", [384], U_),
-            ("xh", [56], B_), ("xt", [128], B_), ("bh", [128], B_), ("cand", [480], F_), ("va", [2048], B_), ("vb", [2048], B_), ("vc", [2048], B_),
-            ("pr", [2048], B_), ("pw", [2048], F_), ("yy", [128], F_), ("yz", [128], F_), ("ab", [384], B_), ("hf", [384], B_), ("ev", [128], B_), ("mi", [64], F_), ("cd", [8], B_),
-            ("pm", [480], F_), ("pn", [480], F_), ("ohb", [128], B_), ("ohf", [128], F_), ("sel", [384], H_), ("fl", [256], B_), ("so", [8], F_), ("su", [8], U_)]:
+            ("raw", [904], I_), ("tab", [1032], F_), ("gm", [4, 128], H_), ("gb", [128], H_), ("nx", [3, 128], H_), ("cl", [24], U_), ("nf", [384], F_), ("nu", [384], U_),
+            ("bh", [128], B_), ("vv", [6144], B_),
+            ("pr", [2048], B_), ("pw", [2048], F_), ("yy", [128], F_), ("ab", [128], B_), ("hf", [512], B_), ("lo", [128], H_), ("cd", [8], B_), ("xs", [512], F_),
+            ("ohb", [128], B_), ("ohf", [128], F_), ("sel", [384], H_), ("fl", [256], B_), ("so", [8], F_), ("su", [8], U_)]:
         SCRATCH[_n + _c] = (S_, [128] + _w, _d)
-for _n in ["rp0", "rp1", "mp0", "mp1", "up0", "up1", "up2", "up3"]:
+for _n in ["rp0", "rp1", "mp0", "mp1"]:
     SCRATCH[_n] = (P_, [128, 512], F_)
+for _n in ["up0", "up1"]:
+    SCRATCH[_n] = (P_, [128, 1024], F_)
 SEMAPHORES = ["v", "s", "p", "g", "sent", "o0", "o1", "cv", "t0", "t1", "y0", "y1", "y2", "y3"] + ["a%d%d" % (t, c) for t in range(1, 4) for c in range(2)]
 
 
@@ -46,13 +57,15 @@ def build(g, T, dst):
     ops = []; stage = [99.0]; crit = [0]
     V, S, P = g.vector, g.scalar, g.tensor
 
-    def op(eng, rd, wr, ns, fn, bank=None, sem=None, lat=0.0):
+    def op(eng, rd, wr, ns, fn, bank=None, sem=None, lat=0.0, ga=False):
         fx = {"v": 50.0, "s": 65.0, "p": 60.0}.get(eng, ns)
-        ops.append({"fx": fx, "n": (ns - fx) / (PEC if eng == "p" else CYC), "ga": any(wr[0].startswith(x) for x in ("va", "vb", "vc", "nf", "nu", "bh", "cand", "pm", "yb", "sel")) and bank is None,
+        ops.append({"fx": fx, "n": (ns - fx) / (PEC if eng == "p" else CYC), "ga": ga,
                     "e": eng, "r": rd, "w": wr, "ns": ns, "fn": fn, "b": bank, "sem": sem, "lat": lat, "k": stage[0], "c": crit[0]})
 
-    def v(rd, wr, n, fn, bank=None): op("v", rd, wr, 50 + max(n, 16) * CYC, fn, bank)
-    def s(rd, wr, n, fn, bank=None): op("s", rd, wr, 65 + max(n, 16) * CYC, fn, bank)
+    def v(rd, wr, n, fn, bank=None): op("v", rd, wr, 50 + max(n, 32) * CYC, fn, bank)
+    def s(rd, wr, n, fn, bank=None): op("s", rd, wr, 65 + max(n, 32) * CYC, fn, bank)
+    def vg(rd, wr, n, fn): op("v", rd, wr, 50 + n * GAM * CYC, fn, ga=True)
+    def sg(rd, wr, n, fn): op("s", rd, wr, 65 + n * GAM * CYC, fn, ga=True)
     def gp(rd, wr, n, fn): op("g", rd, wr, 170 + 2 * n * CYC, fn)
 
     def pe(rd, wr, mms, bank):
@@ -72,61 +85,70 @@ def build(g, T, dst):
     def io(o, pat, b, cm): return lambda: g.iota(o, pat, b, cm, allow_small_or_imprecise_dtypes=True)
     def ioi(o, pat, b, cm): return lambda: g.iota(o, pat, b, cm)
     def sl(o, i, pat, f, b, cm): return lambda: g.affine_select(o, i, pat, f, 0.0, b, cm)
+    def put(o, x, pat, b): return lambda: g.affine_select(o, o, pat, A.not_equal, x, b, 1)
     def dma(q, rd, wr, o, i, sem, lat): op(q, rd, wr, 60, lambda: (g.sync if q == "y" else S).dma_start(o, i), None, sem, lat)
 
-    dma("y", [], ["ob0"], T.ob[:, 0:1024], T.obs[:, 0:1024], "o0", 2500)
+    dma("y", [], ["ob0"], T.ob[:, 0:4, :, :], T.obs[:, 0:1024], "o0", 2500)
     for c in range(2):
         for h in range(4):
             dma("s" if c == 0 else "y", [], ["raw%d.%d" % (c, h)], T["raw%d" % c][:, 226 * h:226 * h + 226],
                 T.tsee[:, 226 * (2 * h + c):226 * (2 * h + c) + 226], "t%d" % c, 4000 + 3000 * c)
         if c == 0:
-            dma("y", [], ["cv"], T.cv[:, 0:2048], T.cvec[:, :], "cv", 5000)
-            dma("y", [], ["ob1"], T.ob[:, 1024:1792], T.obs[:, 1024:1792], "o1", 5500)
+            dma("y", [], ["ob1"], T.ob[:, 4:7, :, :], T.obs[:, 1024:1792], "o1", 3500)
+            dma("y", [], ["cv"], T.cv[:, 0:2048], T.cvec[:, :], "cv", 5500)
 
-    v([], ["on1"], 192, ms(T.ones[:, 0:384], 1.0))
+    def zero(o, n): return ts(o, T.ones[:, 0:n], 0.0, None, A.mult)
+    v([], ["on1"], 64, ms(T.ones[:, 0:128], 1.0))
+    v([], ["on2"], 192, ms(T.ones[:, 128:512], 1.0))
     gp(["on1"], ["idb"], 128, sl(T.idb[:, :], T.ones[:, 0:128], [[-1, 128]], A.is_equal, 0, 1))
     gp(["on1"], ["d8a"], 8, sl(T.d8a[:, :], T.ones[:, 0:8], [[-16, 8]], A.is_ge, 0, 1))
     gp(["d8a"], ["d8"], 8, sl(T.d8[:, :], T.d8a[:, :], [[16, 8]], A.is_ge, 15, -1))
-    v([], ["e2"], 72, ms(T.e2[:, :], 0.0))
-    v(["d8"], ["e2"], 8, cp(T.e2[:, 15:143:16], T.d8[:, :]))
-    gp([], ["off0"], 24, io(T.off0[:, :], [[0, 6], [226, 4]], 0, 0))
-    v(["off0"], ["off"], 24, ts(T.off[:, :], T.off0[:, :], M, None, A.add))
     v([], ["cvz"], 8, ms(T.cv[:, 2048:2064], 0.0))
-    s(["idb"], ["idf"], 128, act(T.idf[:, :], T.idb[:, :], F.Copy))
+    v([], ["gp%d" % ONE], 128, ms(T.gp[:, :, 16 * ONE:16 * ONE + 16], 113.0))
+    v(["idb"], ["ids"], 64, ts(T.ids[:, :], T.idb[:, :], SC, None, A.mult))
     s(["idb"], ["id4"], 128, act(T.id4[:, :], T.idb[:, :], F.Copy, scale=4096.0))
     s(["d8"], ["d8f"], 8, act(T.d8f[:, :], T.d8[:, :], F.Copy))
-    v([], ["ee0"], 192, ms(T.ee0[:, :], -16.0))
-    v([], ["ee0"], 64, ms(T.ee0[:, 128:256], -65536.0))
-    gp(["ee0"], ["ee0"], 384, sl(T.ee0[:, :], T.ee0[:, :], [[-2, 24], [0, 16]], A.is_ge, -8, 1))
-    gp(["ee0"], ["ee", "eeb"], 384, sl(T.ee[:, :], T.ee0[:, :], [[2, 24], [0, 16]], A.is_ge, 9, -1))
-    v([], ["cst"], 192, ms(T.cst[0:64, :], 0.0))
-    for r0, c0, x in ((0, 0, -7.5), (0, 128, -30720.0), (32, 128, -1800.0), (0, 256, -7.5), (32, 256, 1800.0)):
+    s(["d8"], ["d8s"], 8, act(T.d8s[:, :], T.d8[:, :], F.Copy, scale=SC))
+    gp([], ["csf"], 24, io(T.csf[:, :], [[0, 6], [7232, 4]], 0, 0))
+    gp(["csf"], ["csf"], 24, sl(T.csf[:, :], T.csf[:, :], [[0, 24]], A.is_equal, -8 * ONE, 1))
+    gp(["csf"], ["csf"], 24, put(T.csf[:, :], 3584.0, [[0, 24]], -8 * ONE - 1))
+    gp(["csf"], ["csf"], 24, put(T.csf[:, :], 1.0, [[0, 24]], -8 * ONE - 2))
+    gp(["csf"], ["csf"], 24, put(T.csf[:, :], 16.0, [[-1, 24]], 0))
+    v(["csf"], ["cs"], 24, ts(T.cs[:, :], T.csf[:, :], 1.0 / 256, None, A.mult))
+    v(["on1", "on2"], ["eb"], 192, zero(T.eh[:, :], 384))
+    for e, (q, x) in enumerate(((AC, -4096.0), (AB, -SC), (BC, -SC))):
+        gp(["eb"], ["eh%d" % e], 128, put(T.eh[:, 128 * e:128 * e + 128], x, [[-1, 8], [0, 16]], -8 * q))
+    v([], ["cst"], 128, ms(T.cst[0:64, :], 0.0))
+    for r0, c0, x in ((0, 0, -1800.0 * 4096), (32, 0, -1800.0), (0, 128, -3072.0), (32, 128, 3072.0 - 1800 * SC)):
         v([], ["cst"], 64, ms(T.cst[r0:r0 + 1, c0:c0 + 128], x))
     gp([], ["lv0"], 1, ioi(T.lv[:, 0:1], [[0, 1]], 0, 1))
-    for k, (sh, an) in enumerate([(3, 1), (0, 15), (0, 7), (6, 1), (0, 1), (1, 7), (4, 3)]):
+    for k, (sh, an) in enumerate([(3, 1), (0, 15), (0, 7), (6, 1), (4, 3)]):
         v(["lv0"], ["pi%d" % k], 1, ts(T.pint[:, k:k + 1], T.lv[:, 0:1], sh, an, A.logical_shift_right, A.bitwise_and))
-    v(["pi%d" % k for k in range(3)], ["pf"], 8, cp(T.pf[:, 0:3], T.pint[:, 0:3]))
-    v(["pi%d" % k for k in range(3, 7)], ["pg"], 8, cp(T.pf[:, 3:7], T.pint[:, 3:7]))
-    HI, P16, P8, KK, P2, PH, K4 = [T.pf[:, k:k + 1] for k in range(7)]
-    gp([], ["lg"], 24, io(T.lg[:, :], [[128, 3], [2, 8]], 0, 0))
+    v(["pi%d" % k for k in range(5)], ["pf"], 8, cp(T.pf[:, 0:5], T.pint[:, 0:5]))
+    HI, P16, P8, KK, K4 = [T.pf[:, k:k + 1] for k in range(5)]
+    for r0, r1 in zip(CUT, CUT[1:]):
+        gp([], ["lg%d" % r0], 3 * (r1 - r0) // 2, io(T.lg[:, 3 * r0 // 2:3 * r1 // 2], [[128, 3], [2, (r1 - r0) // 2]], r0, 0))
     v(["pf"], ["pq4"], 1, ts(T.pf[:, 13:14], P8, 16.0, HI, A.mult, A.add))
-    v(["lg", "pq4"], ["l4"], 24, ts(T.l4[:, :], T.lg[:, :], T.pf[:, 13:14], None, A.add))
-    WT = [[(0, 0), (2, 2), (-2, 0), (-2, 0)], [(0, 0), (-2, 0), (2, 2), (0, -2)], [(0, 0), (0, -2), (0, -2), (2, 2)],
-          [(64, 64), (-64, -64), (-64, -64), (-64, -64)], [(-1, -1), (1, 1), (-1, 1), (-1, -1)]]
+    v(["lg%d" % r0 for r0 in CUT[:-1]] + ["pq4"], ["l4"], 24, ts(T.l4[:, :], T.lg[:, :], T.pf[:, 13:14], None, A.add))
+    for x in (0, 4): v(["on1", "on2"], ["pb%d" % x], 256, zero(T.ph[:, x:x + 4, :], 512))
+    for x in range(4): v([], ["pw%d" % x], 64, ms(T.zr[0:1, x:512:4], 4096.0 * PRIO[x]))
     names = []
-    for e in range(5):
-        k = 0
-        while k < 4:
-            n = 1
-            while k + n < 4 and WT[e][k + n] == WT[e][k]: n += 1
-            x, y = WT[e][k]
-            gp([], ["wt0.%d.%d" % (e, k)], 16 * n, io(T.wt0[:, 64 * e + 16 * k:64 * e + 16 * (k + n)], [[0, 8 * n], [y - x, 2]], x, 0))
-            names.append("wt0.%d.%d" % (e, k)); k += n
-    gp(names, ["wt1"], 320, sl(T.wt1[:, :], T.wt0[:, :], [[0, 20], [-16, 8], [0, 2]], A.is_ge, 0, 1))
-    gp(["wt1"], ["wt"], 320, sl(T.wt[:, :], T.wt1[:, :], [[0, 20], [16, 8], [0, 2]], A.is_ge, 15, -1))
-    gp([], ["c2k"], 128, io(T.c2k[:, :], [[0, 128]], int(W) // 16, 0))
-    gp([], ["rst"], 64, io(T.rst[:, :], [[0, 32], [-32767, 2]], 32767, 0))
-    s(["rst"], ["rst"], 64, act(T.rst[:, :], T.rst[:, :], F.Copy, scale=2.0 ** 20))
+    for x in (0, 2):
+        q = 0
+        while q < 16:
+            a, b = SRC[x][q], SRC[x + 1][q]; n = 1
+            while q + n < 16 and (SRC[x][q + n], SRC[x + 1][q + n]) == (a + n, b + n) and a + n != 16 and b + n != 16: n += 1
+            u = 4 * (a // 16) + x; names.append("pb%d.%d" % (x, q))
+            gp(["pb%d" % (u & 4)], [names[-1]], 16 * n, put(T.ph[:, u:u + 2, 8 * q:8 * (q + n)], 1.0, [[8 * (a - b), 2], [-1, 8 * n]], -8 * (a % 16)))
+            q += n
+    v([], ["kw0"], 64, ms(T.kw0[:, :], 16384.0))
+    gp(["kw0"], ["kw0"], 128, sl(T.kw0[:, :], T.kw0[:, :], [[0, 16], [-16, 8]], A.is_ge, 0, 1))
+    gp(["kw0"], ["kw"], 128, sl(T.kw[:, 0:128], T.kw0[:, :], [[0, 16], [16, 8]], A.is_ge, 15, -1))
+    s(["kw"], ["kn"], 128, act(T.kw[:, 128:256], T.kw[:, 0:128], F.Copy, scale=-1.0))
+    s(["kw"], ["kf"], 128, act(T.kw[:, 256:384], T.kw[:, 0:128], F.Copy, scale=32.0))
+    s(["idb"], ["id8"], 128, act(T.kw[:, 384:512], T.idb[:, :], F.Copy, scale=8192.0))
+    v([], ["rst"], 256, ms(T.rst[:, :], 0.0))
+    v([], ["rst"], 64, ms(T.rst[:, 0:512:4], -2.0 ** 40))
     v([], ["ge0"], 16, ms(T.geo[:, 0:16], 2.0 ** -9))
     v([], ["ge1"], 16, ms(T.geo[:, 16:32], 0.0))
     v(["ge0", "ge1"], ["ge2"], 16, scan(T.geo[:, 32:48], T.geo[:, 0:16], T.geo[:, 16:32], 2.0 ** 57, A.mult, A.add))
@@ -135,192 +157,170 @@ def build(g, T, dst):
     v(["lf1", "ge2"], ["ge3"], 32, tt(T.geo[:, 48:64], T.lf[:, 16:32], T.geo[:, 32:48], A.mult))
     v(["ge3"], ["wp"], 16, lambda: V.tensor_reduce(T.pf[:, 8:9], T.geo[:, 48:64], AxisListType.X, A.add))
     v(["wp", "d8"], ["cw"], 8, ts(T.cw[:, :], T.d8[:, :], T.pf[:, 8:9], None, A.mult))
-    v(["wp"], ["wq"], 1, ts(T.pf[:, 9:10], T.pf[:, 8:9], W, None, A.mult))
-    for q in range(15):
-        gp([], ["lv1.%d" % q], 2, io(T.lf[:, 32 + 2 * q:34 + 2 * q], [[0, 2]], 2 * sum(PI[q][x] * 32 ** x for x in range(4)) + 1, 0))
-    for k, (sh, an) in enumerate([(0, 3), (2, 3), (1, 1)]):
-        v(["lv0"], ["pj%d" % k], 1, ts(T.pint[:, 8 + k:9 + k], T.lv[:, 0:1], sh, an, A.logical_shift_right, A.bitwise_and))
-    v(["pj0", "pj1", "pj2"], ["ph"], 8, cp(T.pf[:, 16:19], T.pint[:, 8:11]))
-    v(["pg"], ["pq6"], 1, ts(T.pf[:, 19:20], P2, -31.0 / 64, 0.5, A.mult, A.add))
-    v(["ph"], ["pq7"], 1, ts(T.pf[:, 20:21], T.pf[:, 18:19], -1023.0 / 1024, 1.0, A.mult, A.add))
-    v(["pq6", "pq7"], ["pq8"], 1, tt(T.pf[:, 21:22], T.pf[:, 19:20], T.pf[:, 20:21], A.mult))
-    v(["pq8"] + ["lv1.%d" % q for q in range(15)], ["lf2"], 30, ts(T.lf[:, 64:94], T.lf[:, 32:62], T.pf[:, 21:22], -0.5, A.mult, A.add))
-    v(["lf2"], ["lf3"], 30, ts(T.lf[:, 96:126], T.lf[:, 64:94], M, None, A.add))
-    v(["lf3"], ["lv2"], 30, ts(T.lv[:, 32:62], T.lf[:, 96:126], -M, None, A.add))
-    v(["lv2"], ["lv3"], 30, ts(T.lv[:, 64:94], T.lv[:, 32:62], 31, None, A.bitwise_and))
-    v(["lv3", "ph"], ["lf2"], 30, ts(T.lf[:, 64:94], T.lv[:, 64:94], 8.0, T.pf[:, 17:18], A.mult, A.add))
-    gp([], ["mk2"], 30, io(T.mk2[:, 0:30], [[0, 15], [4, 2]], 0, 0))
-    v(["lf2", "mk2"], ["lf3"], 60, tt(T.lf[:, 96:126], T.lf[:, 64:94], T.mk2[:, 0:30], A.add))
-    v(["lf3"], ["l1"], 30, cp(T.l1[:, 0:30], T.lf[:, 96:126]))
-    v(["ph"], ["pq9"], 1, ts(T.pf[:, 15:16], T.pf[:, 16:17], 8.0, T.pf[:, 17:18], A.mult, A.add))
-    v(["pq9"], ["pq5"], 1, ts(T.pf[:, 14:15], T.pf[:, 15:16], 2.0, 1.0, A.mult, A.add))
-    v(["mk2", "pq5", "l1"], ["l2"], 30, ts(T.l2[:, 0:30], T.mk2[:, 0:30], 2.0, T.pf[:, 14:15], A.mult, A.add))
-    gp([], ["rs4"], 480, io(T.rs4[:, :], [[0, 120], [1, 4]], 0, 0))
-    v(["rs4"], ["rs4"], 480, ts(T.rs4[:, :], T.rs4[:, :], 0.0, -2.0 ** 40, A.is_equal, A.mult))
-    v(["pg"], ["pq0"], 1, ts(T.pf[:, 10:11], P2, 128.0, None, A.mult))
-    v(["pg", "pq0"], ["pq1"], 1, ts(T.pf[:, 11:12], PH, 16.0, T.pf[:, 10:11], A.mult, A.add))
-    v(["lf0", "pq1"], ["l3"], 16, ts(T.l3[:, :], T.lf[:, 0:16], T.pf[:, 11:12], None, A.add))
-    v([], ["on2"], 832, ms(T.ones[:, 384:2048], 1.0))
-    gp(["on1", "on2"], ["bcm"], 2048, sl(T.bcm[:, :], T.ones[:, :], [[-1, 16], [-16, 8], [0, 16]], A.is_equal, 0, 1))
-    v(["d8"], ["eo"], 8, ts(T.eo[:, :], T.ones[:, 0:32], 0.0, None, A.mult))
+    for u in range(4):
+        gp(["on1", "on2"], ["bcm%d" % u], 512, sl(T.bcm[:, 512 * u:512 * u + 512], T.ones[:, 0:512], [[-1, 4], [-16, 8], [0, 16]], A.is_equal, -4 * u, 1))
+    v(["on1"], ["eo"], 8, zero(T.eo[:, :], 32))
     v(["d8"], ["eo"], 8, cp(T.eo[:, 2:26:3], T.d8[:, :]))
     for m in range(3):
-        s(["d8"], ["eo3.%d" % m], 8, act(T.eo3[:, m:24:3], T.d8[:, :], F.Copy, scale=1.0 / 4096))
-    gp([], ["ot0", "ot1"], 256, io(T.ot[:, :], [[0, 256]], 0, 0))
+        s(["d8"], ["eo3.%d" % m], 8, act(T.eo3[:, m:24:3], T.d8[:, :], F.Copy, scale=1.0 / 2048))
     gp([], ["binw"], 904, io(T.binw[:, 0:904], [[0, 4], [1, 226]], 0, 0))
+    v(["on1", "on2"], ["t1"], 128, zero(T.t1[:, :], 256))
     for kk in range(2):
-        gp(["on1"], ["t1.%d" % kk], 128, sl(T.t1[:, 128 * kk:128 * kk + 128], T.ones[:, 0:128], [[0, 2], [-1, 4], [0, 16]], A.is_equal, -4 * kk, 1))
-    gp(["on1"], ["rg0"], 128, sl(T.rg0[:, :], T.ones[:, 0:128], [[-16, 8], [0, 16]], A.is_ge, 0, 1))
-    gp(["rg0"], ["rg1"], 128, sl(T.rg1[:, :], T.rg0[:, :], [[16, 8], [0, 16]], A.is_ge, 15, -1))
-    s(["rg1"], ["rg"], 128, act(T.rg[:, :], T.rg1[:, :], F.Copy, scale=-0.0625))
+        gp(["t1"], ["t1"], 128, put(T.t1[:, 128 * kk:128 * kk + 128], 1.0, [[0, 2], [-1, 4], [0, 16]], -8 * OA - 4 * kk))
+    gp(["t1"], ["t1"], 256, put(T.t1[:, :], 224.0, [[0, 256]], -8 * ONE))
+    gp(["t1"], ["t1"], 256, put(T.t1[:, :], 0.0625, [[0, 256]], -8 * ONE - 1))
+    v([], ["rg0"], 64, ms(T.rg0[:, :], -1.0))
+    gp(["rg0"], ["rg0"], 128, sl(T.rg0[:, :], T.rg0[:, :], [[-16, 8], [0, 16]], A.is_ge, 0, 1))
+    gp(["rg0"], ["rg"], 128, sl(T.rg[:, :], T.rg0[:, :], [[16, 8], [0, 16]], A.is_ge, 15, -1))
+    s(["rg"], ["rg2"], 128, act(T.rg2[:, :], T.rg[:, :], F.Copy, scale=2.0))
     gp([], ["mk0"], 256, io(T.mk0[:, :], [[-1, 2], [0, 8], [-2, 16]], 0, 0))
-    v(["pg", "pf"], ["pq2"], 1, ts(T.pf[:, 12:13], P16, 2.0, KK, A.mult, A.add))
-    v(["mk0", "pq2"], ["mk1"], 256, ts(T.mk1[:, :], T.mk0[:, :], T.pf[:, 12:13], 512.0, A.add, A.mult))
-    v(["mk1", "l2"], ["mk2"], 256, ts(T.mk2[:, :], T.mk1[:, :], -0.5, 256.0, A.mult, A.min))
-    v(["mk1", "mk2"], ["mk"], 512, tt(T.mk[:, :], T.mk1[:, :], T.mk2[:, :], A.max))
-    v(["lf0", "pg"], ["h4"], 4, ts(T.h4[:, 0:4], T.lf[:, 0:4], K4, 4096.0, A.is_equal, A.mult))
-    gp([], ["du0"], 8, io(T.dum[:, 8:16], [[16, 8]], int(M) + 904, 0))
+    v(["pf"], ["pq2"], 1, ts(T.pf[:, 12:13], P16, 2.0, KK, A.mult, A.add))
+    v(["mk0", "pq2"], ["mk1"], 128, ts(T.mk1[:, :], T.mk0[:, :], T.pf[:, 12:13], 8192.0, A.add, A.mult))
+    v(["mk1"], ["mk2"], 128, ts(T.mk2[:, :], T.mk1[:, :], -1.0, 4096.0, A.mult, A.min))
+    v(["mk1", "mk2"], ["mk"], 256, tt(T.mk[:, :], T.mk1[:, :], T.mk2[:, :], A.max))
+    v(["lf0", "pf"], ["h4"], 4, ts(T.h4[:, 0:4], T.lf[:, 0:4], K4, 4096.0, A.is_equal, A.mult))
+    gp([], ["du0"], 8, io(T.dum[:, 8:16], [[16, 8]], 904, 0))
     v(["du0", "pf"], ["dum"], 8, ts(T.dum[:, 0:8], T.dum[:, 8:16], P16, None, A.add))
 
-    def oc(j): return slice(256 * j, 256 * j + 256)
-    place = {1: (0, 0), 2: (0, 1), 3: (1, 0), 4: (2, 0), 5: (2, 1), 6: (3, 0)}
-    def pj(j): return T["up%d" % place[j][0]][:, oc(place[j][1])]
-    for u, js in ((0, [1, 2]), (1, [3]), (2, [4, 5]), (3, [6])):
-        pe(["idb", "ob0" if u < 2 else "ob1"], ["up%d" % u], [(T["up%d" % u][:, 0:256 * len(js)], T.idb[:, :], T.ob[:, 256 * js[0]:256 * (js[-1] + 1)], True, True, 256 * len(js))], "up%d" % u)
-
-    def gram(q0, q1):
-        for q in range(q0, q1):
-            j, k = PAIRS[q]; u = "up%d" % place[k][0]
-            v(["ob0" if j < 4 else "ob1", u], ["gp%d" % q], 256, tt(T.gp[:, q, :], T.ob[:, oc(j)], pj(k), A.mult), u)
+    def gram(d0, d1, tiles):
+        for l in range(d0, d1):
+            j, w = PAIRS[l]; q = slot(l)
+            v(["ob0", "ob1"] if w > 3 else ["ob0"], ["gp%d" % q], 256, tt(T.gp[:, :, 16 * q:16 * q + 16], T.ob[:, j, :, :], T.ob[:, w, :, :], A.mult))
         for c in range(2):
-            n = 8 * (q1 - q0); mp = T["mp%d" % c]
-            pe(["e2"] + ["gp%d" % q for q in range(q0, q1)], ["mg%d" % c],
-               [(mp[:, 0:n], T.e2[:, 15 - r:143 - r], T.gp[:, q0:q1, 16 * r + c:16 * r + 16:2], r == 0, r == 15, max(64, n)) for r in range(16)], "mp%d" % c)
-            s(["mg%d" % c], ["g%d0.%d" % (c, q0)], n, act(T["gm%d" % c][:, 0, 24 + 8 * q0:24 + 8 * q1], mp[:, 0:n], F.Copy, scale=0.0625, bias=-0.46875), "mp%d" % c)
-    gram(3, 6)
+            for q0, q1, p0, c0, name in tiles:
+                u = "up%d" % c; m = 8 * (q1 - q0)
+                pe(["d8"] + ["gp%d" % z for z in range(q0, q1)], [u], [(T[u][0:m, c0 + r:c0 + 128:16], T.gp[:, r, 16 * q0 + c:16 * q1:2], T.d8[:, :], True, True, 64) for r in range(16)], u)
+                o = T["gb%d" % c][0:m, :] if q0 == 16 else T["gm%d" % c][p0:m, 0, :]
+                v([u], [name + str(c)], 128, ts(o, T[u][p0:m, c0:c0 + 128], -1800.0, None, A.add), u)
+    gram(0, 3, [(0, 4, 0, 0, "go")])
+    gram(3, 7, [(0, 8, 32, 128, "ga")])
     for c in range(2):
-        v(["raw%d.%d" % (c, h) for h in range(4)], ["tab%d" % c], 904, cp(T["tab%d" % c][:, 0:904], T["raw%d" % c][:, :]))
-        gp([], ["tad%d" % c], 128, io(T["tab%d" % c][:, 904:1032], [[0, 128]], 0, 0))
-    gram(0, 3)
-    gram(6, 21)
+        v([], ["tab%d" % c], 128, ms(T["tab%d" % c][:, 904:1032], 0.0))
+        for h in range(4):
+            gp(["raw%d.%d" % (c, z) for z in range(4)], ["tad%d.%d" % (c, h)], 226, sl(T["tab%d" % c][:, 226 * h:226 * h + 226], T["raw%d" % c][:, 226 * h:226 * h + 226], [[0, 226]], A.is_ge, 0, 0))
+    late = [lambda: gram(7, len(PAIRS), [(0, 16, 64, 128, "gc"), (16, 22, 0, 256, "gb")])]
 
     ubank = [0]
     def nextu():
-        ubank[0] = (ubank[0] + 1) % 4
+        ubank[0] = 1 - ubank[0]
         return "up%d" % ubank[0]
+
+    def out(t, c):
+        def b(n): return T[n + str(c)]
+        def k(n): return n + str(c)
+        mp = b("mp"); mm = []
+        for z in range(8):
+            o = mp[0:24, 128 + z:256:8]
+            mm += [(o, T.eo3[:, :], b("ohb")[:, 16 * z:16 * z + 16], True, False, 24)] + \
+                  [(o, T.eo[:, 2 - m:26 - m], b("sel")[:, 128 * e + 16 * z:128 * e + 16 * z + 16], False, e == 2, 24) for e, m in enumerate((1, 2, 0))]
+        pe([k("sel"), k("ohb"), "eo", "eo3.0", "eo3.1", "eo3.2"], [k("mb"), k("mg")], mm, k("mp"))
+        s([k("mb")], ["yb%d.%d" % (t, c)], 128, act(T.yb[0:24, t, c:256:2], mp[0:24, 128:256], F.Copy, bias=-1.0), k("mp"))
+        if c: dma("y", ["yb%d.0" % t, "yb%d.1" % t], ["yn%d" % t], T.yn[:, 768 * t:768 * t + 768], T.yb[0:24, t, :], "y%d" % t, 2000)
 
     win = T.cv[:, 0:2064]
     for t in range(RO):
         for c in range(2):
             def b(n): return T[n + str(c)]
             def k(n): return n + str(c)
-            G = b("gm"); last = t == RO - 1
-            gO, gE, gN = (["g%d0.3" % c], ["g%d0.0" % c], ["g%d0.6" % c]) if t == 0 else (["g%d%d" % (c, t)],) * 3
-            cf = "cf%d%d" % (c, t); rp, mp = b("rp"), b("mp")
+            last = t == RO - 1
+            G3, G6, GA = b("gm")[0:32, t, :], b("gm")[0:64, t, :], b("gm")[:, t, :]
+            g3, g6 = ([k("go")], [k("go"), k("ga")]) if t == 0 else (["g%d%d" % (c, t)],) * 2
+            rp, mp = b("rp"), b("mp")
             stage[0] = 2 * t + c - EARLY; crit[0] = 1
-            v(gO + ["off"], [cf], 48, tt(G[:, t, 0:24], G[:, t, 48:72], T.off[:, :], A.add))
-            v([cf], [k("cl")], 24, ts(b("cl")[:, :], G[:, t, 0:24], -M, None, A.add))
-            nfs = [k("nf0"), k("nf1"), k("nf2")]
-            for m0, m1 in SPLIT:
-                s([k("cl"), k("tab")], nfs[m0:m1], 128 * (m1 - m0) * GAM, act(b("nf")[:, 128 * m0:128 * m1], b("tab")[:, 0:904].indirect(b("cl")[:, 8 * m0:8 * m1]), F.Copy))
-                v(nfs[m0:m1] + ["l4"], [k("nu%d" % m) for m in range(m0, m1)], 128 * (m1 - m0) * GAM,
-                  cp(b("nu")[:, 128 * m0:128 * m1], b("nf")[:, 128 * m0:128 * m1].indirect(T.l4[:, 0:8 * (m1 - m0)])))
+            pe(g3 + ["cs"], [k("md"), k("mg")], [(mp[:, 384:408], G3, T.cs[0:32, :], True, True, 64)], k("mp"))
+            v([k("md")], [k("cl")], 24, ts(b("cl")[:, :], mp[:, 384:408], M, -M, A.add, A.add), k("mp"))
+            table, tn = (b("raw")[:, :], ["raw%d.%d" % (c, h) for h in range(4)]) if t == 0 else (b("tab")[:, 0:904], [k("tab")])
+            sg([k("cl")] + tn, [k("nf")], 384, act(b("nf")[:, :], table.indirect(b("cl")[:, :]), F.Copy))
+            for n0, n1 in SPLIT:
+                j0, j1 = 24 * CUT[n0], 24 * CUT[n1]
+                vg([k("nf"), "l4"], [k("nu%d" % n) for n in range(n0, n1)], j1 - j0, cp(b("nu")[:, j0:j1], b("nf")[:, :].indirect(T.l4[:, j0 // 16:j1 // 16])))
             crit[0] = 0
-            v([cf, "off"], [k("xb")], 16, tt(b("xh")[:, 0:8], G[:, t, 16:24], T.off[:, 0:8], A.subtract))
-            s(gE, [k("xu")], 24, act(b("xh")[:, 8:56:2], G[:, t, 24:48], F.Copy))
-            v(gE + [k("xu")], [k("xl")], 48, tt(b("xh")[:, 9:56:2], G[:, t, 24:48], b("xh")[:, 8:56:2], A.subtract))
-            pe([k("xb"), k("xu"), k("xl"), "idb"], [k("mx")], [(mp[0:56, 0:128], b("xh")[:, :], T.idb[:, :], True, True, 128)], k("mp"))
-            s([k("mx")], [k("xt")], 128, act(b("xt")[0:56, :], mp[0:56, 0:128], F.Copy), k("mp"))
             if not last:
-                nq = NQ[t + 1]
-                s([k("cl"), "binw"], [k("bh")], 128 * GAM, act(b("bh")[:, :], T.binw[:, 0:904].indirect(b("cl")[:, 16:24]), F.Copy))
-                s(gO + gE + gN + ["l1"], [k("cand")], 32 * nq * GAM, act(b("cand")[:, 0:32 * nq], G[:, t, 24:24 + 8 * NQ[t]].indirect(T.l1[:, 0:2 * nq]), F.Copy))
+                sg([k("cl"), "binw"], [k("bh")], 128, act(b("bh")[:, :], T.binw[:, 0:904].indirect(b("cl")[:, 16:24]), F.Copy))
             stage[0] = 2 * t + c
-            def sub(e, col): return (rp[:, 128 * col:128 * col + 128], T.ee[0:56, 128 * e:128 * e + 128], b("xt")[0:56, :], False, False, 128)
-            pe(["cst", "on1"], [k("rd0"), k("rd1"), k("rd2")], [(rp[:, 0:384], T.ones[0:64, 0:128], T.cst[0:64, 0:384], True, False, 384)], k("rp"))
-            pe([k("xt"), "ee", "eeb", k("rd0")], [k("rx")], [sub(0, 0), sub(1, 1), sub(2, 2)], k("rp"))
-            red = [k("rx")]
+            if t: out(t - 1, c)
+            R1, R0 = rp[:, 0:128], mp[:, 0:128]
+            pe(g6 + ["cst", "on1", "eh0"], [k("ra"), k("rg")], [(R1, T.ones[0:64, 0:128], T.cst[0:64, 0:128], True, False, 128), (R1, T.eh[0:64, 0:128], G6, False, False, 128)], k("rp"))
+            pe(g6 + ["cst", "on1", "eh2"], [k("ma"), k("mg")], [(R0, T.ones[0:64, 0:128], T.cst[0:64, 128:256], True, False, 128), (R0, T.eh[0:64, 256:384], G6, False, False, 128)], k("mp"))
             NB = len(CUT) - 1
             for n in range(NB):
-                R = range(CUT[n], CUT[n + 1]); E = 128 * len(R); cs = slice(128 * CUT[n], 128 * CUT[n + 1]); x = "%d.%d" % (c, n)
-                def gat(m): return win.indirect(b("nu")[:, 128 * m + 8 * CUT[n]:128 * m + 8 * CUT[n + 1]])
-                cvr = ["cv", "cvz"]
-                s(cvr + [k("nu0")], ["vb" + x], E * GAM, act(b("vb")[:, cs], gat(0), F.Copy))
-                s(cvr + [k("nu1")], ["vc" + x], E * GAM, act(b("vc")[:, cs], gat(1), F.Copy))
-                if MIX[t][c][n]: v(cvr + [k("nu2")], ["va" + x], E * GAM, cp(b("va")[:, cs], gat(2)))
-                else: s(cvr + [k("nu2")], ["va" + x], E * GAM, act(b("va")[:, cs], gat(2), F.Copy))
-                ub, uc = nextu(), nextu()
-                pe(["vb" + x, "vc" + x, "idb", "id4"], [ub], [(T[ub][:, 0:E], T.idb[:, :], b("vb")[:, cs], True, False, E), (T[ub][:, 0:E], T.id4[:, :], b("vc")[:, cs], False, True, E)], ub)
-                pe(["vb" + x, "idb"], [uc], [(T[uc][:, 0:E], T.idb[:, :], b("vb")[:, cs], True, True, E)], uc)
-                v(["va" + x, ub], ["p1" + x], E, tt(b("pw")[:, cs], b("va")[:, cs], T[ub][:, 0:E], A.mult), ub)
-                v(["vc" + x, uc], ["p0" + x], E, tt(b("pr")[:, cs], b("vc")[:, cs], T[uc][:, 0:E], A.mult), uc)
-                pe(["p1" + x, "d8f", k("rd0")], ["r1" + x], [(rp[:, 128 + r:256:16], b("pw")[:, 128 * r:128 * r + 128], T.d8f[:, :], False, False, 256) for r in R], k("rp"))
-                red.append("r1" + x)
-                pe(["p0" + x, "d8", k("rd0")] + (red if n == NB - 1 else []), ["r0" + x],
-                   [(rp[:, r:128:16], b("pr")[:, 128 * r:128 * r + 128], T.d8[:, :], False, r == 15, 64) for r in R], k("rp"))
-                red.append("r0" + x)
+                R = range(CUT[n], CUT[n + 1]); E = 128 * len(R); e0 = 128 * CUT[n]; cs = slice(e0, e0 + E); x = "%d.%d" % (c, n); end = n == NB - 1
+                def gat(m0, m1): return win.indirect(b("nu")[:, (3 * e0 + E * m0) // 16:(3 * e0 + E * m1) // 16])
+                def vv(m0, m1, z=0, w=None): return b("vv")[:, 3 * e0 + E * m0 + z:3 * e0 + (E * m1 if w is None else E * m0 + z + w)]
+                cvr = ["cv", "cvz", k("nu%d" % n)]; mix = MIX[t][c][n]
+                if mix == 2: sg(cvr, ["vb" + x, "va" + x], 3 * E, act(vv(0, 3), gat(0, 3), F.Copy))
+                else:
+                    sg(cvr, ["vb" + x], 2 * E, act(vv(0, 2), gat(0, 2), F.Copy))
+                    if mix: vg(cvr, ["va" + x], E, cp(vv(2, 3), gat(2, 3)))
+                    else: sg(cvr, ["va" + x], E, act(vv(2, 3), gat(2, 3), F.Copy))
+                ub = nextu(); mm = []
+                for z in range(0, E, 512):
+                    w = min(512, E - z)
+                    mm += [(T[ub][:, z:z + w], T.idb[:, :], vv(0, 1, z, w), True, False, w), (T[ub][:, z:z + w], T.id4[:, :], vv(1, 2, z, w), False, True, w)]
+                pe(["vb" + x, "idb", "id4"], [ub], mm, ub)
+                v(["vb" + x], ["p0" + x], E, tt(b("pr")[:, cs], vv(0, 1), vv(1, 2), A.mult))
+                v(["va" + x, ub], ["p1" + x], E, tt(b("pw")[:, cs], vv(2, 3), T[ub][:, 0:E], A.mult), ub)
+                pe(["p0" + x, "d8s", k("mg")], [k("ma"), k("mg")] if end else ["r0" + x], [(mp[:, r:128:16], b("pr")[:, 128 * r:128 * r + 128], T.d8s[:, :], False, r == 15, 64) for r in R], k("mp"))
+                pe(["p1" + x, "d8f", k("rg")], [k("ra"), k("rg")] if end else ["r1" + x], [(rp[:, r:128:16], b("pw")[:, 128 * r:128 * r + 128], T.d8f[:, :], False, r == 15, 256) for r in R], k("rp"))
+                if late: late.pop()()
             crit[0] = 1
-            v(red, [k("yy")], 128, ts(b("yy")[:, :], rp[:, 128:256], 1.5 * 2.0 ** 35, -1.5 * 2.0 ** 35, A.add, A.add), k("rp"))
-            v([k("yy")] + red, [k("yz")], 128, tt(b("yz")[:, :], rp[:, 256:384], b("yy")[:, :], A.subtract), k("rp"))
-            v([k("yz")], [k("rd1")], 128, tt(rp[:, 128:256], rp[:, 128:256], b("yz")[:, :], A.add), k("rp"))
-            s([k("yy")], [k("ac")], 128, act(b("ab")[:, 256:384], b("yy")[:, :], F.Abs, scale=1.0 / 4096))
-            s([k("rd0"), k("rd1")], [k("ab")], 256, act(b("ab")[:, 0:256], rp[:, 0:256], F.Abs), k("rp"))
-            v([k("ab"), k("ac")], [k("hf")], 192, ts(b("hf")[:, :], b("ab")[:, :], 150.0, W, A.is_le, A.mult))
-            pe([k("hf"), "idb"], [k("rs")], [(rp[:, 384:512], T.idb[:, :], b("hf")[:, 128 * e:128 * e + 128], e == 0, e == 2, 128) for e in range(3)], k("rp"))
-            v([k("rs")], [k("ev")], 128, ts(b("ev")[:, :], rp[:, 384:512], 3 * W, W, A.is_equal, A.mult), k("rp"))
-            mm = [(mp[:, 192:200], b("ev")[:, :], T.cw[:, :], True, True, 64)]
+            H = [b("hf")[:, 128 * e:128 * e + 128] for e in range(4)]; EV = H[3]
+            v([k("ma")], [k("h0")], 128, ts(H[0], R0, 1.5 * 2.0 ** 32, 1.5 * 2.0 ** 32, A.add, A.not_equal), k("mp"))
+            if not TWO: s([k("ra")], [k("ac")], 128, act(b("ab")[:, :], R1, F.Abs, scale=1.0 / 4096), k("rp"))
+            v([k("ra")], [k("yy")], 128, ts(b("yy")[:, :], R1, 1.5 * 2.0 ** 35, -1.5 * 2.0 ** 35, A.add, A.add), k("rp"))
+            if TWO:
+                v([k("ra")], [k("h1")], 128, ts(H[1], R1, 150.5 * 4096, None, A.is_gt), k("rp"))
+                v([k("ra")], [k("h2")], 128, ts(b("ab")[:, :], R1, -150.5 * 4096, None, A.is_lt), k("rp"))
+            v([k("ra"), k("yy")], [k("lo")], 128, tt(b("lo")[:, :], R1, b("yy")[:, :], A.subtract), k("rp"))
+            if not TWO: v([k("ac")], [k("h1")], 64, ts(H[1], b("ab")[:, :], 150.0, None, A.is_gt))
+            NAC = [H[1], b("ab")[:, :]][:1 + TWO]; nac = [k("h1"), k("h2")][:1 + TWO]
+            Ra, Re = mp[:, 128:256], mp[:, 256:384]
+            pe(g6 + [k("h0"), "eh1", "id8", "on1", "on2", "cst"], [k("mb"), k("mc"), k("mg")],
+               [(mp[:, 128:384], T.cst[0:1, 256:384], T.ones[0:1, 0:256], True, False, 256), (Ra, T.eh[0:64, 128:256], G6, False, False, 128), (Re, T.eh[0:64, 128:256], G6, False, False, 128),
+                (Re, T.kw[:, 384:512], H[0], False, False, 128)], k("mp"))
+            pe([k("lo"), "ids", "id8"] + nac, [k("mb"), k("mc"), k("mg")], [(Re, T.kw[:, 384:512], z, False, False, 128) for z in NAC] +
+               [(Ra, T.ids[:, :], b("lo")[:, :], False, False, 128), (Re, T.ids[:, :], b("lo")[:, :], False, True, 128)], k("mp"))
+            v([k("mb"), k("mc")], [k("ev")], 256, ts(b("hf")[:, 256:512], mp[:, 128:384], 1.5 * 2.0 ** 32, 1.5 * 2.0 ** 32, A.add, A.is_equal), k("mp"))
+            whole = [k("ra"), k("rb"), k("rc")]
             if not last:
-                mm = [(mp[:, 128:192], T.c2k[:, :], T.wt[:, 256:320], True, False, 64)] + \
-                     [(mp[:, 128:192], b("hf")[:, 128 * e:128 * e + 128], T.wt[:, 64 * w:64 * w + 64], False, False, 64) for e, w in enumerate((0, 2, 1))] + \
-                     [(mp[:, 128:192], b("ev")[:, :], T.wt[:, 192:256], False, True, 64)] + mm
-            pe([k("hf"), k("ev"), "cw", "wt", "c2k"], [k("mc")], mm, k("mp"))
-            if not last:
-                v([k("mc"), "rst"], [k("mi")], 64, scan(b("mi")[:, :], T.rst[:, :], mp[:, 128:192], 0.0, A.add, A.min), k("mp"))
-            v([k("mc")], [k("cd")], 8, cp(b("cd")[:, :], mp[:, 192:200]), k("mp"))
-            if last:
-                pe([k("cd"), "bcm"], [k("mb")], [(mp[:, 256 + 8 * r:264 + 8 * r], T.bcm[:, 128 * r:128 * r + 128], b("cd")[:, :], True, True, 64) for r in range(16)], k("mp"))
-                v([k("mb"), "wq"], [k("ohb")], 128, ts(b("ohb")[:, :], mp[:, 256:384], T.pf[:, 9:10], 4096.0, A.is_equal, A.mult), k("mp"))
-                for e in range(3):
-                    v([k("ohb"), nfs[e], "l4"], [k("sel%d" % e)], 128 * GAM, tt(b("sel")[:, 128 * e:128 * e + 128], b("nf")[:, 128 * e:128 * e + 128].indirect(T.l4[:, 0:8]), b("ohb")[:, :], A.min))
-            else:
-                v([k("mi"), k("cand"), "l2"], [k("pm")], 32 * nq * GAM, tt(b("pm")[:, 0:32 * nq], b("mi")[:, :].indirect(T.l2[:, 0:2 * nq]), b("cand")[:, 0:32 * nq], A.min))
-                v([k("pm"), "rs4"], [k("pn")], 32 * nq, scan(b("pn")[:, 0:32 * nq], T.rs4[:, 0:32 * nq], b("pm")[:, 0:32 * nq], 0.0, A.add, A.max))
-                v([k("pn")], ["nx%d%d" % (c, t)], 8 * nq, cp(b("nx")[:, t, 0:8 * nq], b("pn")[:, 3:32 * nq:4]))
+                mm = [(rp[:, :], T.ones[0:1, 0:128], T.zr[0:1, :], True, False, 512)]
+                for x in range(4):
+                    mm.append((rp[:, x:512:4], T.ph[:, x, :], GA, False, False, 128))
+                    if t == 0: mm.append((rp[:, x:512:4], T.ph[0:48, 4 + x, :], b("gb")[0:48, :], False, False, 128))
+                pe(g6 + names + ["pw0", "pw1", "pw2", "pw3", "on1"] + ([k("gb"), k("gc")] if t == 0 else []), whole + [k("rg")], mm, k("rp"))
+                pe([k("h0"), "kn"] + nac, whole + [k("rg")], [(rp[:, x:512:4], T.kw[:, 128:256], z, False, False, 128) for x, z in [(1, H[0])] + [(2, z) for z in NAC]], k("rp"))
+                pe([k("ev"), "kw", "kf"], whole + [k("rg")], [(rp[:, 3:512:4], T.kw[:, 0:128], H[2], False, False, 128), (rp[:, 0:512:4], T.kw[:, 256:384], EV, False, True, 128)], k("rp"))
+                v(whole + ["rst"], [k("xs")], 512, scan(b("xs")[:, :], T.rst[:, :], rp[:, :], 0.0, A.add, A.max), k("rp"))
+                v([k("xs")], [k("ra")], 128, ts(R1, b("xs")[:, 3:512:4], 1.5 * 2.0 ** 35, -1.5 * 2.0 ** 35, A.add, A.add), k("rp"))
+                v([k("xs"), k("ra")], ["nx%d%d" % (c, t)], 128, tt(b("nx")[:, t, :], b("xs")[:, 3:512:4], R1, A.subtract), k("rp"))
                 an = "a%d%d" % (t + 1, c)
                 op("g", ["nx%d%d" % (c, t)], ["g%d%d" % (c, t + 1)], 500,
-                   (lambda o, i, a: lambda: g.remote_dma(o, i, T.sem[a], T.sem.sent, dst[1], dst[0], dst[2]))(G[:, t + 1, 24:24 + 8 * nq], b("nx")[:, t, 0:8 * nq], an),
+                   (lambda o, i, a: lambda: g.remote_dma(o, i, T.sem[a], T.sem.sent, dst[1], dst[0], dst[2]))(b("gm")[:, t + 1, :], b("nx")[:, t, :], an),
                    None, an, RLAT)
                 crit[0] = 0
-                pe([k("cd"), "bcm"], [k("mb")], [(mp[:, 256 + r:384:16], T.bcm[:, 128 * r:128 * r + 128], b("cd")[:, :], True, True, 64) for r in range(16)], k("mp"))
-                v([k("mb"), "wq"], [k("ohb")], 128, ts(b("ohb")[:, :], mp[:, 256:384], T.pf[:, 9:10], 4096.0, A.is_equal, A.mult), k("mp"))
-                s([k("ohb")], [k("ohf")], 128, act(b("ohf")[:, :], b("ohb")[:, :], F.Copy, scale=0.5))
+            pe([k("ev"), "cw"], [k("me"), k("mg")], [(mp[:, 408:416], EV, T.cw[:, :], True, True, 64)], k("mp"))
+            if last: v([k("me")], [k("cd")], 8, cp(b("cd")[:, :], mp[:, 408:416]), k("mp"))
+            else: s([k("me")], [k("cd")], 8, act(b("cd")[:, :], mp[:, 408:416], F.Copy), k("mp"))
+            pe([k("cd")] + ["bcm%d" % u for u in range(4)], [k("mc"), k("mg")], [(mp[:, 256 + r:384:16], T.bcm[:, 128 * r:128 * r + 128], b("cd")[:, :], True, True, 64) for r in range(16)], k("mp"))
+            v([k("mc"), "wp"], [k("ohb")], 128, ts(b("ohb")[:, :], mp[:, 256:384], T.pf[:, 8:9], 2048.0, A.is_equal, A.mult), k("mp"))
+            if not last:
+                gp([k("ohb")], [k("ohf")], 128, sl(b("ohf")[:, :], b("ohb")[:, :], [[0, 128]], A.is_ge, 0, 0))
                 mm = []
                 for kk in range(2):
                     o = rp[:, 128 * kk:128 * kk + 128]
-                    mm += [(o, T.t1[0:32, 128 * kk:128 * kk + 128], b("xt")[0:32, :], True, False, 128), (o, b("bh")[:, :], T.rg[:, :], False, False, 128),
-                           (o, T.idb[:, :], T.mk[:, 128 * kk:128 * kk + 128], False, False, 128), (o, b("ohb")[:, :], T.rg[:, :], False, True, 128)]
-                pe([k("xt"), k("bh"), k("ohb"), "t1.0", "t1.1", "rg", "mk", "idb"], [k("rd0"), k("rd1")], mm, k("rp"))
-                v([k("rd0"), k("rd1")], [k("fl")], 256, ts(b("fl")[:, :], rp[:, 0:256], 0.0, None, A.is_equal), k("rp"))
-                pe([k("fl"), cf, "idf", "h4"], [k("my")], [(mp[:, 200:208], T.idf[:, :], G[:, t, 16:24], True, False, 256)] +
-                   [(mp[:, 200 + 4 * kk:204 + 4 * kk], b("fl")[:, 128 * kk:128 * kk + 128], T.h4[:, 0:4], False, kk == 1, 64) for kk in range(2)], k("mp"))
-                v([k("my"), "dum"], [k("so")], 8, tt(b("so")[:, :], mp[:, 200:208], T.dum[:, 0:8], A.min), k("mp"))
-                v([k("so")], [k("su")], 8, ts(b("su")[:, :], b("so")[:, :], -M, None, A.add))
-                v([k("su"), nfs[2], k("ohf"), k("tad")], [k("tab")], 128 * 3.8, tt(b("tab")[:, :].indirect(b("su")[:, :]), b("nf")[:, 256:384], b("ohf")[:, :], A.max))
-                pe([k("ohb"), "idb"], [k("rd0"), k("rd1"), k("rd2")], [(rp[:, 128 * e:128 * e + 128], T.idb[:, :], b("ohb")[:, :], True, True, 128) for e in range(3)], k("rp"))
-                v([k("rd0"), k("rd1"), k("rd2")] + nfs, [k("sel0"), k("sel1"), k("sel2")], 384, tt(b("sel")[:, :], b("nf")[:, :], rp[:, 0:384], A.min), k("rp"))
-                stage[0] = 2 * t + c + LATE
-            pe([k("sel0"), k("sel1"), k("sel2"), k("ohb"), "eo", "eo3.0", "eo3.1", "eo3.2"], [k("mo")], [(mp[0:24, 384:512], T.eo3[:, :], b("ohb")[:, :], True, False, 128)] +
-               [(mp[0:24, 384:512], T.eo[:, 2 - m:26 - m], b("sel")[:, 128 * e:128 * e + 128], False, e == 2, 128) for e, m in enumerate((1, 2, 0))], k("mp"))
-            if last: s([k("mo")], ["yb3.%d" % c], 128, act(T.yb[0:24, t, c:256:2], mp[0:24, 384:512], F.Copy, bias=-1.0), k("mp"))
-            else: s([k("mo")], [k("ot")], 128, act(T.ot[0:24, 128 * c:128 * c + 128], mp[0:24, 384:512], F.Copy), k("mp"))
-        if not last: s(["ot0", "ot1", "l3"], ["yb%d" % t], 256 * GAM, act(T.yb[:, t, :], T.ot[:, :].indirect(T.l3[:, :]), F.Copy, bias=-1.0))
-        dma("y", ["yb3.0", "yb3.1"] if last else ["yb%d" % t], ["yn%d" % t], T.yn[:, 768 * t:768 * t + 768], T.yb[0:24, t, :], "y%d" % t, 2000)
+                    mm += [(o, T.t1[0:32, 128 * kk:128 * kk + 128], G3, True, False, 128), (o, b("bh")[:, :], T.rg[:, :], False, False, 128),
+                           (o, T.idb[:, :], T.mk[:, 128 * kk:128 * kk + 128], False, False, 128), (o, b("ohb")[:, :], T.rg2[:, :], False, True, 128)]
+                pe(g6 + [k("bh"), k("ohb"), "t1", "rg", "rg2", "mk", "idb"], [k("ra"), k("rb"), k("rg")], mm, k("rp"))
+                v([k("ra"), k("rb")], [k("fl")], 256, ts(b("fl")[:, :], rp[:, 0:256], 1.5 * 2.0 ** 27, 1.5 * 2.0 ** 27, A.add, A.is_equal), k("rp"))
+                pe(g6 + [k("fl"), "cs", "h4"], [k("mf"), k("mg")], [(mp[:, 416:424], G3, T.cs[0:32, 16:24], True, False, 64)] +
+                   [(mp[:, 416 + 4 * kk:420 + 4 * kk], b("fl")[:, 128 * kk:128 * kk + 128], T.h4[:, 0:4], False, kk == 1, 64) for kk in range(2)], k("mp"))
+                v([k("mf"), "dum"], [k("so")], 8, tt(b("so")[:, :], mp[:, 416:424], T.dum[:, 0:8], A.min), k("mp"))
+                v([k("so")], [k("su")], 8, ts(b("su")[:, :], b("so")[:, :], M, -M, A.add, A.add))
+                v([k("su"), k("nf"), k("ohf")] + [k("tad") + ".%d" % h for h in range(4)], [k("tab")], 128 * 3.8, tt(b("tab")[:, :].indirect(b("su")[:, :]), b("nf")[:, 256:384], b("ohf")[:, :], A.max))
+            pe([k("ohb"), "idb"], whole + [k("rg")], [(rp[:, 128 * e:128 * e + 128], T.idb[:, :], b("ohb")[:, :], True, True, 128) for e in range(3)], k("rp"))
+            v(whole + [k("nf")], [k("sel")], 384, tt(b("sel")[:, :], b("nf")[:, :], rp[:, 0:384], A.min), k("rp"))
+            if last: out(t, c)
     return ops
-
-
-DEFER, SLC, RLAT = 1, 100.0, 3000
-SPLIT = [(0, 2), (2, 3)]
-CUT = [0, 4, 8, 12, 16]
 
 
 def order(ops):
@@ -348,7 +348,7 @@ def order(ops):
     pri = [0.0] * n
     for i in range(n - 1, -1, -1):
         ops[i]["k"] = min([ops[i]["k"]] + [ops[j]["k"] for j in succ[i]])
-        pri[i] = (((i + 1) * SEED * 2654435761) % 4096) / 4096.0 * NOISE + ops[i]["ns"] + ops[i]["lat"] + max([pri[j] + HOP for j in succ[i]] + [0.0])
+        pri[i] = ops[i]["ns"] + ops[i]["lat"] + max([pri[j] + HOP for j in succ[i]] + [0.0])
     free = {e: 0.0 for e in "vspgy"}; fin = [None] * n; left = [len(o["d"]) for o in ops]
     ready = [i for i in range(n) if left[i] == 0]; at = [0.0] * n; seq = []
     while ready:
@@ -363,15 +363,39 @@ def order(ops):
     return seq, succ, max(fin)
 
 
-CASES = [(1.56, 0.42, 150.0, 1.1), (1.2, 0.52, 250.0, 1.25), (2.0, 0.52, 200.0, 1.0)]
-STEPS = 40000
+def justify(ops, seq, succ, rounds):
+    n = len(ops); hop = lambda i, j: 0.0 if ops[i]["e"] == "p" and ops[j]["e"] == "p" else HOP
+
+    def place(sq, back):
+        busy = {e: [] for e in "vspgy"}; st = [0.0] * n
+        for i in sq:
+            o = ops[i]; ns = o["ns"]
+            if back: t = max([st[j] + ops[j]["ns"] + hop(i, j) for j in succ[i]] + [0.0]) + o["lat"]
+            else: t = max([st[j] + ops[j]["ns"] + ops[j]["lat"] + hop(i, j) for j in o["d"]] + [0.0])
+            q = busy[o["e"]]; a = len(q)
+            while a and q[a - 1][0] >= t: a -= 1
+            if a: t = max(t, q[a - 1][1])
+            while a < len(q) and q[a][0] < t + ns: t = q[a][1]; a += 1
+            q.insert(a, (t, t + ns)); st[i] = t
+        return st, max(st[i] + ops[i]["ns"] + (0.0 if back else ops[i]["lat"]) for i in range(n))
+    best = None
+    for _ in range(rounds):
+        st, span = place(seq, False); seq = sorted(seq, key=lambda i: st[i])
+        if best is None or span < best[0]: best = (span, seq)
+        sq = sorted(seq[::-1], key=lambda i: -(st[i] + ops[i]["ns"] + ops[i]["lat"])); st, span = place(sq, True)
+        seq = sorted(sq[::-1], key=lambda i: -(st[i] + ops[i]["ns"]))
+    return best[1], best[0]
+
+
+CASES = [(1.56, 1.0, 200.0, 1.05), (1.2, 0.9, 200.0, 1.3), (1.95, 0.7, 200.0, 1.3)]
+STEPS, HEAT = 40000, 100.0
 KEPT = {}
 
 
 def polish(ops, seq, succ, steps):
     n = len(ops); eng = ["vspgy".index(o["e"]) for o in ops]; lat = [o["lat"] for o in ops]
     dep = [[(j, not (o["e"] == "p" and ops[j]["e"] == "p")) for j in o["d"]] for o in ops]
-    cost = [[o["fx"] + o["n"] * (pc if o["e"] == "p" else CYC * gm / GAM if o["ga"] else CYC * f) for o in ops] for gm, pc, hop, f in CASES]
+    cost = [[f * (o["fx"] + (o["ns"] - o["fx"]) * (gm / GAM if o["ga"] else 1.0)) for o in ops] for gm, pc, hop, f in CASES]
 
     def span(sq):
         tot = 0.0
@@ -383,22 +407,55 @@ def polish(ops, seq, succ, steps):
                     x = fin[j] + hop if h else fin[j]
                     if x > st: st = x
                 st += ns[i]; free[eng[i]] = st; fin[i] = st + lat[i]
-            tot += max(fin) + 0.02 * sum(fin) / n
+            tot += pc * (max(fin) + 0.02 * sum(fin) / n)
         return tot / len(CASES)
-    best = span(seq); r = 12345
+
+    def held(sq, case):
+        ns = cost[case]; hop = CASES[case][2]; free = [0.0] * 5; prev = [None] * 5; fin = [0.0] * n; why = [None] * n
+        for i in sq:
+            e = eng[i]; st = free[e]; y = (prev[e], True)
+            for j, h in dep[i]:
+                x = fin[j] + hop if h else fin[j]
+                if x >= st: st = x; y = (j, False)
+            st += ns[i]; free[e] = st; fin[i] = st + lat[i]; why[i] = y; prev[e] = i
+        i = max(range(n), key=lambda z: fin[z]); out = []
+        while why[i][0] is not None:
+            if why[i][1] and eng[i] < 4: out.append((why[i][0], i))
+            i = why[i][0]
+        return out
+
+    def ahead(sq, u, w):
+        a, z = sq.index(u), sq.index(w); need = set(ops[w]["d"]); took = set(); engs = set(); first = [w]; rest = []
+        for i in reversed(sq[a:z]):
+            if i in need or eng[i] in engs:
+                if i == u: return None
+                need |= ops[i]["d"]; engs.add(eng[i]); first.append(i)
+            else: rest.append(i)
+        return sq[:a] + first[::-1] + rest[::-1] + sq[z + 1:]
+    cur = best = span(seq); top = seq; r = 12345; pairs = None
     for it in range(steps):
-        r = (r * 1103515245 + 12345) % 2147483648; a = (r >> 8) % n; i = seq[a]
-        if eng[i] > 2: continue
-        r = (r * 1103515245 + 12345) % 2147483648; hops = 1 + (r >> 8) % 3; up = (r >> 20) & 1
-        near = set(ops[i]["d"]) if up else set(succ[i]); p = a; to = None
-        while hops and 0 < p < n - 1:
-            p += -1 if up else 1
-            if seq[p] in near: break
-            if eng[seq[p]] == eng[i]: to = p; hops -= 1
-        if to is None: continue
-        sq = seq[:a] + seq[a + 1:]; sq.insert(to, i); x = span(sq)
-        if x <= best + 60.0 * (1.0 - it / steps): best, seq = x, sq
-    return seq, best
+        r = (r * 1103515245 + 12345) % 2147483648
+        if (r >> 8) % 4:
+            if pairs is None: pairs = held(seq, (r >> 12) % len(CASES))
+            if not pairs: pairs = None; continue
+            sq = ahead(seq, *pairs.pop((r >> 14) % len(pairs)))
+            if sq is None: continue
+        else:
+            r = (r * 1103515245 + 12345) % 2147483648; a = (r >> 8) % n; i = seq[a]
+            if eng[i] > 3: continue
+            r = (r * 1103515245 + 12345) % 2147483648; hops = 1 + (r >> 8) % 3; up = (r >> 20) & 1
+            near = set(ops[i]["d"]) if up else set(succ[i]); p = a; to = None
+            while hops and 0 < p < n - 1:
+                p += -1 if up else 1
+                if seq[p] in near: break
+                if eng[seq[p]] == eng[i]: to = p; hops -= 1
+            if to is None: continue
+            sq = seq[:a] + seq[a + 1:]; sq.insert(to, i)
+        x = span(sq)
+        if x <= cur + HEAT * (1.0 - it / steps):
+            cur, seq, pairs = x, sq, None
+            if x < best: best, top = x, sq
+    return top, best
 
 
 def rank_program(g, core, T, topo):
@@ -410,7 +467,7 @@ def rank_program(g, core, T, topo):
     ops = build(g, T, (rid, pid, topo.mask(core, nxt)))
     nen = len(topo.engines(core, nxt))
     seq, succ, _ = order(ops)
-    if "seq" not in KEPT: KEPT["seq"] = polish(ops, seq, succ, STEPS)[0]
+    if "seq" not in KEPT: KEPT["seq"] = polish(ops, justify(ops, seq, succ, 20)[0], succ, STEPS)[0]
     seq = KEPT["seq"]
     for a, i in enumerate(seq): ops[i]["t"] = a
     Q = {"v": g.vector, "s": g.scalar, "p": g.tensor, "g": g, "y": g.sync}

@@ -3,14 +3,20 @@ from concourse.mybir import AluOpType, ActivationFunctionType, AxisListType
 A, F = AluOpType, ActivationFunctionType
 RO = 4
 M = 12582912.0
-SC = 218.0 / 128
+SC = 1742.0 / 1024
 PAIRS = [(0, 2), (0, 3), (0, 1), (1, 2), (2, 3), (1, 3)] + [(j, 4) for j in range(4)] + [(j, 5) for j in range(5)] + [(j, 6) for j in range(6)]
 OB, OC, OA, ONE, AB, BC, AC = range(7)
 NEXT = [[1, 2, 3, 4, 5, 6], [0, 4, 2, 3, 5, 6], [0, 1, 4, 3, 5, 6], [0, 1, 2, 4, 5, 6]]
 PRIO = [-1, 2 + 64, 1 + 64, 0]
 
 
-def slot(l): return l if l < ONE else l + 1
+PACK = 0
+TWICE = [(1, 4), (2, 4), (3, 4), (0, 5), (5, 1), (2, 5), (3, 5), (4, 5)]
+
+
+def slot(l):
+    if l >= 15 and PACK: return 24 + [j for j, k in TWICE].index(PAIRS[l][0])
+    return l if l < ONE else l + 1
 
 
 SRC = [[None] * 16 for _ in NEXT]
@@ -18,39 +24,42 @@ for _x, _nx in enumerate(NEXT):
     SRC[_x][ONE] = ONE
     for _l, (_j, _k) in enumerate(PAIRS[:15]):
         SRC[_x][slot(_l)] = slot(PAIRS.index(tuple(sorted((_nx[_j], _nx[_k])))))
-CUT = [0, 4, 8, 12, 16]
-MIX = [[[2, 0, 2, 0], [1, 2, 0, 0]], [[1, 0, 0, 0], [1, 0, 0, 0]], [[1, 0, 0, 1], [1, 0, 0, 0]], [[1, 2, 2, 1], [1, 1, 0, 0]]]
-SLACK, EARLY, LATE = 0.0, 1.1, 1.6
-CYC, GAM, PEC, HOP = 0.83, 1.56, 0.42, 200.0
-SLC, RLAT, TWO = 100.0, 3000, 1
-SPLIT = [(0, 1), (1, 4)]
+CUTS = [[0, 4, 8, 12, 16], [0, 4, 8, 12, 14, 16]]
+MIX = [[[2, 2, 0, 0], [1, 2, 0, 0]], [[4, 2, 0, 0], [4, 2, 0, 0]], [[4, 2, 0, 0], [4, 2, 0, 0]], [[4, 2, 0, 0], [4, 1, 0, 0, 0]]]
+SLACK, EARLY, LATE = 0.0, 1.1, 1
+CYC, GAM, PEC, HOP = 0.83, 1.56, 0.42, 135.0
+SLC, RLAT, TWO, GDMA, XLAT, NFV = 100.0, 2550, 1, 1000, 3500, 0
+CDV, EVS, NXV, RSP, PFX, OB1 = 1, 1, 0, 4, 30.0, 0
+NUS, CLV = [(0, 1, "s"), (1, 9, "v")], 1
 
 S_, P_, B_, F_, H_, U_, I_ = "sbuf", "psum", "bfloat16", "float32", "float16", "uint16", "int32"
 SCRATCH = {}
 for _n, _w, _d in [
-        ("cv", 2064, B_), ("ones", 512, B_), ("zr", 512, B_), ("idb", 128, B_), ("id4", 128, B_), ("ids", 128, H_),
-        ("d8a", 8, B_), ("d8", 8, B_), ("d8s", 8, B_), ("d8f", 8, F_), ("eo", 32, H_), ("eo3", 24, B_), ("pint", 16, I_), ("pf", 24, F_), ("rst", 512, B_),
+        ("cv", 2064, B_), ("ones", 512, B_), ("zr", 128, B_), ("idb", 128, B_), ("id4", 128, B_), ("ids", 128, H_),
+        ("d8a", 8, B_), ("d8", 8, B_), ("d8s", 8, H_), ("d8f", 24, F_), ("dif", 128, F_), ("eo", 32, H_), ("eo3", 24, B_), ("pint", 16, I_), ("pf", 24, F_), ("rst", 512, B_),
         ("eh", 384, H_), ("cst", 384, B_), ("t1", 256, H_), ("binw", 912, B_), ("kw0", 128, B_), ("kw", 512, B_),
-        ("csf", 24, F_), ("cs", 24, H_), ("geo", 64, F_), ("cw", 8, B_), ("bcm", 2048, B_), ("rg0", 128, B_), ("rg", 128, B_), ("rg2", 128, B_),
-        ("mk0", 256, B_), ("mk1", 256, B_), ("mk2", 256, B_), ("mk", 256, B_), ("h4", 8, B_), ("dum", 16, F_),
-        ("lv", 8, I_), ("lf", 32, F_), ("lg", 24, F_), ("l4", 24, U_)]:
+        ("csf", 24, F_), ("csd", 48, F_), ("cs", 24, H_), ("geo", 64, F_), ("cw", 256, B_), ("rg0", 128, B_), ("rg", 128, B_), ("rg2", 128, B_),
+        ("mk0", 256, B_), ("mk1", 256, B_), ("mk", 256, B_), ("h4", 8, B_), ("dum", 16, F_),
+        ("lv", 8, I_), ("lf", 32, F_), ("lg", 48, F_), ("l4", 48, U_)]:
     SCRATCH[_n] = (S_, [128, _w], _d)
 SCRATCH["ob"] = (S_, [128, 7, 16, 16], B_)
 SCRATCH["gp"] = (S_, [128, 16, 352], B_)
+SCRATCH["gq"] = (S_, [128, 17, 128], F_)
 SCRATCH["yb"] = (S_, [128, 4, 256], F_)
 SCRATCH["ph"] = (S_, [128, 8, 128], H_)
 for _c in "01":
     for _n, _w, _d in [
-            ("raw", [904], I_), ("tab", [1032], F_), ("gm", [4, 128], H_), ("gb", [128], H_), ("nx", [3, 128], H_), ("cl", [24], U_), ("nf", [384], F_), ("nu", [384], U_),
-            ("bh", [128], B_), ("vv", [6144], B_),
-            ("pr", [2048], B_), ("pw", [2048], F_), ("yy", [128], F_), ("ab", [128], B_), ("hf", [512], B_), ("lo", [128], H_), ("cd", [8], B_), ("xs", [512], F_),
+            ("raw", [904], I_), ("tab", [1032], F_), ("gm", [4, 128], H_), ("gb", [128], H_), ("nx", [3, 128], H_), ("cl", [4, 24], U_), ("cx", [3, 24], U_), ("nf", [384], F_), ("nu", [384], U_),
+            ("bh", [128], B_), ("vv", [4, 1536], B_), ("xx", [2048], F_),
+            ("pr", [2048], H_), ("px", [2048], F_), ("pw", [2048], F_), ("yy", [128], F_), ("ab", [128], B_), ("hf", [512], B_), ("lo", [128], H_), ("cd", [128], B_), ("xs", [512], F_),
             ("ohb", [128], B_), ("ohf", [128], F_), ("sel", [384], H_), ("fl", [256], B_), ("so", [8], F_), ("su", [8], U_)]:
         SCRATCH[_n + _c] = (S_, [128] + _w, _d)
 for _n in ["rp0", "rp1", "mp0", "mp1"]:
     SCRATCH[_n] = (P_, [128, 512], F_)
-for _n in ["up0", "up1"]:
-    SCRATCH[_n] = (P_, [128, 1024], F_)
-SEMAPHORES = ["v", "s", "p", "g", "sent", "o0", "o1", "cv", "t0", "t1", "y0", "y1", "y2", "y3"] + ["a%d%d" % (t, c) for t in range(1, 4) for c in range(2)]
+NU = 4
+for _n in range(NU):
+    SCRATCH["up%d" % _n] = (P_, [128, 2048 // NU], F_)
+SEMAPHORES = ["v", "s", "p", "g", "sent", "o0", "o1", "cv", "t0", "t1", "y0", "y1", "y2", "y3"] + [a % (t, c) for t in range(1, 4) for c in range(2) for a in ("a%d%d", "ac%d%d")]
 
 
 def build(g, T, dst):
@@ -58,7 +67,7 @@ def build(g, T, dst):
     V, S, P = g.vector, g.scalar, g.tensor
 
     def op(eng, rd, wr, ns, fn, bank=None, sem=None, lat=0.0, ga=False):
-        fx = {"v": 50.0, "s": 65.0, "p": 60.0}.get(eng, ns)
+        fx = {"v": 50.0, "s": 65.0, "p": PFX}.get(eng, ns)
         ops.append({"fx": fx, "n": (ns - fx) / (PEC if eng == "p" else CYC), "ga": ga,
                     "e": eng, "r": rd, "w": wr, "ns": ns, "fn": fn, "b": bank, "sem": sem, "lat": lat, "k": stage[0], "c": crit[0]})
 
@@ -72,7 +81,7 @@ def build(g, T, dst):
         def fn():
             for (o, l, r, a, z, n) in mms: last = P.matmul(o, l, r, a, z)
             return last
-        op("p", rd, wr, 60 + sum(m[5] for m in mms) * PEC, fn, bank)
+        op("p", rd, wr, PFX + sum(m[5] for m in mms) * PEC, fn, bank)
 
     def ts(o, i, a, b, o0, o1=None):
         return (lambda: V.tensor_scalar(o, i, a, None, o0)) if o1 is None else (lambda: V.tensor_scalar(o, i, a, b, o0, o1))
@@ -85,19 +94,20 @@ def build(g, T, dst):
     def io(o, pat, b, cm): return lambda: g.iota(o, pat, b, cm, allow_small_or_imprecise_dtypes=True)
     def ioi(o, pat, b, cm): return lambda: g.iota(o, pat, b, cm)
     def sl(o, i, pat, f, b, cm): return lambda: g.affine_select(o, i, pat, f, 0.0, b, cm)
-    def put(o, x, pat, b): return lambda: g.affine_select(o, o, pat, A.not_equal, x, b, 1)
+    def put(o, x, pat, b, i=None): return lambda: g.affine_select(o, o if i is None else i, pat, A.not_equal, x, b, 1)
     def dma(q, rd, wr, o, i, sem, lat): op(q, rd, wr, 60, lambda: (g.sync if q == "y" else S).dma_start(o, i), None, sem, lat)
 
-    dma("y", [], ["ob0"], T.ob[:, 0:4, :, :], T.obs[:, 0:1024], "o0", 2500)
+    dma("y", [], ["ob0"], T.ob[:, 0:4, :, :], T.obs[:, 0:1024], "o0", 2300)
     for c in range(2):
         for h in range(4):
             dma("s" if c == 0 else "y", [], ["raw%d.%d" % (c, h)], T["raw%d" % c][:, 226 * h:226 * h + 226],
-                T.tsee[:, 226 * (2 * h + c):226 * (2 * h + c) + 226], "t%d" % c, 4000 + 3000 * c)
+                T.tsee[:, 226 * (2 * h + c):226 * (2 * h + c) + 226], "t%d" % c, 3700 + 3000 * c)
         if c == 0:
-            dma("y", [], ["ob1"], T.ob[:, 4:7, :, :], T.obs[:, 1024:1792], "o1", 3500)
-            dma("y", [], ["cv"], T.cv[:, 0:2048], T.cvec[:, :], "cv", 5500)
+            dma("y", [], ["cv"], T.cv[:, 0:2048], T.cvec[:, :], "cv", 4600)
+            dma("y", [], ["ob1"], T.ob[:, 4:7, :, :], T.obs[:, 1024:1792], "o1", 5200)
 
     def zero(o, n): return ts(o, T.ones[:, 0:n], 0.0, None, A.mult)
+    def fill(wr, o, n, x, p=128): s(["on1", "on2"], wr, n, act(o, T.ones[0:p, 0:n], F.Copy, scale=x))
     v([], ["on1"], 64, ms(T.ones[:, 0:128], 1.0))
     v([], ["on2"], 192, ms(T.ones[:, 128:512], 1.0))
     gp(["on1"], ["idb"], 128, sl(T.idb[:, :], T.ones[:, 0:128], [[-1, 128]], A.is_equal, 0, 1))
@@ -105,33 +115,47 @@ def build(g, T, dst):
     gp(["d8a"], ["d8"], 8, sl(T.d8[:, :], T.d8a[:, :], [[16, 8]], A.is_ge, 15, -1))
     v([], ["cvz"], 8, ms(T.cv[:, 2048:2064], 0.0))
     v([], ["gp%d" % ONE], 128, ms(T.gp[:, :, 16 * ONE:16 * ONE + 16], 113.0))
-    v(["idb"], ["ids"], 64, ts(T.ids[:, :], T.idb[:, :], SC, None, A.mult))
+    s(["idb"], ["ids"], 128, act(T.ids[:, :], T.idb[:, :], F.Copy, scale=SC))
     s(["idb"], ["id4"], 128, act(T.id4[:, :], T.idb[:, :], F.Copy, scale=4096.0))
-    s(["d8"], ["d8f"], 8, act(T.d8f[:, :], T.d8[:, :], F.Copy))
+    for z, (name, x) in enumerate((("d8f", 1.0), ("d8g", SC), ("d8q", 4096.0))):
+        s(["d8"], [name], 8, act(T.d8f[:, 8 * z:8 * z + 8], T.d8[:, :], F.Copy, scale=x))
     s(["d8"], ["d8s"], 8, act(T.d8s[:, :], T.d8[:, :], F.Copy, scale=SC))
+    gp(["on1"], ["dif"], 128, sl(T.dif[:, :], T.ones[:, 0:128], [[-1, 128]], A.is_equal, 0, 1))
+    gp(["dif"], ["dif"], 128, put(T.dif[:, :], -1.0, [[0, 16], [-1, 8]], -8 * ONE))
+    gp(["dif"], ["dif"], 8, put(T.dif[:, 8 * ONE:8 * ONE + 8], 0.0, [[-1, 8]], -8 * ONE))
     gp([], ["csf"], 24, io(T.csf[:, :], [[0, 6], [7232, 4]], 0, 0))
     gp(["csf"], ["csf"], 24, sl(T.csf[:, :], T.csf[:, :], [[0, 24]], A.is_equal, -8 * ONE, 1))
     gp(["csf"], ["csf"], 24, put(T.csf[:, :], 3584.0, [[0, 24]], -8 * ONE - 1))
     gp(["csf"], ["csf"], 24, put(T.csf[:, :], 1.0, [[0, 24]], -8 * ONE - 2))
     gp(["csf"], ["csf"], 24, put(T.csf[:, :], 16.0, [[-1, 24]], 0))
     v(["csf"], ["cs"], 24, ts(T.cs[:, :], T.csf[:, :], 1.0 / 256, None, A.mult))
-    v(["on1", "on2"], ["eb"], 192, zero(T.eh[:, :], 384))
+    v([], ["eb"], 64, ms(T.zr[:, :], 0.0))
+    gp(["eb"], ["csd"], 24, put(T.csd[:, 0:24], 0.0625, [[-1, 24]], 0, T.zr[:, 0:24]))
+    gp(["csd"], ["csd"], 24, put(T.csd[:, 0:24], -0.0625, [[0, 3], [-1, 8]], -8 * ONE))
+    gp([], ["cof"], 24, io(T.csd[:, 24:48], [[0, 6], [7232, 4]], 3601, 0))
+    s(["cof"], ["cof"], 24, act(T.csd[:, 24:48], T.csd[:, 24:48], F.Copy, scale=1.0 / 32))
     for e, (q, x) in enumerate(((AC, -4096.0), (AB, -SC), (BC, -SC))):
-        gp(["eb"], ["eh%d" % e], 128, put(T.eh[:, 128 * e:128 * e + 128], x, [[-1, 8], [0, 16]], -8 * q))
+        gp(["eb"], ["eh%d" % e], 128, put(T.eh[:, 128 * e:128 * e + 128], x, [[-1, 8], [0, 16]], -8 * q, T.zr[:, :]))
     v([], ["cst"], 128, ms(T.cst[0:64, :], 0.0))
-    for r0, c0, x in ((0, 0, -1800.0 * 4096), (32, 0, -1800.0), (0, 128, -3072.0), (32, 128, 3072.0 - 1800 * SC)):
+    for r0, c0, x in ((0, 0, -1800.0 * 4096), (32, 0, -1800.0), (0, 128, -3072.0), (32, 128, 9.125), (0, 256, -1800.0)):
         v([], ["cst"], 64, ms(T.cst[r0:r0 + 1, c0:c0 + 128], x))
     gp([], ["lv0"], 1, ioi(T.lv[:, 0:1], [[0, 1]], 0, 1))
     for k, (sh, an) in enumerate([(3, 1), (0, 15), (0, 7), (6, 1), (4, 3)]):
         v(["lv0"], ["pi%d" % k], 1, ts(T.pint[:, k:k + 1], T.lv[:, 0:1], sh, an, A.logical_shift_right, A.bitwise_and))
     v(["pi%d" % k for k in range(5)], ["pf"], 8, cp(T.pf[:, 0:5], T.pint[:, 0:5]))
     HI, P16, P8, KK, K4 = [T.pf[:, k:k + 1] for k in range(5)]
-    for r0, r1 in zip(CUT, CUT[1:]):
-        gp([], ["lg%d" % r0], 3 * (r1 - r0) // 2, io(T.lg[:, 3 * r0 // 2:3 * r1 // 2], [[128, 3], [2, (r1 - r0) // 2]], r0, 0))
+    runs = []
+    for u, cut in enumerate(CUTS):
+        for r0, r1 in zip(cut, cut[1:]):
+            if runs and runs[-1][0] == u and runs[-1][2] == r1 - r0: runs[-1][3] += 1
+            else: runs.append([u, r0, r1 - r0, 1])
+    for u, r0, w, n in runs:
+        j = 24 * u + 3 * r0 // 2
+        gp([], ["lg%d" % j], 3 * w * n // 2, io(T.lg[:, j:j + 3 * w * n // 2], [[w, n], [128, 3], [2, w // 2]], r0, 0))
     v(["pf"], ["pq4"], 1, ts(T.pf[:, 13:14], P8, 16.0, HI, A.mult, A.add))
-    v(["lg%d" % r0 for r0 in CUT[:-1]] + ["pq4"], ["l4"], 24, ts(T.l4[:, :], T.lg[:, :], T.pf[:, 13:14], None, A.add))
-    for x in (0, 4): v(["on1", "on2"], ["pb%d" % x], 256, zero(T.ph[:, x:x + 4, :], 512))
-    for x in range(4): v([], ["pw%d" % x], 64, ms(T.zr[0:1, x:512:4], 4096.0 * PRIO[x]))
+    v(["lg%d" % (24 * u + 3 * r0 // 2) for u, r0, w, n in runs] + ["pq4"], ["l4"], 48, ts(T.l4[:, :], T.lg[:, :], T.pf[:, 13:14], None, A.add))
+    fill(["pb0"], T.ph[:, 0:4, 88:128], 160, 0.0)
+    fill(["pb4"], T.ph[:, 4:8, 0:88], 352, 0.0)
     names = []
     for x in (0, 2):
         q = 0
@@ -139,16 +163,16 @@ def build(g, T, dst):
             a, b = SRC[x][q], SRC[x + 1][q]; n = 1
             while q + n < 16 and (SRC[x][q + n], SRC[x + 1][q + n]) == (a + n, b + n) and a + n != 16 and b + n != 16: n += 1
             u = 4 * (a // 16) + x; names.append("pb%d.%d" % (x, q))
-            gp(["pb%d" % (u & 4)], [names[-1]], 16 * n, put(T.ph[:, u:u + 2, 8 * q:8 * (q + n)], 1.0, [[8 * (a - b), 2], [-1, 8 * n]], -8 * (a % 16)))
+            gp(["on1"], [names[-1]], 16 * n, sl(T.ph[:, u:u + 2, 8 * q:8 * (q + n)], T.ones[:, 0:16 * n], [[8 * (a - b), 2], [-1, 8 * n]], A.is_equal, -8 * (a % 16), 1))
             q += n
+    names += ["pb0", "pb4"]
     v([], ["kw0"], 64, ms(T.kw0[:, :], 16384.0))
     gp(["kw0"], ["kw0"], 128, sl(T.kw0[:, :], T.kw0[:, :], [[0, 16], [-16, 8]], A.is_ge, 0, 1))
     gp(["kw0"], ["kw"], 128, sl(T.kw[:, 0:128], T.kw0[:, :], [[0, 16], [16, 8]], A.is_ge, 15, -1))
     s(["kw"], ["kn"], 128, act(T.kw[:, 128:256], T.kw[:, 0:128], F.Copy, scale=-1.0))
     s(["kw"], ["kf"], 128, act(T.kw[:, 256:384], T.kw[:, 0:128], F.Copy, scale=32.0))
     s(["idb"], ["id8"], 128, act(T.kw[:, 384:512], T.idb[:, :], F.Copy, scale=8192.0))
-    v([], ["rst"], 256, ms(T.rst[:, :], 0.0))
-    v([], ["rst"], 64, ms(T.rst[:, 0:512:4], -2.0 ** 40))
+    for x in range(4): fill(["rst%d" % x], T.rst[:, x:512:4], 128, 4096.0 * (PRIO[x - 1] - PRIO[x]) if x else -2.0 ** 40)
     v([], ["ge0"], 16, ms(T.geo[:, 0:16], 2.0 ** -9))
     v([], ["ge1"], 16, ms(T.geo[:, 16:32], 0.0))
     v(["ge0", "ge1"], ["ge2"], 16, scan(T.geo[:, 32:48], T.geo[:, 0:16], T.geo[:, 16:32], 2.0 ** 57, A.mult, A.add))
@@ -156,28 +180,27 @@ def build(g, T, dst):
     v(["lf0", "pf"], ["lf1"], 16, ts(T.lf[:, 16:32], T.lf[:, 0:16], P16, None, A.is_equal))
     v(["lf1", "ge2"], ["ge3"], 32, tt(T.geo[:, 48:64], T.lf[:, 16:32], T.geo[:, 32:48], A.mult))
     v(["ge3"], ["wp"], 16, lambda: V.tensor_reduce(T.pf[:, 8:9], T.geo[:, 48:64], AxisListType.X, A.add))
-    v(["wp", "d8"], ["cw"], 8, ts(T.cw[:, :], T.d8[:, :], T.pf[:, 8:9], None, A.mult))
-    for u in range(4):
-        gp(["on1", "on2"], ["bcm%d" % u], 512, sl(T.bcm[:, 512 * u:512 * u + 512], T.ones[:, 0:512], [[-1, 4], [-16, 8], [0, 16]], A.is_equal, -4 * u, 1))
+    v(["wp"], ["wn"], 1, ts(T.pf[:, 9:10], T.pf[:, 8:9], -1.0, None, A.mult))
+    gp([], ["off"], 128, io(T.cw[:, 128:256], [[0, 8], [1, 16]], 0, 0))
+    v(["off", "pf"], ["off"], 64, ts(T.cw[:, 128:256], T.cw[:, 128:256], P16, -2.0 ** 60, A.not_equal, A.mult))
     v(["on1"], ["eo"], 8, zero(T.eo[:, :], 32))
     v(["d8"], ["eo"], 8, cp(T.eo[:, 2:26:3], T.d8[:, :]))
     for m in range(3):
         s(["d8"], ["eo3.%d" % m], 8, act(T.eo3[:, m:24:3], T.d8[:, :], F.Copy, scale=1.0 / 2048))
     gp([], ["binw"], 904, io(T.binw[:, 0:904], [[0, 4], [1, 226]], 0, 0))
-    v(["on1", "on2"], ["t1"], 128, zero(T.t1[:, :], 256))
     for kk in range(2):
-        gp(["t1"], ["t1"], 128, put(T.t1[:, 128 * kk:128 * kk + 128], 1.0, [[0, 2], [-1, 4], [0, 16]], -8 * OA - 4 * kk))
-    gp(["t1"], ["t1"], 256, put(T.t1[:, :], 224.0, [[0, 256]], -8 * ONE))
+        gp(["on1"], ["t1"], 128, sl(T.t1[:, 128 * kk:128 * kk + 128], T.ones[:, 0:128], [[0, 2], [-1, 4], [0, 16]], A.is_equal, -8 * OA - 4 * kk, 1))
+    gp(["t1"], ["t1"], 256, put(T.t1[:, :], 224.0 - 288.0, [[0, 256]], -8 * ONE))
     gp(["t1"], ["t1"], 256, put(T.t1[:, :], 0.0625, [[0, 256]], -8 * ONE - 1))
     v([], ["rg0"], 64, ms(T.rg0[:, :], -1.0))
     gp(["rg0"], ["rg0"], 128, sl(T.rg0[:, :], T.rg0[:, :], [[-16, 8], [0, 16]], A.is_ge, 0, 1))
     gp(["rg0"], ["rg"], 128, sl(T.rg[:, :], T.rg0[:, :], [[16, 8], [0, 16]], A.is_ge, 15, -1))
     s(["rg"], ["rg2"], 128, act(T.rg2[:, :], T.rg[:, :], F.Copy, scale=2.0))
+    s(["rg", "wn"], ["cw"], 128, act(T.cw[:, 0:128], T.rg[:, :], F.Copy, scale=T.pf[:, 9:10]))
     gp([], ["mk0"], 256, io(T.mk0[:, :], [[-1, 2], [0, 8], [-2, 16]], 0, 0))
     v(["pf"], ["pq2"], 1, ts(T.pf[:, 12:13], P16, 2.0, KK, A.mult, A.add))
-    v(["mk0", "pq2"], ["mk1"], 128, ts(T.mk1[:, :], T.mk0[:, :], T.pf[:, 12:13], 8192.0, A.add, A.mult))
-    v(["mk1"], ["mk2"], 128, ts(T.mk2[:, :], T.mk1[:, :], -1.0, 4096.0, A.mult, A.min))
-    v(["mk1", "mk2"], ["mk"], 256, tt(T.mk[:, :], T.mk1[:, :], T.mk2[:, :], A.max))
+    s(["mk0", "pq2"], ["mk1"], 256, act(T.mk1[:, :], T.mk0[:, :], F.Sign, bias=T.pf[:, 12:13]))
+    s(["mk1"], ["mk"], 256, act(T.mk[:, :], T.mk1[:, :], F.Square, scale=128.0, bias=48.0))
     v(["lf0", "pf"], ["h4"], 4, ts(T.h4[:, 0:4], T.lf[:, 0:4], K4, 4096.0, A.is_equal, A.mult))
     gp([], ["du0"], 8, io(T.dum[:, 8:16], [[16, 8]], 904, 0))
     v(["du0", "pf"], ["dum"], 8, ts(T.dum[:, 0:8], T.dum[:, 8:16], P16, None, A.add))
@@ -191,18 +214,38 @@ def build(g, T, dst):
                 u = "up%d" % c; m = 8 * (q1 - q0)
                 pe(["d8"] + ["gp%d" % z for z in range(q0, q1)], [u], [(T[u][0:m, c0 + r:c0 + 128:16], T.gp[:, r, 16 * q0 + c:16 * q1:2], T.d8[:, :], True, True, 64) for r in range(16)], u)
                 o = T["gb%d" % c][0:m, :] if q0 == 16 else T["gm%d" % c][p0:m, 0, :]
-                v([u], [name + str(c)], 128, ts(o, T[u][p0:m, c0:c0 + 128], -1800.0, None, A.add), u)
+                if EVS and name + str(c) in ("go0", "go1", "ga0", "ga1")[:EVS]: s([u], [name + str(c)], 128, act(o, T[u][p0:m, c0:c0 + 128], F.Copy, bias=-1800.0), u)
+                else: v([u], [name + str(c)], 128, ts(o, T[u][p0:m, c0:c0 + 128], -1800.0, None, A.add), u)
     gram(0, 3, [(0, 4, 0, 0, "go")])
     gram(3, 7, [(0, 8, 32, 128, "ga")])
     for c in range(2):
-        v([], ["tab%d" % c], 128, ms(T["tab%d" % c][:, 904:1032], 0.0))
+        gp([], ["tab%d" % c], 128, io(T["tab%d" % c][:, 904:1032], [[0, 128]], 0, 0))
         for h in range(4):
             gp(["raw%d.%d" % (c, z) for z in range(4)], ["tad%d.%d" % (c, h)], 226, sl(T["tab%d" % c][:, 226 * h:226 * h + 226], T["raw%d" % c][:, 226 * h:226 * h + 226], [[0, 226]], A.is_ge, 0, 0))
-    late = [lambda: gram(7, len(PAIRS), [(0, 16, 64, 128, "gc"), (16, 22, 0, 256, "gb")])]
+    sums = {4: ("rp1", "ra1", 0), 5: ("rp1", "rc1", 256), 1: ("mp1", "ma1", 0)} if PACK else {}
+    for w, (u, name, c0) in sums.items():
+        o = T[u][:, c0:c0 + 256]
+        pe(["ob0", "ob1", "idb", "id4"], [name], [(o, T.idb[:, :], T.ob[:, w, :, :], True, False, 256), (o, T.id4[:, :], T.ob[:, 6, :, :], False, True, 256)], u)
+    for q, (j, w) in enumerate(TWICE if PACK else []):
+        u, name, c0 = sums[w]
+        v(["ob0", "ob1", name], ["gq%d" % q], 256, tt(T.gq[:, 1:17, 16 * q:16 * q + 16], T.ob[:, j, :, :], T[u][:, c0:c0 + 256], A.mult), u)
+    if PACK: fill(["gq"], T.gq[:, 0, :], 128, 0.0)
+
+    def apart():
+        for c in range(2):
+            u = nextu(); x = T[u][64:128, 0:128]; y = T["yy%d" % c][64:128, :]
+            fill(["gz%d" % c], T["gb%d" % c][0:64, :], 128, 0.0, 64)
+            pe(["cst", "on1"], [u], [(T[u][:, 0:128], T.ones[0:1, 0:128], T.cst[0:1, 256:384], True, False, 128)], u)
+            for r0 in range(0, 16, 4):
+                pe(["d8f", "gq"] + ["gq%d" % q for q in range(8)], [u], [(T[u][:, r:128:16], T.gq[:, r:r + 2, c:128:2], T.d8f[:, 0:8], False, r == 15, 256) for r in range(r0, r0 + 4)], u)
+            v([u], ["yy%d" % c], 128, ts(y, x, 1.5 * 2.0 ** 35, -1.5 * 2.0 ** 35, A.add, A.add), u)
+            v([u, "yy%d" % c], ["gc%d" % c], 128, tt(T["gm%d" % c][64:128, 0, :], x, y, A.subtract), u)
+            v(["yy%d" % c, "gz%d" % c], ["gb%d" % c], 128, ts(T["gb%d" % c][64:128, :], y, 1.0 / 4096, -1800.0, A.mult, A.add))
+    late = [apart if PACK else lambda: gram(7, len(PAIRS), [(0, 16, 64, 128, "gc"), (16, 22, 0, 256, "gb")])]
 
     ubank = [0]
     def nextu():
-        ubank[0] = 1 - ubank[0]
+        ubank[0] = (ubank[0] + 1) % NU
         return "up%d" % ubank[0]
 
     def out(t, c):
@@ -227,42 +270,54 @@ def build(g, T, dst):
             g3, g6 = ([k("go")], [k("go"), k("ga")]) if t == 0 else (["g%d%d" % (c, t)],) * 2
             rp, mp = b("rp"), b("mp")
             stage[0] = 2 * t + c - EARLY; crit[0] = 1
-            pe(g3 + ["cs"], [k("md"), k("mg")], [(mp[:, 384:408], G3, T.cs[0:32, :], True, True, 64)], k("mp"))
-            v([k("md")], [k("cl")], 24, ts(b("cl")[:, :], mp[:, 384:408], M, -M, A.add, A.add), k("mp"))
+            cl = "cl%d%d" % (c, t)
+            if t == 0:
+                pe(g3 + ["cs"], [k("md"), k("mg")], [(mp[:, 384:408], G3, T.cs[0:32, :], True, True, 64)], k("mp"))
+                v([k("md")], [cl], 24, ts(b("cl")[:, 0, :], mp[:, 384:408], M, -M, A.add, A.add), k("mp"))
             table, tn = (b("raw")[:, :], ["raw%d.%d" % (c, h) for h in range(4)]) if t == 0 else (b("tab")[:, 0:904], [k("tab")])
-            sg([k("cl")] + tn, [k("nf")], 384, act(b("nf")[:, :], table.indirect(b("cl")[:, :]), F.Copy))
-            for n0, n1 in SPLIT:
-                j0, j1 = 24 * CUT[n0], 24 * CUT[n1]
-                vg([k("nf"), "l4"], [k("nu%d" % n) for n in range(n0, n1)], j1 - j0, cp(b("nu")[:, j0:j1], b("nf")[:, :].indirect(T.l4[:, j0 // 16:j1 // 16])))
+            sg([cl] + tn, [k("nf"), k("ng")], 384, act(b("nf")[:, :], table.indirect(b("cl")[:, t, :]), F.Copy))
+            u = int(last and c == 1); cut = CUTS[u]
+            for n0, n1, e in [(n0, min(n1, len(cut) - 1), e) for n0, n1, e in NUS]:
+                j0, j1 = 24 * cut[n0], 24 * cut[n1]; src = b("nf")[:, :].indirect(T.l4[:, 24 * u + j0 // 16:24 * u + j1 // 16])
+                (vg if e == "v" else sg)([k("nf"), k("ng"), "l4"], [k("nu%d" % n) for n in range(n0, n1)], j1 - j0, cp(b("nu")[:, j0:j1], src) if e == "v" else act(b("nu")[:, j0:j1], src, F.Copy))
             crit[0] = 0
             if not last:
-                sg([k("cl"), "binw"], [k("bh")], 128, act(b("bh")[:, :], T.binw[:, 0:904].indirect(b("cl")[:, 16:24]), F.Copy))
+                sg([cl, "binw"], [k("bh")], 128, act(b("bh")[:, :], T.binw[:, 0:904].indirect(b("cl")[:, t, 16:24]), F.Copy))
             stage[0] = 2 * t + c
             if t: out(t - 1, c)
             R1, R0 = rp[:, 0:128], mp[:, 0:128]
             pe(g6 + ["cst", "on1", "eh0"], [k("ra"), k("rg")], [(R1, T.ones[0:64, 0:128], T.cst[0:64, 0:128], True, False, 128), (R1, T.eh[0:64, 0:128], G6, False, False, 128)], k("rp"))
             pe(g6 + ["cst", "on1", "eh2"], [k("ma"), k("mg")], [(R0, T.ones[0:64, 0:128], T.cst[0:64, 128:256], True, False, 128), (R0, T.eh[0:64, 256:384], G6, False, False, 128)], k("mp"))
-            NB = len(CUT) - 1
+            NB = len(cut) - 1; wait = []
             for n in range(NB):
-                R = range(CUT[n], CUT[n + 1]); E = 128 * len(R); e0 = 128 * CUT[n]; cs = slice(e0, e0 + E); x = "%d.%d" % (c, n); end = n == NB - 1
+                R = range(cut[n], cut[n + 1]); E = 128 * len(R); e0 = 128 * cut[n]; cs = slice(e0, e0 + E); x = "%d.%d" % (c, n); end = n == NB - 1
                 def gat(m0, m1): return win.indirect(b("nu")[:, (3 * e0 + E * m0) // 16:(3 * e0 + E * m1) // 16])
-                def vv(m0, m1, z=0, w=None): return b("vv")[:, 3 * e0 + E * m0 + z:3 * e0 + (E * m1 if w is None else E * m0 + z + w)]
+                def vv(m0, m1, z=0, w=None): return b("vv")[:, e0 // 512, 3 * (e0 % 512) + E * m0 + z:3 * (e0 % 512) + (E * m1 if w is None else E * m0 + z + w)]
                 cvr = ["cv", "cvz", k("nu%d" % n)]; mix = MIX[t][c][n]
-                if mix == 2: sg(cvr, ["vb" + x, "va" + x], 3 * E, act(vv(0, 3), gat(0, 3), F.Copy))
+                if mix == 4:
+                    X = b("xx")[:, cs]; ub = nextu()
+                    sg(cvr, ["vb" + x], E, act(vv(0, 1), gat(0, 1), F.Copy, scale=1.0 / 4096))
+                    vg(cvr + ["vb" + x], ["xx" + x], E, tt(X, gat(1, 2), vv(0, 1), A.add))
+                    pe(["vb" + x, "id4"], [ub], [(T[ub][:, 0:E], T.id4[:, :], vv(0, 1), True, True, E)], ub)
+                    v(["xx" + x, ub], ["p0" + x], E, tt(b("px")[:, cs], X, T[ub][:, 0:E], A.mult), ub)
+                    vg(cvr + ["xx" + x], ["p1" + x], E, tt(b("pw")[:, cs], gat(2, 3), X, A.mult))
+                elif mix == 2: sg(cvr, ["vb" + x, "va" + x], 3 * E, act(vv(0, 3), gat(0, 3), F.Copy))
                 else:
                     sg(cvr, ["vb" + x], 2 * E, act(vv(0, 2), gat(0, 2), F.Copy))
                     if mix: vg(cvr, ["va" + x], E, cp(vv(2, 3), gat(2, 3)))
                     else: sg(cvr, ["va" + x], E, act(vv(2, 3), gat(2, 3), F.Copy))
-                ub = nextu(); mm = []
-                for z in range(0, E, 512):
-                    w = min(512, E - z)
-                    mm += [(T[ub][:, z:z + w], T.idb[:, :], vv(0, 1, z, w), True, False, w), (T[ub][:, z:z + w], T.id4[:, :], vv(1, 2, z, w), False, True, w)]
-                pe(["vb" + x, "idb", "id4"], [ub], mm, ub)
-                v(["vb" + x], ["p0" + x], E, tt(b("pr")[:, cs], vv(0, 1), vv(1, 2), A.mult))
-                v(["va" + x, ub], ["p1" + x], E, tt(b("pw")[:, cs], vv(2, 3), T[ub][:, 0:E], A.mult), ub)
-                pe(["p0" + x, "d8s", k("mg")], [k("ma"), k("mg")] if end else ["r0" + x], [(mp[:, r:128:16], b("pr")[:, 128 * r:128 * r + 128], T.d8s[:, :], False, r == 15, 64) for r in R], k("mp"))
-                pe(["p1" + x, "d8f", k("rg")], [k("ra"), k("rg")] if end else ["r1" + x], [(rp[:, r:128:16], b("pw")[:, 128 * r:128 * r + 128], T.d8f[:, :], False, r == 15, 256) for r in R], k("rp"))
-                if late: late.pop()()
+                if mix < 3:
+                    ub = nextu(); mm = []
+                    for z in range(0, E, 512):
+                        w = min(512, E - z)
+                        mm += [(T[ub][:, z:z + w], T.idb[:, :], vv(0, 1, z, w), True, False, w), (T[ub][:, z:z + w], T.id4[:, :], vv(1, 2, z, w), False, True, w)]
+                    pe(["vb" + x, "idb", "id4"], [ub], mm, ub)
+                    v(["vb" + x], ["p0" + x], E, tt(b("pr")[:, cs], vv(0, 1), vv(1, 2), A.mult))
+                    v(["va" + x, ub], ["p1" + x], E, tt(b("pw")[:, cs], vv(2, 3), T[ub][:, 0:E], A.mult), ub)
+                p0, w0, n0, w1 = (b("px"), T.d8f[:, 8:16], 256, T.d8f[:, 16:24]) if mix == 4 else (b("pr"), T.d8s[:, :], 64, T.d8f[:, 0:8])
+                pe(["p0" + x, k("mg"), "d8s", "d8g"], [k("ma"), k("mg")] if end else ["r0" + x], [(mp[:, r:128:16], p0[:, 128 * r:128 * r + 128], w0, False, r == 15, n0) for r in R], k("mp"))
+                pe(["p1" + x, k("rg"), "d8f", "d8q"], [k("ra"), k("rg")] if end else ["r1" + x], [(rp[:, r:128:16], b("pw")[:, 128 * r:128 * r + 128], w1, False, r == 15, 256) for r in R], k("rp"))
+                if late and n == LATE: late.pop()()
             crit[0] = 1
             H = [b("hf")[:, 128 * e:128 * e + 128] for e in range(4)]; EV = H[3]
             v([k("ma")], [k("h0")], 128, ts(H[0], R0, 1.5 * 2.0 ** 32, 1.5 * 2.0 ** 32, A.add, A.not_equal), k("mp"))
@@ -275,50 +330,54 @@ def build(g, T, dst):
             if not TWO: v([k("ac")], [k("h1")], 64, ts(H[1], b("ab")[:, :], 150.0, None, A.is_gt))
             NAC = [H[1], b("ab")[:, :]][:1 + TWO]; nac = [k("h1"), k("h2")][:1 + TWO]
             Ra, Re = mp[:, 128:256], mp[:, 256:384]
-            pe(g6 + [k("h0"), "eh1", "id8", "on1", "on2", "cst"], [k("mb"), k("mc"), k("mg")],
-               [(mp[:, 128:384], T.cst[0:1, 256:384], T.ones[0:1, 0:256], True, False, 256), (Ra, T.eh[0:64, 128:256], G6, False, False, 128), (Re, T.eh[0:64, 128:256], G6, False, False, 128),
-                (Re, T.kw[:, 384:512], H[0], False, False, 128)], k("mp"))
-            pe([k("lo"), "ids", "id8"] + nac, [k("mb"), k("mc"), k("mg")], [(Re, T.kw[:, 384:512], z, False, False, 128) for z in NAC] +
-               [(Ra, T.ids[:, :], b("lo")[:, :], False, False, 128), (Re, T.ids[:, :], b("lo")[:, :], False, True, 128)], k("mp"))
-            v([k("mb"), k("mc")], [k("ev")], 256, ts(b("hf")[:, 256:512], mp[:, 128:384], 1.5 * 2.0 ** 32, 1.5 * 2.0 ** 32, A.add, A.is_equal), k("mp"))
+            pe(g6 + [k("h0"), "eh1", "id8"], [k("mc"), k("mg")], [(Re, T.eh[0:64, 128:256], G6, True, False, 128), (Re, T.kw[:, 384:512], H[0], False, False, 128)], k("mp"))
+            pe(nac + ["id8"], [k("mc"), k("mg")], [(Re, T.kw[:, 384:512], z, False, False, 128) for z in NAC], k("mp"))
+            pe(g6 + [k("lo"), "ids"], [k("mb"), k("mc"), k("mg")], [(Re, T.ids[:, :], b("lo")[:, :], False, True, 128)] +
+               ([] if last else [(Ra, T.eh[0:64, 128:256], G6, True, False, 128), (Ra, T.ids[:, :], b("lo")[:, :], False, True, 128)]), k("mp"))
+            z = 128 * last
+            v([k("mb"), k("mc")], [k("ev")], 256 - z, ts(b("hf")[:, 256 + z:512], mp[:, 128 + z:384], 1.5 * 2.0 ** 32, 1.5 * 2.0 ** 32, A.add, A.is_equal), k("mp"))
             whole = [k("ra"), k("rb"), k("rc")]
             if not last:
-                mm = [(rp[:, :], T.ones[0:1, 0:128], T.zr[0:1, :], True, False, 512)]
-                for x in range(4):
-                    mm.append((rp[:, x:512:4], T.ph[:, x, :], GA, False, False, 128))
-                    if t == 0: mm.append((rp[:, x:512:4], T.ph[0:48, 4 + x, :], b("gb")[0:48, :], False, False, 128))
-                pe(g6 + names + ["pw0", "pw1", "pw2", "pw3", "on1"] + ([k("gb"), k("gc")] if t == 0 else []), whole + [k("rg")], mm, k("rp"))
-                pe([k("h0"), "kn"] + nac, whole + [k("rg")], [(rp[:, x:512:4], T.kw[:, 128:256], z, False, False, 128) for x, z in [(1, H[0])] + [(2, z) for z in NAC]], k("rp"))
-                pe([k("ev"), "kw", "kf"], whole + [k("rg")], [(rp[:, 3:512:4], T.kw[:, 0:128], H[2], False, False, 128), (rp[:, 0:512:4], T.kw[:, 256:384], EV, False, True, 128)], k("rp"))
-                v(whole + ["rst"], [k("xs")], 512, scan(b("xs")[:, :], T.rst[:, :], rp[:, :], 0.0, A.add, A.max), k("rp"))
-                v([k("xs")], [k("ra")], 128, ts(R1, b("xs")[:, 3:512:4], 1.5 * 2.0 ** 35, -1.5 * 2.0 ** 35, A.add, A.add), k("rp"))
-                v([k("xs"), k("ra")], ["nx%d%d" % (c, t)], 128, tt(b("nx")[:, t, :], b("xs")[:, 3:512:4], R1, A.subtract), k("rp"))
+                def val(x): return [(rp[:, x:512:4], T.ph[:, x, :], GA, True, False, 128)] + [(rp[:, x:512:4], T.ph[0:48 + 80 * PACK, 4 + x, :], b("gb")[0:48 + 80 * PACK, :], False, False, 128)] * (t == 0)
+                def cnt(x, w, zs): return [(rp[:, x:512:4], T.kw[:, 128 * w:128 * w + 128], z, False, z is zs[-1], 128) for z in zs]
+                gall = g6 + names + ([k("gb"), k("gc")] if t == 0 else [])
+                pe(gall + [k("h0"), "kn"], whole + [k("rg")], val(1) + cnt(1, 1, [H[0]]), k("rp"))
+                pe(gall + nac + ["kn"], whole + [k("rg")], val(2) + cnt(2, 1, NAC) + val(3), k("rp"))
+                pe(gall + [k("ev"), "kw", "kf"], whole + [k("rg")], cnt(3, 0, [H[2]]) + val(0) + cnt(0, 2, [EV]), k("rp"))
+                v(whole + ["rst0", "rst1", "rst2", "rst3"], [k("xs")], 512, scan(b("xs")[:, :], T.rst[:, :], rp[:, :], 0.0, A.add, A.max), k("rp"))
+                pe([k("xs"), "csd"], [k("rb"), k("rg")], [(rp[:, 128:152], b("xs")[:, 3:512:4], T.csd[:, 0:24], True, True, 256)], k("rp"))
+                v([k("rb"), "cof"], ["cx%d%d" % (c, t)], 24, tt(b("cx")[:, t, :], rp[:, 128:152], T.csd[:, 24:48], A.add), k("rp"))
+                pe([k("xs"), "dif"], [k("ra"), k("rg")], [(R1, T.dif[:, :], b("xs")[:, 3:512:4], True, True, 512)], k("rp"))
+                op("g", ["cx%d%d" % (c, t)], ["cl%d%d" % (c, t + 1)], 500,
+                   (lambda o, i, a: lambda: g.remote_dma(o, i, T.sem[a], T.sem.sent, dst[1], dst[0], dst[2]))(b("cl")[:, t + 1, :], b("cx")[:, t, :], "ac%d%d" % (t + 1, c)),
+                   None, "ac%d%d" % (t + 1, c), RLAT)
+                if NXV: v([k("ra")], ["nx%d%d" % (c, t)], 128, ts(b("nx")[:, t, :], R1, 8.0, None, A.add), k("rp"))
+                else: s([k("ra")], ["nx%d%d" % (c, t)], 128, act(b("nx")[:, t, :], R1, F.Copy, bias=8.0), k("rp"))
                 an = "a%d%d" % (t + 1, c)
                 op("g", ["nx%d%d" % (c, t)], ["g%d%d" % (c, t + 1)], 500,
                    (lambda o, i, a: lambda: g.remote_dma(o, i, T.sem[a], T.sem.sent, dst[1], dst[0], dst[2]))(b("gm")[:, t + 1, :], b("nx")[:, t, :], an),
                    None, an, RLAT)
                 crit[0] = 0
-            pe([k("ev"), "cw"], [k("me"), k("mg")], [(mp[:, 408:416], EV, T.cw[:, :], True, True, 64)], k("mp"))
-            if last: v([k("me")], [k("cd")], 8, cp(b("cd")[:, :], mp[:, 408:416]), k("mp"))
-            else: s([k("me")], [k("cd")], 8, act(b("cd")[:, :], mp[:, 408:416], F.Copy), k("mp"))
-            pe([k("cd")] + ["bcm%d" % u for u in range(4)], [k("mc"), k("mg")], [(mp[:, 256 + r:384:16], T.bcm[:, 128 * r:128 * r + 128], b("cd")[:, :], True, True, 64) for r in range(16)], k("mp"))
-            v([k("mc"), "wp"], [k("ohb")], 128, ts(b("ohb")[:, :], mp[:, 256:384], T.pf[:, 8:9], 2048.0, A.is_equal, A.mult), k("mp"))
+            pe([k("ev"), "cw", "idb", "off"], [k("mb"), k("mg")], [(Ra, T.idb[:, :], T.cw[:, 128:256], True, False, 128), (Ra, EV, T.cw[:, 0:128], False, True, 128)], k("mp"))
+            if CDV or last: v([k("mb")], [k("cd")], 128, ts(b("cd")[:, :], Ra, 0.0, None, A.max), k("mp"))
+            else: s([k("mb")], [k("cd")], 128, act(b("cd")[:, :], Ra, F.Relu), k("mp"))
+            pe([k("cd"), "rg"], [k("mc"), k("mg")], [(Re, T.rg[:, :], b("cd")[:, :], True, True, 128)], k("mp"))
+            v([k("mc"), "wn"], [k("ohb")], 128, ts(b("ohb")[:, :], Re, T.pf[:, 9:10], 2048.0, A.is_equal, A.mult), k("mp"))
             if not last:
                 gp([k("ohb")], [k("ohf")], 128, sl(b("ohf")[:, :], b("ohb")[:, :], [[0, 128]], A.is_ge, 0, 0))
-                mm = []
+                ub = nextu(); up = T[ub]; mm = [(up[:, 0:256], T.idb[:, :], T.mk[:, :], True, False, 256)]
                 for kk in range(2):
-                    o = rp[:, 128 * kk:128 * kk + 128]
-                    mm += [(o, T.t1[0:32, 128 * kk:128 * kk + 128], G3, True, False, 128), (o, b("bh")[:, :], T.rg[:, :], False, False, 128),
-                           (o, T.idb[:, :], T.mk[:, 128 * kk:128 * kk + 128], False, False, 128), (o, b("ohb")[:, :], T.rg2[:, :], False, True, 128)]
-                pe(g6 + [k("bh"), k("ohb"), "t1", "rg", "rg2", "mk", "idb"], [k("ra"), k("rb"), k("rg")], mm, k("rp"))
-                v([k("ra"), k("rb")], [k("fl")], 256, ts(b("fl")[:, :], rp[:, 0:256], 1.5 * 2.0 ** 27, 1.5 * 2.0 ** 27, A.add, A.is_equal), k("rp"))
+                    o = up[:, 128 * kk:128 * kk + 128]
+                    mm += [(o, T.t1[0:32, 128 * kk:128 * kk + 128], G3, False, False, 128), (o, b("bh")[:, :], T.rg[:, :], False, False, 128)]
+                pe(g6 + [k("bh"), k("lo"), "t1", "rg", "mk", "idb"], [ub], mm, ub)
+                pe([k("ohb"), "rg2"], [ub], [(up[:, 128 * kk:128 * kk + 128], b("ohb")[:, :], T.rg2[:, :], False, kk == 1, 128) for kk in range(2)], ub)
+                v([ub], [k("fl")], 256, ts(b("fl")[:, :], up[:, 0:256], 1.5 * 2.0 ** 27, 1.5 * 2.0 ** 27, A.add, A.is_equal), ub)
                 pe(g6 + [k("fl"), "cs", "h4"], [k("mf"), k("mg")], [(mp[:, 416:424], G3, T.cs[0:32, 16:24], True, False, 64)] +
                    [(mp[:, 416 + 4 * kk:420 + 4 * kk], b("fl")[:, 128 * kk:128 * kk + 128], T.h4[:, 0:4], False, kk == 1, 64) for kk in range(2)], k("mp"))
-                v([k("mf"), "dum"], [k("so")], 8, tt(b("so")[:, :], mp[:, 416:424], T.dum[:, 0:8], A.min), k("mp"))
-                v([k("so")], [k("su")], 8, ts(b("su")[:, :], b("so")[:, :], M, -M, A.add, A.add))
+                v([k("mf"), "dum"], [k("su")], 8, tt(b("su")[:, :], mp[:, 416:424], T.dum[:, 0:8], A.min), k("mp"))
                 v([k("su"), k("nf"), k("ohf")] + [k("tad") + ".%d" % h for h in range(4)], [k("tab")], 128 * 3.8, tt(b("tab")[:, :].indirect(b("su")[:, :]), b("nf")[:, 256:384], b("ohf")[:, :], A.max))
             pe([k("ohb"), "idb"], whole + [k("rg")], [(rp[:, 128 * e:128 * e + 128], T.idb[:, :], b("ohb")[:, :], True, True, 128) for e in range(3)], k("rp"))
-            v(whole + [k("nf")], [k("sel")], 384, tt(b("sel")[:, :], b("nf")[:, :], rp[:, 0:384], A.min), k("rp"))
+            v(whole + [k("nf"), k("ng")], [k("sel")], 384, tt(b("sel")[:, :], b("nf")[:, :], rp[:, 0:384], A.min), k("rp"))
             if last: out(t, c)
     return ops
 
@@ -387,8 +446,8 @@ def justify(ops, seq, succ, rounds):
     return best[1], best[0]
 
 
-CASES = [(1.56, 1.0, 200.0, 1.05), (1.2, 0.9, 200.0, 1.3), (1.95, 0.7, 200.0, 1.3)]
-STEPS, HEAT = 40000, 100.0
+CASES = [(1.56, 1.0, 135.0, 1.0), (1.12, 1.0, 120.0, 1.1), (1.95, 0.5, 150.0, 1.3), (1.3, 0.5, 190.0, 1.2)]
+STEPS, HEAT = 60000, 80.0
 KEPT = {}
 
 
@@ -397,18 +456,28 @@ def polish(ops, seq, succ, steps):
     dep = [[(j, not (o["e"] == "p" and ops[j]["e"] == "p")) for j in o["d"]] for o in ops]
     cost = [[f * (o["fx"] + (o["ns"] - o["fx"]) * (gm / GAM if o["ga"] else 1.0)) for o in ops] for gm, pc, hop, f in CASES]
 
-    def span(sq):
-        tot = 0.0
-        for ns, (gm, pc, hop, f) in zip(cost, CASES):
-            free = [0.0] * 5; fin = [0.0] * n
-            for i in sq:
-                st = free[eng[i]]
-                for j, h in dep[i]:
-                    x = fin[j] + hop if h else fin[j]
-                    if x > st: st = x
-                st += ns[i]; free[eng[i]] = st; fin[i] = st + lat[i]
-            tot += pc * (max(fin) + 0.02 * sum(fin) / n)
-        return tot / len(CASES)
+    above = []
+    for i, o in enumerate(ops):
+        far = 0
+        for j in o["d"]: far |= above[j]
+        dep[i] = [(j, h) for j, h in dep[i] if not far >> j & 1]
+        for j in o["d"]: far |= 1 << j
+        above.append(far)
+    step = [[(eng[i], [(j, hop if h else 0.0) for j, h in dep[i]], ns[i], 10.0 * hop + 1200.0 if eng[i] == 3 and lat[i] else lat[i]) for i in range(n)] for ns, (gm, pc, hop, f) in zip(cost, CASES)]
+
+    def span(sq, old=None, a=0):
+        tot = 0.0; new = []; a = a // 32 if old else 0
+        for x, (gm, pc, hop, f) in enumerate(CASES):
+            fin = old[x][0][:] if old else [0.0] * n; marks = old[x][1][:a + 1] if old else [[0.0] * 5]; free = marks[a][:]; sx = step[x]
+            for p in range(32 * a, n, 32):
+                for i in sq[p:p + 32]:
+                    e, dp, ns, lt = sx[i]; st = free[e]
+                    for j, h in dp:
+                        if fin[j] + h > st: st = fin[j] + h
+                    st += ns; free[e] = st; fin[i] = st + lt
+                marks.append(free[:])
+            tot += pc * (max(fin) + 0.02 * sum(fin) / n); new.append((fin, marks))
+        return tot / len(CASES), new
 
     def held(sq, case):
         ns = cost[case]; hop = CASES[case][2]; free = [0.0] * 5; prev = [None] * 5; fin = [0.0] * n; why = [None] * n
@@ -417,7 +486,7 @@ def polish(ops, seq, succ, steps):
             for j, h in dep[i]:
                 x = fin[j] + hop if h else fin[j]
                 if x >= st: st = x; y = (j, False)
-            st += ns[i]; free[e] = st; fin[i] = st + lat[i]; why[i] = y; prev[e] = i
+            st += ns[i]; free[e] = st; fin[i] = st + step[case][i][3]; why[i] = y; prev[e] = i
         i = max(range(n), key=lambda z: fin[z]); out = []
         while why[i][0] is not None:
             if why[i][1] and eng[i] < 4: out.append((why[i][0], i))
@@ -432,13 +501,13 @@ def polish(ops, seq, succ, steps):
                 need |= ops[i]["d"]; engs.add(eng[i]); first.append(i)
             else: rest.append(i)
         return sq[:a] + first[::-1] + rest[::-1] + sq[z + 1:]
-    cur = best = span(seq); top = seq; r = 12345; pairs = None
+    cur, kept = span(seq); best = cur; top = seq; r = 12345; pairs = None
     for it in range(steps):
         r = (r * 1103515245 + 12345) % 2147483648
         if (r >> 8) % 4:
             if pairs is None: pairs = held(seq, (r >> 12) % len(CASES))
             if not pairs: pairs = None; continue
-            sq = ahead(seq, *pairs.pop((r >> 14) % len(pairs)))
+            u, w = pairs.pop((r >> 14) % len(pairs)); sq = ahead(seq, u, w); a = seq.index(u)
             if sq is None: continue
         else:
             r = (r * 1103515245 + 12345) % 2147483648; a = (r >> 8) % n; i = seq[a]
@@ -450,10 +519,10 @@ def polish(ops, seq, succ, steps):
                 if seq[p] in near: break
                 if eng[seq[p]] == eng[i]: to = p; hops -= 1
             if to is None: continue
-            sq = seq[:a] + seq[a + 1:]; sq.insert(to, i)
-        x = span(sq)
+            sq = seq[:a] + seq[a + 1:]; sq.insert(to, i); a = min(a, to)
+        x, new = span(sq, kept, a)
         if x <= cur + HEAT * (1.0 - it / steps):
-            cur, seq, pairs = x, sq, None
+            cur, seq, pairs, kept = x, sq, None, new
             if x < best: best, top = x, sq
     return top, best
 
@@ -468,12 +537,13 @@ def rank_program(g, core, T, topo):
     nen = len(topo.engines(core, nxt))
     seq, succ, _ = order(ops)
     if "seq" not in KEPT: KEPT["seq"] = polish(ops, justify(ops, seq, succ, 20)[0], succ, STEPS)[0]
-    seq = KEPT["seq"]
+    loads = [i for i, o in enumerate(ops) if o["sem"] and not o["d"]]
+    seq = loads + [i for i in KEPT["seq"] if i not in loads]
     for a, i in enumerate(seq): ops[i]["t"] = a
     Q = {"v": g.vector, "s": g.scalar, "p": g.tensor, "g": g, "y": g.sync}
     total = {}
     for o in ops:
-        if o["sem"]: total[o["sem"]] = total.get(o["sem"], 0) + (nen if o["e"] == "g" else 16)
+        if o["sem"]: total[o["sem"]] = total.get(o["sem"], 0) + (nen if o["sem"][0] == "a" else 16)
     count = {e: 0 for e in "vspg"}; known = {e: {} for e in Q}; mark = {}; clock = {}
     for i in seq:
         o = ops[i]; e = o["e"]; kn = known[e]; need = {}
@@ -489,11 +559,11 @@ def rank_program(g, core, T, topo):
         ins = o["fn"]()
         if o["sem"]:
             mark[i] = (o["sem"], total[o["sem"]]); clock[i] = {}
-            if e != "g": ins.then_inc(T.sem[o["sem"]], 16)
+            if o["sem"][0] != "a": ins.then_inc(T.sem[o["sem"]], 16)
         elif [j for j in succ[i] if not (e == "p" and ops[j]["e"] == "p")]:
             count[e] += 1; ins.then_inc(T.sem[e], 1); mark[i] = (e, count[e]); clock[i] = dict(kn)
     for e in "vspg":
         g.wait_ge(T.sem[e], count[e])
-    g.wait_ge(T.sem.sent, nen * 6)
+    g.wait_ge(T.sem.sent, nen * 12)
     for t in range(RO):
         g.wait_ge(T.sem["y%d" % t], 16)

from concourse.mybir import AluOpType, ActivationFunctionType, AxisListType

A, F = AluOpType, ActivationFunctionType
RO = 4
M = 12582912.0
SC = 1742.0 / 1024
PAIRS = [(0, 2), (0, 3), (0, 1), (1, 2), (2, 3), (1, 3)] + [(j, 4) for j in range(4)] + [(j, 5) for j in range(5)] + [(j, 6) for j in range(6)]
OB, OC, OA, ONE, AB, BC, AC = range(7)
NEXT = [[1, 2, 3, 4, 5, 6], [0, 4, 2, 3, 5, 6], [0, 1, 4, 3, 5, 6], [0, 1, 2, 4, 5, 6]]
PRIO = [-1, 2 + 64, 1 + 64, 0]


PACK = 0
TWICE = [(1, 4), (2, 4), (3, 4), (0, 5), (5, 1), (2, 5), (3, 5), (4, 5)]


def slot(l):
    if l >= 15 and PACK: return 24 + [j for j, k in TWICE].index(PAIRS[l][0])
    return l if l < ONE else l + 1


SRC = [[None] * 16 for _ in NEXT]
for _x, _nx in enumerate(NEXT):
    SRC[_x][ONE] = ONE
    for _l, (_j, _k) in enumerate(PAIRS[:15]):
        SRC[_x][slot(_l)] = slot(PAIRS.index(tuple(sorted((_nx[_j], _nx[_k])))))
CUTS = [[0, 4, 8, 12, 16], [0, 4, 8, 12, 14, 16]]
MIX = [[[2, 2, 0, 0], [1, 2, 0, 0]], [[4, 2, 0, 0], [4, 2, 0, 0]], [[4, 2, 0, 0], [4, 2, 0, 0]], [[4, 2, 0, 0], [4, 1, 0, 0, 0]]]
SLACK, EARLY, LATE = 0.0, 1.1, 1
CYC, GAM, PEC, HOP = 0.83, 1.56, 0.42, 135.0
SLC, RLAT, TWO, GDMA, XLAT, NFV = 100.0, 2550, 1, 1000, 3500, 0
CDV, EVS, NXV, RSP, PFX, OB1 = 1, 1, 0, 4, 30.0, 0
NUS, CLV = [(0, 1, "s"), (1, 9, "v")], 1

S_, P_, B_, F_, H_, U_, I_ = "sbuf", "psum", "bfloat16", "float32", "float16", "uint16", "int32"
SCRATCH = {}
for _n, _w, _d in [
        ("cv", 2064, B_), ("ones", 512, B_), ("zr", 128, B_), ("idb", 128, B_), ("id4", 128, B_), ("ids", 128, H_),
        ("d8a", 8, B_), ("d8", 8, B_), ("d8s", 8, H_), ("d8f", 24, F_), ("dif", 128, F_), ("eo", 32, H_), ("eo3", 24, B_), ("pint", 16, I_), ("pf", 24, F_), ("rst", 512, B_),
        ("eh", 384, H_), ("cst", 384, B_), ("t1", 256, H_), ("binw", 912, B_), ("kw0", 128, B_), ("kw", 512, B_),
        ("csf", 24, F_), ("csd", 48, F_), ("cs", 24, H_), ("geo", 64, F_), ("cw", 256, B_), ("rg0", 128, B_), ("rg", 128, B_), ("rg2", 128, B_),
        ("mk0", 256, B_), ("mk1", 256, B_), ("mk", 256, B_), ("h4", 8, B_), ("dum", 16, F_),
        ("lv", 8, I_), ("lf", 32, F_), ("lg", 48, F_), ("l4", 48, U_)]:
    SCRATCH[_n] = (S_, [128, _w], _d)
SCRATCH["ob"] = (S_, [128, 7, 16, 16], B_)
SCRATCH["gp"] = (S_, [128, 16, 352], B_)
SCRATCH["gq"] = (S_, [128, 17, 128], F_)
SCRATCH["yb"] = (S_, [128, 4, 256], F_)
SCRATCH["ph"] = (S_, [128, 8, 128], H_)
for _c in "01":
    for _n, _w, _d in [
            ("raw", [904], I_), ("tab", [1032], F_), ("gm", [4, 128], H_), ("gb", [128], H_), ("nx", [3, 128], H_), ("cl", [4, 24], U_), ("cx", [3, 24], U_), ("nf", [384], F_), ("nu", [384], U_),
            ("bh", [128], B_), ("vv", [4, 1536], B_), ("xx", [2048], F_),
            ("pr", [2048], H_), ("px", [2048], F_), ("pw", [2048], F_), ("yy", [128], F_), ("ab", [128], B_), ("hf", [512], B_), ("lo", [128], H_), ("cd", [128], B_), ("xs", [512], F_),
            ("ohb", [128], B_), ("ohf", [128], F_), ("sel", [384], H_), ("fl", [256], B_), ("so", [8], F_), ("su", [8], U_)]:
        SCRATCH[_n + _c] = (S_, [128] + _w, _d)
for _n in ["rp0", "rp1", "mp0", "mp1"]:
    SCRATCH[_n] = (P_, [128, 512], F_)
NU = 4
for _n in range(NU):
    SCRATCH["up%d" % _n] = (P_, [128, 2048 // NU], F_)
SEMAPHORES = ["v", "s", "p", "g", "sent", "o0", "o1", "cv", "t0", "t1", "y0", "y1", "y2", "y3"] + [a % (t, c) for t in range(1, 4) for c in range(2) for a in ("a%d%d", "ac%d%d")]


def build(g, T, dst):
    ops = []; stage = [99.0]; crit = [0]
    V, S, P = g.vector, g.scalar, g.tensor

    def op(eng, rd, wr, ns, fn, bank=None, sem=None, lat=0.0, ga=False):
        fx = {"v": 50.0, "s": 65.0, "p": PFX}.get(eng, ns)
        ops.append({"fx": fx, "n": (ns - fx) / (PEC if eng == "p" else CYC), "ga": ga,
                    "e": eng, "r": rd, "w": wr, "ns": ns, "fn": fn, "b": bank, "sem": sem, "lat": lat, "k": stage[0], "c": crit[0]})

    def v(rd, wr, n, fn, bank=None): op("v", rd, wr, 50 + max(n, 32) * CYC, fn, bank)
    def s(rd, wr, n, fn, bank=None): op("s", rd, wr, 65 + max(n, 32) * CYC, fn, bank)
    def vg(rd, wr, n, fn): op("v", rd, wr, 50 + n * GAM * CYC, fn, ga=True)
    def sg(rd, wr, n, fn): op("s", rd, wr, 65 + n * GAM * CYC, fn, ga=True)
    def gp(rd, wr, n, fn): op("g", rd, wr, 170 + 2 * n * CYC, fn)

    def pe(rd, wr, mms, bank):
        def fn():
            for (o, l, r, a, z, n) in mms: last = P.matmul(o, l, r, a, z)
            return last
        op("p", rd, wr, PFX + sum(m[5] for m in mms) * PEC, fn, bank)

    def ts(o, i, a, b, o0, o1=None):
        return (lambda: V.tensor_scalar(o, i, a, None, o0)) if o1 is None else (lambda: V.tensor_scalar(o, i, a, b, o0, o1))

    def tt(o, i, j, f): return lambda: V.tensor_tensor(o, i, j, f)
    def cp(o, i): return lambda: V.tensor_copy(o, i)
    def ms(o, x): return lambda: V.memset(o, x)
    def scan(o, i, j, x, f0, f1): return lambda: V.tensor_tensor_scan(o, i, j, x, f0, f1)
    def act(o, i, f, **k): return lambda: S.activation(o, i, f, **k)
    def io(o, pat, b, cm): return lambda: g.iota(o, pat, b, cm, allow_small_or_imprecise_dtypes=True)
    def ioi(o, pat, b, cm): return lambda: g.iota(o, pat, b, cm)
    def sl(o, i, pat, f, b, cm): return lambda: g.affine_select(o, i, pat, f, 0.0, b, cm)
    def put(o, x, pat, b, i=None): return lambda: g.affine_select(o, o if i is None else i, pat, A.not_equal, x, b, 1)
    def dma(q, rd, wr, o, i, sem, lat): op(q, rd, wr, 60, lambda: (g.sync if q == "y" else S).dma_start(o, i), None, sem, lat)

    dma("y", [], ["ob0"], T.ob[:, 0:4, :, :], T.obs[:, 0:1024], "o0", 2300)
    for c in range(2):
        for h in range(4):
            dma("s" if c == 0 else "y", [], ["raw%d.%d" % (c, h)], T["raw%d" % c][:, 226 * h:226 * h + 226],
                T.tsee[:, 226 * (2 * h + c):226 * (2 * h + c) + 226], "t%d" % c, 3700 + 3000 * c)
        if c == 0:
            dma("y", [], ["cv"], T.cv[:, 0:2048], T.cvec[:, :], "cv", 4600)
            dma("y", [], ["ob1"], T.ob[:, 4:7, :, :], T.obs[:, 1024:1792], "o1", 5200)

    def zero(o, n): return ts(o, T.ones[:, 0:n], 0.0, None, A.mult)
    def fill(wr, o, n, x, p=128): s(["on1", "on2"], wr, n, act(o, T.ones[0:p, 0:n], F.Copy, scale=x))
    v([], ["on1"], 64, ms(T.ones[:, 0:128], 1.0))
    v([], ["on2"], 192, ms(T.ones[:, 128:512], 1.0))
    gp(["on1"], ["idb"], 128, sl(T.idb[:, :], T.ones[:, 0:128], [[-1, 128]], A.is_equal, 0, 1))
    gp(["on1"], ["d8a"], 8, sl(T.d8a[:, :], T.ones[:, 0:8], [[-16, 8]], A.is_ge, 0, 1))
    gp(["d8a"], ["d8"], 8, sl(T.d8[:, :], T.d8a[:, :], [[16, 8]], A.is_ge, 15, -1))
    v([], ["cvz"], 8, ms(T.cv[:, 2048:2064], 0.0))
    v([], ["gp%d" % ONE], 128, ms(T.gp[:, :, 16 * ONE:16 * ONE + 16], 113.0))
    s(["idb"], ["ids"], 128, act(T.ids[:, :], T.idb[:, :], F.Copy, scale=SC))
    s(["idb"], ["id4"], 128, act(T.id4[:, :], T.idb[:, :], F.Copy, scale=4096.0))
    for z, (name, x) in enumerate((("d8f", 1.0), ("d8g", SC), ("d8q", 4096.0))):
        s(["d8"], [name], 8, act(T.d8f[:, 8 * z:8 * z + 8], T.d8[:, :], F.Copy, scale=x))
    s(["d8"], ["d8s"], 8, act(T.d8s[:, :], T.d8[:, :], F.Copy, scale=SC))
    gp(["on1"], ["dif"], 128, sl(T.dif[:, :], T.ones[:, 0:128], [[-1, 128]], A.is_equal, 0, 1))
    gp(["dif"], ["dif"], 128, put(T.dif[:, :], -1.0, [[0, 16], [-1, 8]], -8 * ONE))
    gp(["dif"], ["dif"], 8, put(T.dif[:, 8 * ONE:8 * ONE + 8], 0.0, [[-1, 8]], -8 * ONE))
    gp([], ["csf"], 24, io(T.csf[:, :], [[0, 6], [7232, 4]], 0, 0))
    gp(["csf"], ["csf"], 24, sl(T.csf[:, :], T.csf[:, :], [[0, 24]], A.is_equal, -8 * ONE, 1))
    gp(["csf"], ["csf"], 24, put(T.csf[:, :], 3584.0, [[0, 24]], -8 * ONE - 1))
    gp(["csf"], ["csf"], 24, put(T.csf[:, :], 1.0, [[0, 24]], -8 * ONE - 2))
    gp(["csf"], ["csf"], 24, put(T.csf[:, :], 16.0, [[-1, 24]], 0))
    v(["csf"], ["cs"], 24, ts(T.cs[:, :], T.csf[:, :], 1.0 / 256, None, A.mult))
    v([], ["eb"], 64, ms(T.zr[:, :], 0.0))
    gp(["eb"], ["csd"], 24, put(T.csd[:, 0:24], 0.0625, [[-1, 24]], 0, T.zr[:, 0:24]))
    gp(["csd"], ["csd"], 24, put(T.csd[:, 0:24], -0.0625, [[0, 3], [-1, 8]], -8 * ONE))
    gp([], ["cof"], 24, io(T.csd[:, 24:48], [[0, 6], [7232, 4]], 3601, 0))
    s(["cof"], ["cof"], 24, act(T.csd[:, 24:48], T.csd[:, 24:48], F.Copy, scale=1.0 / 32))
    for e, (q, x) in enumerate(((AC, -4096.0), (AB, -SC), (BC, -SC))):
        gp(["eb"], ["eh%d" % e], 128, put(T.eh[:, 128 * e:128 * e + 128], x, [[-1, 8], [0, 16]], -8 * q, T.zr[:, :]))
    v([], ["cst"], 128, ms(T.cst[0:64, :], 0.0))
    for r0, c0, x in ((0, 0, -1800.0 * 4096), (32, 0, -1800.0), (0, 128, -3072.0), (32, 128, 9.125), (0, 256, -1800.0)):
        v([], ["cst"], 64, ms(T.cst[r0:r0 + 1, c0:c0 + 128], x))
    gp([], ["lv0"], 1, ioi(T.lv[:, 0:1], [[0, 1]], 0, 1))
    for k, (sh, an) in enumerate([(3, 1), (0, 15), (0, 7), (6, 1), (4, 3)]):
        v(["lv0"], ["pi%d" % k], 1, ts(T.pint[:, k:k + 1], T.lv[:, 0:1], sh, an, A.logical_shift_right, A.bitwise_and))
    v(["pi%d" % k for k in range(5)], ["pf"], 8, cp(T.pf[:, 0:5], T.pint[:, 0:5]))
    HI, P16, P8, KK, K4 = [T.pf[:, k:k + 1] for k in range(5)]
    runs = []
    for u, cut in enumerate(CUTS):
        for r0, r1 in zip(cut, cut[1:]):
            if runs and runs[-1][0] == u and runs[-1][2] == r1 - r0: runs[-1][3] += 1
            else: runs.append([u, r0, r1 - r0, 1])
    for u, r0, w, n in runs:
        j = 24 * u + 3 * r0 // 2
        gp([], ["lg%d" % j], 3 * w * n // 2, io(T.lg[:, j:j + 3 * w * n // 2], [[w, n], [128, 3], [2, w // 2]], r0, 0))
    v(["pf"], ["pq4"], 1, ts(T.pf[:, 13:14], P8, 16.0, HI, A.mult, A.add))
    v(["lg%d" % (24 * u + 3 * r0 // 2) for u, r0, w, n in runs] + ["pq4"], ["l4"], 48, ts(T.l4[:, :], T.lg[:, :], T.pf[:, 13:14], None, A.add))
    fill(["pb0"], T.ph[:, 0:4, 88:128], 160, 0.0)
    fill(["pb4"], T.ph[:, 4:8, 0:88], 352, 0.0)
    names = []
    for x in (0, 2):
        q = 0
        while q < 16:
            a, b = SRC[x][q], SRC[x + 1][q]; n = 1
            while q + n < 16 and (SRC[x][q + n], SRC[x + 1][q + n]) == (a + n, b + n) and a + n != 16 and b + n != 16: n += 1
            u = 4 * (a // 16) + x; names.append("pb%d.%d" % (x, q))
            gp(["on1"], [names[-1]], 16 * n, sl(T.ph[:, u:u + 2, 8 * q:8 * (q + n)], T.ones[:, 0:16 * n], [[8 * (a - b), 2], [-1, 8 * n]], A.is_equal, -8 * (a % 16), 1))
            q += n
    names += ["pb0", "pb4"]
    v([], ["kw0"], 64, ms(T.kw0[:, :], 16384.0))
    gp(["kw0"], ["kw0"], 128, sl(T.kw0[:, :], T.kw0[:, :], [[0, 16], [-16, 8]], A.is_ge, 0, 1))
    gp(["kw0"], ["kw"], 128, sl(T.kw[:, 0:128], T.kw0[:, :], [[0, 16], [16, 8]], A.is_ge, 15, -1))
    s(["kw"], ["kn"], 128, act(T.kw[:, 128:256], T.kw[:, 0:128], F.Copy, scale=-1.0))
    s(["kw"], ["kf"], 128, act(T.kw[:, 256:384], T.kw[:, 0:128], F.Copy, scale=32.0))
    s(["idb"], ["id8"], 128, act(T.kw[:, 384:512], T.idb[:, :], F.Copy, scale=8192.0))
    for x in range(4): fill(["rst%d" % x], T.rst[:, x:512:4], 128, 4096.0 * (PRIO[x - 1] - PRIO[x]) if x else -2.0 ** 40)
    v([], ["ge0"], 16, ms(T.geo[:, 0:16], 2.0 ** -9))
    v([], ["ge1"], 16, ms(T.geo[:, 16:32], 0.0))
    v(["ge0", "ge1"], ["ge2"], 16, scan(T.geo[:, 32:48], T.geo[:, 0:16], T.geo[:, 16:32], 2.0 ** 57, A.mult, A.add))
    gp([], ["lf0"], 16, io(T.lf[:, 0:16], [[1, 16]], 0, 0))
    v(["lf0", "pf"], ["lf1"], 16, ts(T.lf[:, 16:32], T.lf[:, 0:16], P16, None, A.is_equal))
    v(["lf1", "ge2"], ["ge3"], 32, tt(T.geo[:, 48:64], T.lf[:, 16:32], T.geo[:, 32:48], A.mult))
    v(["ge3"], ["wp"], 16, lambda: V.tensor_reduce(T.pf[:, 8:9], T.geo[:, 48:64], AxisListType.X, A.add))
    v(["wp"], ["wn"], 1, ts(T.pf[:, 9:10], T.pf[:, 8:9], -1.0, None, A.mult))
    gp([], ["off"], 128, io(T.cw[:, 128:256], [[0, 8], [1, 16]], 0, 0))
    v(["off", "pf"], ["off"], 64, ts(T.cw[:, 128:256], T.cw[:, 128:256], P16, -2.0 ** 60, A.not_equal, A.mult))
    v(["on1"], ["eo"], 8, zero(T.eo[:, :], 32))
    v(["d8"], ["eo"], 8, cp(T.eo[:, 2:26:3], T.d8[:, :]))
    for m in range(3):
        s(["d8"], ["eo3.%d" % m], 8, act(T.eo3[:, m:24:3], T.d8[:, :], F.Copy, scale=1.0 / 2048))
    gp([], ["binw"], 904, io(T.binw[:, 0:904], [[0, 4], [1, 226]], 0, 0))
    for kk in range(2):
        gp(["on1"], ["t1"], 128, sl(T.t1[:, 128 * kk:128 * kk + 128], T.ones[:, 0:128], [[0, 2], [-1, 4], [0, 16]], A.is_equal, -8 * OA - 4 * kk, 1))
    gp(["t1"], ["t1"], 256, put(T.t1[:, :], 224.0 - 288.0, [[0, 256]], -8 * ONE))
    gp(["t1"], ["t1"], 256, put(T.t1[:, :], 0.0625, [[0, 256]], -8 * ONE - 1))
    v([], ["rg0"], 64, ms(T.rg0[:, :], -1.0))
    gp(["rg0"], ["rg0"], 128, sl(T.rg0[:, :], T.rg0[:, :], [[-16, 8], [0, 16]], A.is_ge, 0, 1))
    gp(["rg0"], ["rg"], 128, sl(T.rg[:, :], T.rg0[:, :], [[16, 8], [0, 16]], A.is_ge, 15, -1))
    s(["rg"], ["rg2"], 128, act(T.rg2[:, :], T.rg[:, :], F.Copy, scale=2.0))
    s(["rg", "wn"], ["cw"], 128, act(T.cw[:, 0:128], T.rg[:, :], F.Copy, scale=T.pf[:, 9:10]))
    gp([], ["mk0"], 256, io(T.mk0[:, :], [[-1, 2], [0, 8], [-2, 16]], 0, 0))
    v(["pf"], ["pq2"], 1, ts(T.pf[:, 12:13], P16, 2.0, KK, A.mult, A.add))
    s(["mk0", "pq2"], ["mk1"], 256, act(T.mk1[:, :], T.mk0[:, :], F.Sign, bias=T.pf[:, 12:13]))
    s(["mk1"], ["mk"], 256, act(T.mk[:, :], T.mk1[:, :], F.Square, scale=128.0, bias=48.0))
    v(["lf0", "pf"], ["h4"], 4, ts(T.h4[:, 0:4], T.lf[:, 0:4], K4, 4096.0, A.is_equal, A.mult))
    gp([], ["du0"], 8, io(T.dum[:, 8:16], [[16, 8]], 904, 0))
    v(["du0", "pf"], ["dum"], 8, ts(T.dum[:, 0:8], T.dum[:, 8:16], P16, None, A.add))

    def gram(d0, d1, tiles):
        for l in range(d0, d1):
            j, w = PAIRS[l]; q = slot(l)
            v(["ob0", "ob1"] if w > 3 else ["ob0"], ["gp%d" % q], 256, tt(T.gp[:, :, 16 * q:16 * q + 16], T.ob[:, j, :, :], T.ob[:, w, :, :], A.mult))
        for c in range(2):
            for q0, q1, p0, c0, name in tiles:
                u = "up%d" % c; m = 8 * (q1 - q0)
                pe(["d8"] + ["gp%d" % z for z in range(q0, q1)], [u], [(T[u][0:m, c0 + r:c0 + 128:16], T.gp[:, r, 16 * q0 + c:16 * q1:2], T.d8[:, :], True, True, 64) for r in range(16)], u)
                o = T["gb%d" % c][0:m, :] if q0 == 16 else T["gm%d" % c][p0:m, 0, :]
                if EVS and name + str(c) in ("go0", "go1", "ga0", "ga1")[:EVS]: s([u], [name + str(c)], 128, act(o, T[u][p0:m, c0:c0 + 128], F.Copy, bias=-1800.0), u)
                else: v([u], [name + str(c)], 128, ts(o, T[u][p0:m, c0:c0 + 128], -1800.0, None, A.add), u)
    gram(0, 3, [(0, 4, 0, 0, "go")])
    gram(3, 7, [(0, 8, 32, 128, "ga")])
    for c in range(2):
        gp([], ["tab%d" % c], 128, io(T["tab%d" % c][:, 904:1032], [[0, 128]], 0, 0))
        for h in range(4):
            gp(["raw%d.%d" % (c, z) for z in range(4)], ["tad%d.%d" % (c, h)], 226, sl(T["tab%d" % c][:, 226 * h:226 * h + 226], T["raw%d" % c][:, 226 * h:226 * h + 226], [[0, 226]], A.is_ge, 0, 0))
    sums = {4: ("rp1", "ra1", 0), 5: ("rp1", "rc1", 256), 1: ("mp1", "ma1", 0)} if PACK else {}
    for w, (u, name, c0) in sums.items():
        o = T[u][:, c0:c0 + 256]
        pe(["ob0", "ob1", "idb", "id4"], [name], [(o, T.idb[:, :], T.ob[:, w, :, :], True, False, 256), (o, T.id4[:, :], T.ob[:, 6, :, :], False, True, 256)], u)
    for q, (j, w) in enumerate(TWICE if PACK else []):
        u, name, c0 = sums[w]
        v(["ob0", "ob1", name], ["gq%d" % q], 256, tt(T.gq[:, 1:17, 16 * q:16 * q + 16], T.ob[:, j, :, :], T[u][:, c0:c0 + 256], A.mult), u)
    if PACK: fill(["gq"], T.gq[:, 0, :], 128, 0.0)

    def apart():
        for c in range(2):
            u = nextu(); x = T[u][64:128, 0:128]; y = T["yy%d" % c][64:128, :]
            fill(["gz%d" % c], T["gb%d" % c][0:64, :], 128, 0.0, 64)
            pe(["cst", "on1"], [u], [(T[u][:, 0:128], T.ones[0:1, 0:128], T.cst[0:1, 256:384], True, False, 128)], u)
            for r0 in range(0, 16, 4):
                pe(["d8f", "gq"] + ["gq%d" % q for q in range(8)], [u], [(T[u][:, r:128:16], T.gq[:, r:r + 2, c:128:2], T.d8f[:, 0:8], False, r == 15, 256) for r in range(r0, r0 + 4)], u)
            v([u], ["yy%d" % c], 128, ts(y, x, 1.5 * 2.0 ** 35, -1.5 * 2.0 ** 35, A.add, A.add), u)
            v([u, "yy%d" % c], ["gc%d" % c], 128, tt(T["gm%d" % c][64:128, 0, :], x, y, A.subtract), u)
            v(["yy%d" % c, "gz%d" % c], ["gb%d" % c], 128, ts(T["gb%d" % c][64:128, :], y, 1.0 / 4096, -1800.0, A.mult, A.add))
    late = [apart if PACK else lambda: gram(7, len(PAIRS), [(0, 16, 64, 128, "gc"), (16, 22, 0, 256, "gb")])]

    ubank = [0]
    def nextu():
        ubank[0] = (ubank[0] + 1) % NU
        return "up%d" % ubank[0]

    def out(t, c):
        def b(n): return T[n + str(c)]
        def k(n): return n + str(c)
        mp = b("mp"); mm = []
        for z in range(8):
            o = mp[0:24, 128 + z:256:8]
            mm += [(o, T.eo3[:, :], b("ohb")[:, 16 * z:16 * z + 16], True, False, 24)] + \
                  [(o, T.eo[:, 2 - m:26 - m], b("sel")[:, 128 * e + 16 * z:128 * e + 16 * z + 16], False, e == 2, 24) for e, m in enumerate((1, 2, 0))]
        pe([k("sel"), k("ohb"), "eo", "eo3.0", "eo3.1", "eo3.2"], [k("mb"), k("mg")], mm, k("mp"))
        s([k("mb")], ["yb%d.%d" % (t, c)], 128, act(T.yb[0:24, t, c:256:2], mp[0:24, 128:256], F.Copy, bias=-1.0), k("mp"))
        if c: dma("y", ["yb%d.0" % t, "yb%d.1" % t], ["yn%d" % t], T.yn[:, 768 * t:768 * t + 768], T.yb[0:24, t, :], "y%d" % t, 2000)

    win = T.cv[:, 0:2064]
    for t in range(RO):
        for c in range(2):
            def b(n): return T[n + str(c)]
            def k(n): return n + str(c)
            last = t == RO - 1
            G3, G6, GA = b("gm")[0:32, t, :], b("gm")[0:64, t, :], b("gm")[:, t, :]
            g3, g6 = ([k("go")], [k("go"), k("ga")]) if t == 0 else (["g%d%d" % (c, t)],) * 2
            rp, mp = b("rp"), b("mp")
            stage[0] = 2 * t + c - EARLY; crit[0] = 1
            cl = "cl%d%d" % (c, t)
            if t == 0:
                pe(g3 + ["cs"], [k("md"), k("mg")], [(mp[:, 384:408], G3, T.cs[0:32, :], True, True, 64)], k("mp"))
                v([k("md")], [cl], 24, ts(b("cl")[:, 0, :], mp[:, 384:408], M, -M, A.add, A.add), k("mp"))
            table, tn = (b("raw")[:, :], ["raw%d.%d" % (c, h) for h in range(4)]) if t == 0 else (b("tab")[:, 0:904], [k("tab")])
            sg([cl] + tn, [k("nf"), k("ng")], 384, act(b("nf")[:, :], table.indirect(b("cl")[:, t, :]), F.Copy))
            u = int(last and c == 1); cut = CUTS[u]
            for n0, n1, e in [(n0, min(n1, len(cut) - 1), e) for n0, n1, e in NUS]:
                j0, j1 = 24 * cut[n0], 24 * cut[n1]; src = b("nf")[:, :].indirect(T.l4[:, 24 * u + j0 // 16:24 * u + j1 // 16])
                (vg if e == "v" else sg)([k("nf"), k("ng"), "l4"], [k("nu%d" % n) for n in range(n0, n1)], j1 - j0, cp(b("nu")[:, j0:j1], src) if e == "v" else act(b("nu")[:, j0:j1], src, F.Copy))
            crit[0] = 0
            if not last:
                sg([cl, "binw"], [k("bh")], 128, act(b("bh")[:, :], T.binw[:, 0:904].indirect(b("cl")[:, t, 16:24]), F.Copy))
            stage[0] = 2 * t + c
            if t: out(t - 1, c)
            R1, R0 = rp[:, 0:128], mp[:, 0:128]
            pe(g6 + ["cst", "on1", "eh0"], [k("ra"), k("rg")], [(R1, T.ones[0:64, 0:128], T.cst[0:64, 0:128], True, False, 128), (R1, T.eh[0:64, 0:128], G6, False, False, 128)], k("rp"))
            pe(g6 + ["cst", "on1", "eh2"], [k("ma"), k("mg")], [(R0, T.ones[0:64, 0:128], T.cst[0:64, 128:256], True, False, 128), (R0, T.eh[0:64, 256:384], G6, False, False, 128)], k("mp"))
            NB = len(cut) - 1; wait = []
            for n in range(NB):
                R = range(cut[n], cut[n + 1]); E = 128 * len(R); e0 = 128 * cut[n]; cs = slice(e0, e0 + E); x = "%d.%d" % (c, n); end = n == NB - 1
                def gat(m0, m1): return win.indirect(b("nu")[:, (3 * e0 + E * m0) // 16:(3 * e0 + E * m1) // 16])
                def vv(m0, m1, z=0, w=None): return b("vv")[:, e0 // 512, 3 * (e0 % 512) + E * m0 + z:3 * (e0 % 512) + (E * m1 if w is None else E * m0 + z + w)]
                cvr = ["cv", "cvz", k("nu%d" % n)]; mix = MIX[t][c][n]
                if mix == 4:
                    X = b("xx")[:, cs]; ub = nextu()
                    sg(cvr, ["vb" + x], E, act(vv(0, 1), gat(0, 1), F.Copy, scale=1.0 / 4096))
                    vg(cvr + ["vb" + x], ["xx" + x], E, tt(X, gat(1, 2), vv(0, 1), A.add))
                    pe(["vb" + x, "id4"], [ub], [(T[ub][:, 0:E], T.id4[:, :], vv(0, 1), True, True, E)], ub)
                    v(["xx" + x, ub], ["p0" + x], E, tt(b("px")[:, cs], X, T[ub][:, 0:E], A.mult), ub)
                    vg(cvr + ["xx" + x], ["p1" + x], E, tt(b("pw")[:, cs], gat(2, 3), X, A.mult))
                elif mix == 2: sg(cvr, ["vb" + x, "va" + x], 3 * E, act(vv(0, 3), gat(0, 3), F.Copy))
                else:
                    sg(cvr, ["vb" + x], 2 * E, act(vv(0, 2), gat(0, 2), F.Copy))
                    if mix: vg(cvr, ["va" + x], E, cp(vv(2, 3), gat(2, 3)))
                    else: sg(cvr, ["va" + x], E, act(vv(2, 3), gat(2, 3), F.Copy))
                if mix < 3:
                    ub = nextu(); mm = []
                    for z in range(0, E, 512):
                        w = min(512, E - z)
                        mm += [(T[ub][:, z:z + w], T.idb[:, :], vv(0, 1, z, w), True, False, w), (T[ub][:, z:z + w], T.id4[:, :], vv(1, 2, z, w), False, True, w)]
                    pe(["vb" + x, "idb", "id4"], [ub], mm, ub)
                    v(["vb" + x], ["p0" + x], E, tt(b("pr")[:, cs], vv(0, 1), vv(1, 2), A.mult))
                    v(["va" + x, ub], ["p1" + x], E, tt(b("pw")[:, cs], vv(2, 3), T[ub][:, 0:E], A.mult), ub)
                p0, w0, n0, w1 = (b("px"), T.d8f[:, 8:16], 256, T.d8f[:, 16:24]) if mix == 4 else (b("pr"), T.d8s[:, :], 64, T.d8f[:, 0:8])
                pe(["p0" + x, k("mg"), "d8s", "d8g"], [k("ma"), k("mg")] if end else ["r0" + x], [(mp[:, r:128:16], p0[:, 128 * r:128 * r + 128], w0, False, r == 15, n0) for r in R], k("mp"))
                pe(["p1" + x, k("rg"), "d8f", "d8q"], [k("ra"), k("rg")] if end else ["r1" + x], [(rp[:, r:128:16], b("pw")[:, 128 * r:128 * r + 128], w1, False, r == 15, 256) for r in R], k("rp"))
                if late and n == LATE: late.pop()()
            crit[0] = 1
            H = [b("hf")[:, 128 * e:128 * e + 128] for e in range(4)]; EV = H[3]
            v([k("ma")], [k("h0")], 128, ts(H[0], R0, 1.5 * 2.0 ** 32, 1.5 * 2.0 ** 32, A.add, A.not_equal), k("mp"))
            if not TWO: s([k("ra")], [k("ac")], 128, act(b("ab")[:, :], R1, F.Abs, scale=1.0 / 4096), k("rp"))
            v([k("ra")], [k("yy")], 128, ts(b("yy")[:, :], R1, 1.5 * 2.0 ** 35, -1.5 * 2.0 ** 35, A.add, A.add), k("rp"))
            if TWO:
                v([k("ra")], [k("h1")], 128, ts(H[1], R1, 150.5 * 4096, None, A.is_gt), k("rp"))
                v([k("ra")], [k("h2")], 128, ts(b("ab")[:, :], R1, -150.5 * 4096, None, A.is_lt), k("rp"))
            v([k("ra"), k("yy")], [k("lo")], 128, tt(b("lo")[:, :], R1, b("yy")[:, :], A.subtract), k("rp"))
            if not TWO: v([k("ac")], [k("h1")], 64, ts(H[1], b("ab")[:, :], 150.0, None, A.is_gt))
            NAC = [H[1], b("ab")[:, :]][:1 + TWO]; nac = [k("h1"), k("h2")][:1 + TWO]
            Ra, Re = mp[:, 128:256], mp[:, 256:384]
            pe(g6 + [k("h0"), "eh1", "id8"], [k("mc"), k("mg")], [(Re, T.eh[0:64, 128:256], G6, True, False, 128), (Re, T.kw[:, 384:512], H[0], False, False, 128)], k("mp"))
            pe(nac + ["id8"], [k("mc"), k("mg")], [(Re, T.kw[:, 384:512], z, False, False, 128) for z in NAC], k("mp"))
            pe(g6 + [k("lo"), "ids"], [k("mb"), k("mc"), k("mg")], [(Re, T.ids[:, :], b("lo")[:, :], False, True, 128)] +
               ([] if last else [(Ra, T.eh[0:64, 128:256], G6, True, False, 128), (Ra, T.ids[:, :], b("lo")[:, :], False, True, 128)]), k("mp"))
            z = 128 * last
            v([k("mb"), k("mc")], [k("ev")], 256 - z, ts(b("hf")[:, 256 + z:512], mp[:, 128 + z:384], 1.5 * 2.0 ** 32, 1.5 * 2.0 ** 32, A.add, A.is_equal), k("mp"))
            whole = [k("ra"), k("rb"), k("rc")]
            if not last:
                def val(x): return [(rp[:, x:512:4], T.ph[:, x, :], GA, True, False, 128)] + [(rp[:, x:512:4], T.ph[0:48 + 80 * PACK, 4 + x, :], b("gb")[0:48 + 80 * PACK, :], False, False, 128)] * (t == 0)
                def cnt(x, w, zs): return [(rp[:, x:512:4], T.kw[:, 128 * w:128 * w + 128], z, False, z is zs[-1], 128) for z in zs]
                gall = g6 + names + ([k("gb"), k("gc")] if t == 0 else [])
                pe(gall + [k("h0"), "kn"], whole + [k("rg")], val(1) + cnt(1, 1, [H[0]]), k("rp"))
                pe(gall + nac + ["kn"], whole + [k("rg")], val(2) + cnt(2, 1, NAC) + val(3), k("rp"))
                pe(gall + [k("ev"), "kw", "kf"], whole + [k("rg")], cnt(3, 0, [H[2]]) + val(0) + cnt(0, 2, [EV]), k("rp"))
                v(whole + ["rst0", "rst1", "rst2", "rst3"], [k("xs")], 512, scan(b("xs")[:, :], T.rst[:, :], rp[:, :], 0.0, A.add, A.max), k("rp"))
                pe([k("xs"), "csd"], [k("rb"), k("rg")], [(rp[:, 128:152], b("xs")[:, 3:512:4], T.csd[:, 0:24], True, True, 256)], k("rp"))
                v([k("rb"), "cof"], ["cx%d%d" % (c, t)], 24, tt(b("cx")[:, t, :], rp[:, 128:152], T.csd[:, 24:48], A.add), k("rp"))
                pe([k("xs"), "dif"], [k("ra"), k("rg")], [(R1, T.dif[:, :], b("xs")[:, 3:512:4], True, True, 512)], k("rp"))
                op("g", ["cx%d%d" % (c, t)], ["cl%d%d" % (c, t + 1)], 500,
                   (lambda o, i, a: lambda: g.remote_dma(o, i, T.sem[a], T.sem.sent, dst[1], dst[0], dst[2]))(b("cl")[:, t + 1, :], b("cx")[:, t, :], "ac%d%d" % (t + 1, c)),
                   None, "ac%d%d" % (t + 1, c), RLAT)
                if NXV: v([k("ra")], ["nx%d%d" % (c, t)], 128, ts(b("nx")[:, t, :], R1, 8.0, None, A.add), k("rp"))
                else: s([k("ra")], ["nx%d%d" % (c, t)], 128, act(b("nx")[:, t, :], R1, F.Copy, bias=8.0), k("rp"))
                an = "a%d%d" % (t + 1, c)
                op("g", ["nx%d%d" % (c, t)], ["g%d%d" % (c, t + 1)], 500,
                   (lambda o, i, a: lambda: g.remote_dma(o, i, T.sem[a], T.sem.sent, dst[1], dst[0], dst[2]))(b("gm")[:, t + 1, :], b("nx")[:, t, :], an),
                   None, an, RLAT)
                crit[0] = 0
            pe([k("ev"), "cw", "idb", "off"], [k("mb"), k("mg")], [(Ra, T.idb[:, :], T.cw[:, 128:256], True, False, 128), (Ra, EV, T.cw[:, 0:128], False, True, 128)], k("mp"))
            if CDV or last: v([k("mb")], [k("cd")], 128, ts(b("cd")[:, :], Ra, 0.0, None, A.max), k("mp"))
            else: s([k("mb")], [k("cd")], 128, act(b("cd")[:, :], Ra, F.Relu), k("mp"))
            pe([k("cd"), "rg"], [k("mc"), k("mg")], [(Re, T.rg[:, :], b("cd")[:, :], True, True, 128)], k("mp"))
            v([k("mc"), "wn"], [k("ohb")], 128, ts(b("ohb")[:, :], Re, T.pf[:, 9:10], 2048.0, A.is_equal, A.mult), k("mp"))
            if not last:
                gp([k("ohb")], [k("ohf")], 128, sl(b("ohf")[:, :], b("ohb")[:, :], [[0, 128]], A.is_ge, 0, 0))
                ub = nextu(); up = T[ub]; mm = [(up[:, 0:256], T.idb[:, :], T.mk[:, :], True, False, 256)]
                for kk in range(2):
                    o = up[:, 128 * kk:128 * kk + 128]
                    mm += [(o, T.t1[0:32, 128 * kk:128 * kk + 128], G3, False, False, 128), (o, b("bh")[:, :], T.rg[:, :], False, False, 128)]
                pe(g6 + [k("bh"), k("lo"), "t1", "rg", "mk", "idb"], [ub], mm, ub)
                pe([k("ohb"), "rg2"], [ub], [(up[:, 128 * kk:128 * kk + 128], b("ohb")[:, :], T.rg2[:, :], False, kk == 1, 128) for kk in range(2)], ub)
                v([ub], [k("fl")], 256, ts(b("fl")[:, :], up[:, 0:256], 1.5 * 2.0 ** 27, 1.5 * 2.0 ** 27, A.add, A.is_equal), ub)
                pe(g6 + [k("fl"), "cs", "h4"], [k("mf"), k("mg")], [(mp[:, 416:424], G3, T.cs[0:32, 16:24], True, False, 64)] +
                   [(mp[:, 416 + 4 * kk:420 + 4 * kk], b("fl")[:, 128 * kk:128 * kk + 128], T.h4[:, 0:4], False, kk == 1, 64) for kk in range(2)], k("mp"))
                v([k("mf"), "dum"], [k("su")], 8, tt(b("su")[:, :], mp[:, 416:424], T.dum[:, 0:8], A.min), k("mp"))
                v([k("su"), k("nf"), k("ohf")] + [k("tad") + ".%d" % h for h in range(4)], [k("tab")], 128 * 3.8, tt(b("tab")[:, :].indirect(b("su")[:, :]), b("nf")[:, 256:384], b("ohf")[:, :], A.max))
            pe([k("ohb"), "idb"], whole + [k("rg")], [(rp[:, 128 * e:128 * e + 128], T.idb[:, :], b("ohb")[:, :], True, True, 128) for e in range(3)], k("rp"))
            v(whole + [k("nf"), k("ng")], [k("sel")], 384, tt(b("sel")[:, :], b("nf")[:, :], rp[:, 0:384], A.min), k("rp"))
            if last: out(t, c)
    return ops


def order(ops):
    n = len(ops); lw, rds, lb = {}, {}, {}
    for i, o in enumerate(ops):
        d = set()
        for r in o["r"]:
            d.add(lw[r])
        for w in o["w"]:
            if w in lw: d.add(lw[w])
            d.update(rds.get(w, []))
        if o["b"] is not None:
            run = lb.get(o["b"], [])
            if run and ops[run[-1]]["e"] == o["e"]:
                o["bd"] = ops[run[-1]]["bd"]; run.append(i)
            else:
                o["bd"] = set(run); lb[o["b"]] = [i]
            d |= o["bd"]
        d.discard(i); o["d"] = d
        for r in o["r"]: rds.setdefault(r, []).append(i)
        for w in o["w"]: lw[w] = i; rds[w] = []
    succ = [[] for _ in ops]
    for i, o in enumerate(ops):
        for j in o["d"]: succ[j].append(i)
    pri = [0.0] * n
    for i in range(n - 1, -1, -1):
        ops[i]["k"] = min([ops[i]["k"]] + [ops[j]["k"] for j in succ[i]])
        pri[i] = ops[i]["ns"] + ops[i]["lat"] + max([pri[j] + HOP for j in succ[i]] + [0.0])
    free = {e: 0.0 for e in "vspgy"}; fin = [None] * n; left = [len(o["d"]) for o in ops]
    ready = [i for i in range(n) if left[i] == 0]; at = [0.0] * n; seq = []
    while ready:
        st = {i: max(at[i], free[ops[i]["e"]]) for i in ready}
        t0 = min(st.values()); e = ops[min(ready, key=lambda i: (st[i], -pri[i]))]["e"]
        best = max([i for i in ready if ops[i]["e"] == e and st[i] <= t0 + (SLC if ops[i]["c"] else SLACK)], key=lambda i: (-ops[i]["k"], pri[i]))
        ready.remove(best); seq.append(best)
        free[e] = st[best] + ops[best]["ns"]; fin[best] = free[e] + ops[best]["lat"]; ops[best]["t"] = st[best]
        for j in succ[best]:
            at[j] = max(at[j], fin[best] + (0.0 if e == "p" and ops[j]["e"] == "p" else HOP)); left[j] -= 1
            if left[j] == 0: ready.append(j)
    return seq, succ, max(fin)


def justify(ops, seq, succ, rounds):
    n = len(ops); hop = lambda i, j: 0.0 if ops[i]["e"] == "p" and ops[j]["e"] == "p" else HOP

    def place(sq, back):
        busy = {e: [] for e in "vspgy"}; st = [0.0] * n
        for i in sq:
            o = ops[i]; ns = o["ns"]
            if back: t = max([st[j] + ops[j]["ns"] + hop(i, j) for j in succ[i]] + [0.0]) + o["lat"]
            else: t = max([st[j] + ops[j]["ns"] + ops[j]["lat"] + hop(i, j) for j in o["d"]] + [0.0])
            q = busy[o["e"]]; a = len(q)
            while a and q[a - 1][0] >= t: a -= 1
            if a: t = max(t, q[a - 1][1])
            while a < len(q) and q[a][0] < t + ns: t = q[a][1]; a += 1
            q.insert(a, (t, t + ns)); st[i] = t
        return st, max(st[i] + ops[i]["ns"] + (0.0 if back else ops[i]["lat"]) for i in range(n))
    best = None
    for _ in range(rounds):
        st, span = place(seq, False); seq = sorted(seq, key=lambda i: st[i])
        if best is None or span < best[0]: best = (span, seq)
        sq = sorted(seq[::-1], key=lambda i: -(st[i] + ops[i]["ns"] + ops[i]["lat"])); st, span = place(sq, True)
        seq = sorted(sq[::-1], key=lambda i: -(st[i] + ops[i]["ns"]))
    return best[1], best[0]


CASES = [(1.56, 1.0, 135.0, 1.0), (1.12, 1.0, 120.0, 1.1), (1.95, 0.5, 150.0, 1.3), (1.3, 0.5, 190.0, 1.2)]
STEPS, HEAT = 60000, 80.0
KEPT = {}


def polish(ops, seq, succ, steps):
    n = len(ops); eng = ["vspgy".index(o["e"]) for o in ops]; lat = [o["lat"] for o in ops]
    dep = [[(j, not (o["e"] == "p" and ops[j]["e"] == "p")) for j in o["d"]] for o in ops]
    cost = [[f * (o["fx"] + (o["ns"] - o["fx"]) * (gm / GAM if o["ga"] else 1.0)) for o in ops] for gm, pc, hop, f in CASES]

    above = []
    for i, o in enumerate(ops):
        far = 0
        for j in o["d"]: far |= above[j]
        dep[i] = [(j, h) for j, h in dep[i] if not far >> j & 1]
        for j in o["d"]: far |= 1 << j
        above.append(far)
    step = [[(eng[i], [(j, hop if h else 0.0) for j, h in dep[i]], ns[i], 10.0 * hop + 1200.0 if eng[i] == 3 and lat[i] else lat[i]) for i in range(n)] for ns, (gm, pc, hop, f) in zip(cost, CASES)]

    def span(sq, old=None, a=0):
        tot = 0.0; new = []; a = a // 32 if old else 0
        for x, (gm, pc, hop, f) in enumerate(CASES):
            fin = old[x][0][:] if old else [0.0] * n; marks = old[x][1][:a + 1] if old else [[0.0] * 5]; free = marks[a][:]; sx = step[x]
            for p in range(32 * a, n, 32):
                for i in sq[p:p + 32]:
                    e, dp, ns, lt = sx[i]; st = free[e]
                    for j, h in dp:
                        if fin[j] + h > st: st = fin[j] + h
                    st += ns; free[e] = st; fin[i] = st + lt
                marks.append(free[:])
            tot += pc * (max(fin) + 0.02 * sum(fin) / n); new.append((fin, marks))
        return tot / len(CASES), new

    def held(sq, case):
        ns = cost[case]; hop = CASES[case][2]; free = [0.0] * 5; prev = [None] * 5; fin = [0.0] * n; why = [None] * n
        for i in sq:
            e = eng[i]; st = free[e]; y = (prev[e], True)
            for j, h in dep[i]:
                x = fin[j] + hop if h else fin[j]
                if x >= st: st = x; y = (j, False)
            st += ns[i]; free[e] = st; fin[i] = st + step[case][i][3]; why[i] = y; prev[e] = i
        i = max(range(n), key=lambda z: fin[z]); out = []
        while why[i][0] is not None:
            if why[i][1] and eng[i] < 4: out.append((why[i][0], i))
            i = why[i][0]
        return out

    def ahead(sq, u, w):
        a, z = sq.index(u), sq.index(w); need = set(ops[w]["d"]); took = set(); engs = set(); first = [w]; rest = []
        for i in reversed(sq[a:z]):
            if i in need or eng[i] in engs:
                if i == u: return None
                need |= ops[i]["d"]; engs.add(eng[i]); first.append(i)
            else: rest.append(i)
        return sq[:a] + first[::-1] + rest[::-1] + sq[z + 1:]
    cur, kept = span(seq); best = cur; top = seq; r = 12345; pairs = None
    for it in range(steps):
        r = (r * 1103515245 + 12345) % 2147483648
        if (r >> 8) % 4:
            if pairs is None: pairs = held(seq, (r >> 12) % len(CASES))
            if not pairs: pairs = None; continue
            u, w = pairs.pop((r >> 14) % len(pairs)); sq = ahead(seq, u, w); a = seq.index(u)
            if sq is None: continue
        else:
            r = (r * 1103515245 + 12345) % 2147483648; a = (r >> 8) % n; i = seq[a]
            if eng[i] > 3: continue
            r = (r * 1103515245 + 12345) % 2147483648; hops = 1 + (r >> 8) % 3; up = (r >> 20) & 1
            near = set(ops[i]["d"]) if up else set(succ[i]); p = a; to = None
            while hops and 0 < p < n - 1:
                p += -1 if up else 1
                if seq[p] in near: break
                if eng[seq[p]] == eng[i]: to = p; hops -= 1
            if to is None: continue
            sq = seq[:a] + seq[a + 1:]; sq.insert(to, i); a = min(a, to)
        x, new = span(sq, kept, a)
        if x <= cur + HEAT * (1.0 - it / steps):
            cur, seq, pairs, kept = x, sq, None, new
            if x < best: best, top = x, sq
    return top, best


def rank_program(g, core, T, topo):
    rank = T.rank_of(core)
    if rank is None:
        return
    nxt = T.cores[(rank + 1) % len(T.cores)]
    rid, pid = topo.addr(nxt, core)
    ops = build(g, T, (rid, pid, topo.mask(core, nxt)))
    nen = len(topo.engines(core, nxt))
    seq, succ, _ = order(ops)
    if "seq" not in KEPT: KEPT["seq"] = polish(ops, justify(ops, seq, succ, 20)[0], succ, STEPS)[0]
    loads = [i for i, o in enumerate(ops) if o["sem"] and not o["d"]]
    seq = loads + [i for i in KEPT["seq"] if i not in loads]
    for a, i in enumerate(seq): ops[i]["t"] = a
    Q = {"v": g.vector, "s": g.scalar, "p": g.tensor, "g": g, "y": g.sync}
    total = {}
    for o in ops:
        if o["sem"]: total[o["sem"]] = total.get(o["sem"], 0) + (nen if o["sem"][0] == "a" else 16)
    count = {e: 0 for e in "vspg"}; known = {e: {} for e in Q}; mark = {}; clock = {}
    for i in seq:
        o = ops[i]; e = o["e"]; kn = known[e]; need = {}
        deps = [j for j in o["d"] if not (e == "p" and ops[j]["e"] == "p")]
        for j in deps:
            sm, val = mark[j]
            need[sm] = max(need.get(sm, 0), val)
        for j in sorted(deps, key=lambda j: -ops[j]["t"]):
            sm, val = mark[j]
            if val == need[sm] and kn.get(sm, 0) < val:
                Q[e].wait_ge(T.sem[sm], val); kn[sm] = val
                for a, x in clock[j].items(): kn[a] = max(kn.get(a, 0), x)
        ins = o["fn"]()
        if o["sem"]:
            mark[i] = (o["sem"], total[o["sem"]]); clock[i] = {}
            if o["sem"][0] != "a": ins.then_inc(T.sem[o["sem"]], 16)
        elif [j for j in succ[i] if not (e == "p" and ops[j]["e"] == "p")]:
            count[e] += 1; ins.then_inc(T.sem[e], 1); mark[i] = (e, count[e]); clock[i] = dict(kn)
    for e in "vspg":
        g.wait_ge(T.sem[e], count[e])
    g.wait_ge(T.sem.sent, nen * 12)
    for t in range(RO):
        g.wait_ge(T.sem["y%d" % t], 16)
